import numpy as np, ml_dtypes
CORES = [1,5,17,21,33,37,49,53]
N = 8
import mx_ref
BF = ml_dtypes.bfloat16
def cols(t, e):
    v = np.concatenate([t.reshape(128, -1, 4), np.zeros((128, 1, 4), BF)], axis=1)
    return np.ascontiguousarray(v[:, e]).reshape(128, -1)
def tile(rs):
    return np.stack(rs, axis=2).reshape(128, -1).astype(BF)
def pick(q, e):
    c = np.concatenate([q[0].reshape(128, -1, 4), np.zeros((128, 1, 4), np.uint8)], axis=1); s = np.concatenate([q[1], np.ones((16, 1), np.uint8)], axis=1)
    return (np.ascontiguousarray(c[:, e].reshape(128, -1)), np.ascontiguousarray(s[:, e]))
def join(*qs):
    return (np.concatenate([q[0] for q in qs], axis=1), np.concatenate([q[1] for q in qs], axis=1))
def put(q, e, v):
    c, s = q[0].reshape(128, -1, 4).copy(), q[1].copy(); c[:, e] = v[0].reshape(128, -1, 4); s[:, e] = v[1]
    return (c.reshape(128, -1), s)
def pk(c, s):
    return (np.ascontiguousarray(c), mx_ref.live(s))
def emit(q):
    return q[0], q[1]
def packed(v, rng):
    q = [mx_ref.quantize(np.ascontiguousarray(v[r])) for r in range(N)]
    return np.stack([a for a, b in q]), np.stack([mx_ref.plane(b, rng) for a, b in q])
def decode(q):
    o = []
    for b in range(4):
        e = np.zeros((128, 128, 4), np.float32); e[np.arange(128), np.arange(128), b] = 1
        o.append(mx_ref.matmul(mx_ref.quantize(e.reshape(128, 512).astype(BF)), q))
    return np.stack(o, axis=2).reshape(128, -1)
def f(rng, *shape):
    return mx_ref.flush((rng.standard_normal(shape, dtype=np.float32) * np.exp2(rng.integers(-2, 3, shape[:-1] + (1,)))).astype(BF))
def wide(rng, *shape, cols=0):
    v = rng.standard_normal(shape, dtype=np.float32) * np.exp2(rng.integers(-12, 13, shape)).astype(np.float32)
    if cols: v *= np.repeat(np.exp2(rng.integers(-cols, cols + 1, shape[:-2] + (1, shape[-1] // 4))) * (rng.random(shape[:-2] + (1, shape[-1] // 4)) > 0.0625), 4, axis=-1).astype(np.float32)
    return mx_ref.flush(v.astype(BF))
C, S, K, R = 256, 32, 4, 3
def home(j):
    return j % N * S + j // N
def choose(z):
    e = np.arange(C).reshape(S, N)
    return np.concatenate([e[np.argsort(-z[e[:, a]], kind="stable")[:K], a] for a in range(N)])
def big(v, k):
    v = v.astype(np.float32) * np.float32(k)
    v[np.abs(v) < np.float32(2.0 ** -16)] = 0
    return v.astype(BF)
def weights(rng, k, zero=0, still=slice(0)):
    w = big(f(rng, 128, 2048), k)
    w[:zero] = 0
    w = w.reshape(128, 4, 128, 4)
    w[:, :, still] = 0
    w = w.reshape(128, 2048)
    c, p = packed(np.stack([w] * N), rng)
    return {"wc": c, "ws": p}
def numbers_of(rng):
    return {"x": big(f(rng, N, 128, 4 * C), 1), "pr": big(f(rng, N, 128, 4 * S), 1), "pd": big(f(rng, N, 128, 4 * S), 1), "u": np.array(f(rng, N, 128, 512)), "v": np.array(f(rng, N, 128, 512))}
def signs(rng):
    g = np.stack([rng.permutation(N) % 2 * 2.0 - 1.0 for r in range(N)])
    return g[:, np.arange(C) % N].astype(np.float32)
def setup_inputs(rng):
    return {**numbers_of(rng), **weights(rng, 0.25)}
def setup_inputs_ties(rng):
    d = setup_inputs(rng)
    for r in range(N):
        k = np.stack([rng.permutation(S) % 3 for a in range(N)], axis=1).reshape(-1)
        d["x"][r] = cols(d["x"][r], np.where(k == 2, -1, k))
        for n in ("pr", "pd"): d[n][r] = cols(d[n][r], np.zeros(S, int))
    return d
def setup_inputs_near(rng):
    d = {**numbers_of(rng), **weights(rng, 0.25, 0, np.r_[0:16, 64:64 + 8 * R])}
    x = d["x"].reshape(N, 128, C, 4)
    d["u"][:, :, :4 * R] = 0
    d["v"][:, :, :4 * R] = 0
    for n, g in (("pr", -1), ("pd", 1)):
        p = d[n].reshape(N, 128, S, 4)
        p[:, 0, :, 0] = g
        d[n] = p.reshape(N, 128, 4 * S)
    x[:, :8] = 0
    x[:, 8, :, 0] = signs(rng).astype(BF)
    x[:, 64:64 + 8 * R] = 0
    for t in range(R):
        p = 64 + 8 * t
        d["v"][:, 0, 4 * t] = 1
        d["u"][:, 8, 4 * t] = 1
        d["u"][:, p:p + 2, 4 * t:4 * t + 4] = 1
        s = (np.arange(C) // N + t * (K + 1)) % S + K % 4
        v = (((s[:, None] >> np.arange(8)) & 1) * np.exp2(np.arange(8) - 23.0)).astype(np.float32).astype(BF)
        x[:, p] = v[None, :, :4]
        x[:, p + 1] = v[None, :, 4:]
    return {**d, "x": x.reshape(N, 128, 4 * C)}
def setup_inputs_huge(rng):
    d = numbers_of(rng)
    d["u"][:, :, :4 * R] = ((1.5 + 0.5 * rng.random((N, 128, 4 * R))) * 2.0 ** 29).astype(np.float32).astype(BF)
    g = signs(rng)
    top = (np.arange(C) // N // K)[None, :] == np.arange(N)[:, None]
    size = np.repeat(np.where(top == (g > 0), 1.5, 1.0625), 4, axis=1)[:, None, :]
    x = (size + 0.25 * rng.random((N, 128, 4 * C))) * np.repeat(np.where(g > 0, 2.0 ** 26, -2.0 ** 28), 4, axis=1)[:, None, :]
    return {**d, "x": x.astype(np.float32).astype(BF), "pr": big(d["pr"], 2.0 ** 22), "pd": big(d["pd"], 2.0 ** 22), "v": big(d["v"], 2.0 ** 25), **weights(rng, 2.0 ** -7)}
def setup_inputs_crowd(rng):
    d = {**numbers_of(rng), **weights(rng, 0.25, 64)}
    x = d["x"].reshape(N, 128, C, 4)
    d["u"][:, :, :4 * R] = 0
    d["u"][:, :8, :4 * R] = 1
    d["v"][:, :8, :4 * R] = 0
    for kind, lo, hi, n in (("pr", 0, S // 2, K // 2), ("pd", S // 2, S - 1, K - K // 2)):
        p = d[kind].reshape(N, 128, S, 4)
        for a in range(N):
            for i, s in enumerate(lo + rng.permutation(hi - lo)[:R * n]):
                v = rng.integers(4, 8, (56, 4)) * np.exp2(rng.integers(-2, 1, (56, 4))) * rng.choice([-1.0, 1.0], (56, 4))
                o = rng.permutation(N)
                for r in range(N):
                    j = s * N + a + (r if kind == "pd" else 0)
                    g = 1.0 if r == o[0] else -1.0 if r == o[1] else 2.0 ** -26
                    x[r, :8, j] = 256 * 2 ** (R - 1 - i // n)
                    x[r, 8:64, j] = (v * g).astype(np.float32).astype(BF)
                    x[r, 64:, j] = 0
                p[a, 8:64, s] = (v * 2.0 ** -25).astype(np.float32).astype(BF)
        d[kind] = p.reshape(N, 128, 4 * S)
    return {**d, "x": x.reshape(N, 128, 4 * C)}
def setup_inputs_spread(rng):
    d = setup_inputs(rng)
    d["x"] = big(wide(rng, N, 128, 4 * C, cols=6), 1)
    for n in ("pr", "pd"): d[n] = big(wide(rng, N, 128, 4 * S, cols=6), 1)
    return d
def check_inputs(d):
    b = []
    for k in ("x", "pr", "pd", "u", "v"):
        a = np.abs(d[k].astype(np.float32))
        if not (np.isfinite(a).all() and ((a == 0) | (a >= 2.0 ** -30) & (a <= 2.0 ** 30)).all()): b.append("a value of " + k)
    if (d["wc"] != d["wc"][:1]).any(): b.append("wc differs between ranks")
    s = [mx_ref.live(p) for p in d["ws"]]
    if any((p != s[0]).any() for p in s): b.append("ws differs between ranks")
    return b
def reference(x, pr, pd, u, v, wc, ws):
    w = pk(wc[0], ws[0])
    qu, qv = [mx_ref.quantize(u[r]) for r in range(N)], [mx_ref.quantize(v[r]) for r in range(N)]
    data = join(*[mx_ref.quantize(x[r]) for r in range(N)])
    par = join(*[mx_ref.quantize(pr[r]) for r in range(N)], *[mx_ref.quantize(pd[r]) for r in range(N)])
    mine = [C * r + np.arange(C) for r in range(N)]
    own = [np.concatenate([S * r + np.arange(S), C + S * r + np.arange(S)]) for r in range(N)]
    n = N * K
    for t in range(R):
        s = np.zeros(2 * C, np.float32)
        for r in range(N): s[own[r]] = mx_ref.matmul(qv[r], pick(par, own[r]))[t]
        took, rows, diags = [], [], []
        for r in range(N):
            j = np.arange(C)
            a = mx_ref.matmul(qu[r], pick(data, mine[r]))[t]
            z = (a - s[home(j)]) - s[C + home((j - r) % C)]
            e = choose(z + np.float32(0.0))
            took.append(C * r + e)
            rows.append(home(e))
            diags.append(C + home((e - r) % C))
        at = np.concatenate(took)
        old = pick(data, at)
        new = mx_ref.quantize(tile([np.maximum(mx_ref.matmul(pick(w, np.arange(128 * b, 128 * b + 128)), old), np.float32(0.0)) * np.float32(0.0625) for b in range(4)]))
        delta = decode(mx_ref.quantize((decode(new) - decode(old)).astype(BF))).reshape(128, -1, 4)
        p, anew = decode(par).reshape(128, -1, 4), np.zeros(2 * C, bool)
        for r in range(N):
            for h in (rows[r], diags[r]):
                p[:, h] = p[:, h] + delta[:, n * r:n * r + n]
                anew[h] = True
        e = np.flatnonzero(anew)
        par = put(par, e, pick(mx_ref.quantize(np.ascontiguousarray(p.reshape(128, -1).astype(BF))), e))
        data = put(data, at, new)
    y = np.zeros((N, 128, C + 2 * S), np.float32)
    oc, osc = np.zeros((N, 128, 4 * (C + 2 * S)), np.uint8), np.zeros((N, 16, C + 2 * S), np.uint8)
    for r in range(N):
        a, b = pick(data, mine[r]), pick(par, own[r])
        y[r] = np.concatenate([mx_ref.matmul(qu[r], a), mx_ref.matmul(qv[r], b)], axis=1)
        oc[r], osc[r] = emit(join(a, b))
    return {"y": y, "oc": oc, "osc": osc}

@@ -1,0 +1,641 @@
+from concourse.bass import DstId, RemoteDMATransfer
+from concourse.mybir import dt, AluOpType as A, AxisListType, ActivationFunctionType as F
+
+R = 3
+FP8, U8, BF, F32, I32, U16 = "float8_e4m3fn_x4", "uint8", "bfloat16", "float32", "int32", "uint16"
+SCRATCH = {"ps": ("psum", [128, 4096], F32)}
+
+
+def _add(d, text, mx=False):
+    for item in text.split():
+        name, n = item.split(":")
+        if mx:
+            SCRATCH["c_" + name] = ("sbuf", [128, int(n)], FP8)
+            SCRATCH["z_" + name] = ("sbuf", [128, int(n)], U8)
+        else:
+            SCRATCH[name] = ("sbuf", [128, int(n)], d)
+
+
+_add(BF, "XB:1024 PT:640 UB:512 VB:512 ONE:520 EB:520 NB:520 ZB:512 HT0:1024 DT0:1024 HT1:512 DT1:512 NT:512 "
+         "INV0:512 INV1:512 INV2:512 INVT:512 VALS:64")
+_add(FP8, "X:256 U:128 V:128 W:512 E:1024 D0:384 D1:384 D2:384 D3:256 FD:256 NX:416 DL:416 PB0:288 PB1:288 PB2:288 "
+          "PB3:160 DC0:160 DC1:160 DC2:160 SN0:64 SN1:64 SN2:64 LA0:72 LA1:72 LA2:72 AR0:512 AR1:512 AR2:512", mx=True)
+_add(U16, "WL0:32 WL1:32 WL2:32 LL0:28 LL1:28 LL2:28 L1U:2 L2U:4 DLS:16 SEL:16")
+_add(F32, "N0:12 N1:12 N2:12 SC0:1 SC1:1 SC2:1 FC:32 IOI:64 MAP:64 KT:64 K4:64 OFR:64 OFD:64 LM:64 SM:96 TMPF:256 "
+          "ACOL:8 RA:64 AROW:64 RB:128 TB:128 S1:64 ST:64 RR:64 G1:64 G2:64 CC:64 XR:8 RG:64 RT:64 MM:64 MP:64 MPR:128 "
+          "NEQ:32 JUNK:8 ACC:256 YB:320 UP:128")
+_add(I32, "PI:1 INTC:16 TMPI:256")
+SMALL = {"OWN": 0, "C1": 16, "WD": 32, "WE": 48, "SQ": 64, "AN": 68, "SE": 72, "L1F": 76, "L2F": 80}
+LISTS = {"nat": 0, "out": 16, "bl": 32, "sh": 40, "rg": 44, "ac": 48, "w": 52, "w2": 54, "sn": 56, "ow": 60, "se": 62}
+_add(U16, "LST:64")
+SEMAPHORES = ["qg", "qv", "qs", "qt", "snt"] + [s + str(t) for s in ("sc", "dA", "dB") for t in range(R)] + ["m%d" % i for i in range(40)]
+
+
+def rank_program(g, core, T, topo):
+    me = T.rank_of(core)
+    if me is None:
+        return
+    cores = [int(c) for c in T.cores]
+    n_ranks = len(cores)
+    r = me
+    Q = {"g": g, "v": g.vector, "s": g.scalar, "t": g.tensor, "y": g.sync}
+    csem = {"g": "qg", "v": "qv", "s": "qs", "t": "qt"}
+    total, known, hist = {}, {q: {} for q in Q}, {}
+    ndma = [0]
+
+    def w(name, c0, c1, step=1, p0=0, p1=128):
+        if name in SMALL:
+            name, c0, c1 = "SM", c0 + SMALL[name], c1 + SMALL[name]
+        t = T[name]
+        if p0 == 0 and p1 == 128:
+            a = t[:, c0:c1] if step == 1 else t[:, c0:c1:step]
+        else:
+            a = t[p0:p1, c0:c1] if step == 1 else t[p0:p1, c0:c1:step]
+        return (a, [(name, c0, c1, p0, p1)])
+
+    def ind(v, o):
+        return (v[0].indirect(o[0]), v[1] + o[1])
+
+    def lst(name, n, off=0):
+        a = LISTS[name] + off
+        return w("LST", a, a + n)
+
+    def norm(reg):
+        name, c0, c1, p0, p1 = reg
+        if name == "ps":
+            return (name, c0 // 512 * 512, (c1 + 511) // 512 * 512, 0, 128)
+        return reg
+
+    def waits(q, reads, writes):
+        need = {}
+        def want(h):
+            sem, n, clock = h[7], h[8], h[9]
+            if known[q].get(sem, 0) >= n:
+                return
+            if sem not in need or need[sem][0] < n:
+                need[sem] = (n, clock)
+        for reg in reads:
+            name, c0, c1, p0, p1 = norm(reg)
+            for h in hist.get(name, ()):
+                if h[0] < c1 and c0 < h[1] and h[2] < p1 and p0 < h[3] and (h[4] or (name == "ps" and h[5] != q)):
+                    want(h)
+        for reg in writes:
+            name, c0, c1, p0, p1 = norm(reg)
+            for h in hist.get(name, ()):
+                if h[0] < c1 and c0 < h[1] and h[2] < p1 and p0 < h[3]:
+                    if name == "ps" and h[5] == q:
+                        continue
+                    want(h)
+        for sem in sorted(need):
+            n, clock = need[sem]
+            if any(s2 != sem and c2.get(sem, 0) >= n for s2, (n2, c2) in need.items()):
+                continue
+            Q[q].wait_ge(T.sem[sem], n)
+        for sem in need:
+            n, clock = need[sem]
+            for k, v in clock.items():
+                if known[q].get(k, 0) < v:
+                    known[q][k] = v
+            known[q][sem] = max(known[q].get(sem, 0), n)
+
+    def record(q, reads, writes, sem, n, clock, dma):
+        for reg in writes:
+            reg = norm(reg)
+            name, c0, c1, p0, p1 = reg
+            hs = [h for h in hist.get(name, ()) if not (c0 <= h[0] and h[1] <= c1 and p0 <= h[2] and h[3] <= p1)]
+            hs.append((c0, c1, p0, p1, True, q, dma, sem, n, clock))
+            hist[name] = hs
+        for reg in reads:
+            reg = norm(reg)
+            name, c0, c1, p0, p1 = reg
+            hs = [h for h in hist.get(name, ()) if not (not h[4] and not dma and not h[6] and h[5] == q and (c0, c1, p0, p1) == tuple(h[:4]))]
+            hs.append((c0, c1, p0, p1, False, q, dma, sem, n, clock))
+            hist[name] = hs
+
+    def run(q, call, reads, writes, dma=False):
+        rr = [x for v in reads for x in v[1]]
+        ww = [x for v in writes for x in v[1]]
+        waits(q, rr, ww)
+        if dma:
+            sem, inc = "m%d" % ndma[0], 16
+            ndma[0] += 1
+        else:
+            sem, inc = csem[q], 1
+        total[sem] = total.get(sem, 0) + inc
+        call().then_inc(T.sem[sem], inc)
+        clock = dict(known[q])
+        clock[sem] = total[sem]
+        record(q, rr, ww, sem, total[sem], clock, dma)
+
+    def arrive(views, sem, n):
+        total[sem] = n
+        record("x", [], [x for v in views for x in v[1]], sem, n, {sem: n}, True)
+
+    def S(x):
+        return x[0] if isinstance(x, tuple) else x
+
+    def deps(*xs):
+        return [x for x in xs if isinstance(x, tuple)]
+
+    def cp(q, out, a):
+        if q == "v":
+            run("v", lambda: g.vector.tensor_copy(out[0], a[0]), [a], [out])
+        else:
+            run("s", lambda: g.scalar.activation(out[0], a[0], F.Copy), [a], [out])
+
+    def sa(out, a, scale=1.0, bias=0.0):
+        run("s", lambda: g.scalar.activation(out[0], a[0], F.Identity, bias=S(bias), scale=S(scale)), [a] + deps(scale, bias), [out])
+
+    def tt(out, a, b, op):
+        run("v", lambda: g.vector.tensor_tensor(out[0], a[0], b[0], op), [a, b], [out])
+
+    def ts(out, a, s1, op0, s2=None, op1=None):
+        if op1 is None:
+            run("v", lambda: g.vector.tensor_scalar(out[0], a[0], S(s1), None, op0), [a] + deps(s1), [out])
+        else:
+            run("v", lambda: g.vector.tensor_scalar(out[0], a[0], S(s1), S(s2), op0, op1), [a] + deps(s1, s2), [out])
+
+    def red(out, a, op):
+        run("v", lambda: g.vector.tensor_reduce(out[0], a[0], AxisListType.X, op), [a], [out])
+
+    def tr(out, a):
+        run("v", lambda: g.vector.transpose(out[0], a[0]), [a], [out])
+
+    def fill(out, c):
+        run("v", lambda: g.vector.memset(out[0], c), [], [out])
+
+    def iota(out, pattern, base=0, ch=0, small=True):
+        if small:
+            run("g", lambda: g.iota(out[0], pattern, base, ch, allow_small_or_imprecise_dtypes=True), [], [out])
+        else:
+            run("g", lambda: g.iota(out[0], pattern, base, ch), [], [out])
+
+    def quant(name, c0, src):
+        n = (src[1][0][2] - src[1][0][1]) // 4
+        c, z = w("c_" + name, c0, c0 + n), w("z_" + name, c0, c0 + n)
+        run("v", lambda: g.vector.quantize_mx(c[0], z[0], src[0]), [src], [c, z])
+
+    def pick(dst, d0, n, src, width, off):
+        b, k = off
+        o = w(b, k, k + n // 16)
+        co, ci = w("c_" + dst, d0, d0 + n), w("c_" + src, 0, width)
+        run("v", lambda: g.vector.tensor_copy(co[0].bitcast(dt.uint32), ci[0].bitcast(dt.uint32).indirect(o[0])), [ci, o], [co])
+        zo, zi = w("z_" + dst, d0, d0 + n), w("z_" + src, 0, width)
+        run("s", lambda: g.scalar.activation(zo[0], zi[0].indirect(o[0]), F.Copy), [zi, o], [zo])
+
+    def mm(bank, n, lhs, l0, rhs, r0, start=True, stop=True):
+        out = w("ps", 512 * bank, 512 * bank + n)
+        a, az = w("c_" + lhs, l0, l0 + 128), w("z_" + lhs, l0, l0 + 128)
+        b, bz = w("c_" + rhs, r0, r0 + n), w("z_" + rhs, r0, r0 + n)
+        run("t", lambda: g.tensor.matmul_mx(out[0], a[0], az[0], b[0], bz[0], start, stop), [a, az, b, bz], [out])
+
+    def bank(b, n, c0=0):
+        return w("ps", 512 * b + c0, 512 * b + c0 + n)
+
+    def load(q, out, a):
+        run(q, lambda: Q[q].dma_start(out[0], a), [], [out], dma=True)
+
+    def store(q, a, src):
+        run(q, lambda: Q[q].dma_start(a, src[0]), [src], [], dma=True)
+
+    others = [o for o in range(n_ranks) if o != me]
+    def pos(s, d):
+        return s if s < d else s - 1
+    def far(s):
+        return [o for o in range(n_ranks) if o != s and topo.chip(cores[s]) != topo.chip(cores[o])]
+    def plan(j, s, d):
+        fs = far(s)
+        away = topo.engines(cores[s], cores[fs[0]])
+        e = topo.engines(cores[s], cores[d])
+        if d not in fs:
+            return [x for x in e if x not in away][:2]
+        half = len(away) // 2
+        one, two = (away[:half], away[half:]) if j % 2 == 0 else (away[half:], away[:half])
+        i = (fs.index(d) + 2 * j) % len(fs)
+        return [one[i]] if i < half else two[2 * (i - half):2 * (i - half) + 2]
+    def bits(e):
+        return sum(1 << x for x in e)
+    def to(o):
+        rid, pid = topo.addr(cores[o])[:2]
+        return DstId(rid=rid, pnc=pid)
+
+    def fused(reads, transfers, engines):
+        waits("g", [x for v in reads for x in v[1]], [])
+        g.remote_dma_fused(transfers, local_sem=T.sem.snt)
+        total["snt"] = total.get("snt", 0) + engines
+
+    def send_scores(t):
+        src = w("SC%d" % t, 0, 1)
+        sem, fs = T.sem["sc%d" % t], far(me)
+        e = topo.engines(cores[me], cores[fs[0]])
+        land = T["N%d" % t][:, me:me + 1]
+        tf, ne = [RemoteDMATransfer(dst_ids=[to(o) for o in fs], dma_engine_mask=bits(e), remote_sem=sem, srcs=[src[0]], dsts=[land for o in fs])], len(e)
+        for o in others:
+            if o not in fs:
+                e = plan(0, me, o)
+                tf.append(RemoteDMATransfer(dst_ids=[to(o)], dma_engine_mask=bits(e), remote_sem=sem, srcs=[src[0]], dsts=[land]))
+                ne += len(e)
+        fused([src], tf, ne)
+
+    def score_count():
+        return sum(len(topo.engines(cores[s], cores[me])) if me in far(s) else len(plan(0, s, me)) for s in others)
+
+    def send_each(j, t, src_of, dst_of, reads):
+        tf, ne = [], 0
+        for o in others:
+            p = pos(me, o)
+            e = plan(j, me, o)
+            tf.append(RemoteDMATransfer(dst_ids=[to(o)], dma_engine_mask=bits(e), remote_sem=T.sem[("dA%d" if p < 3 else "dB%d") % t], srcs=[src_of(o)], dsts=[dst_of(p)]))
+            ne += len(e)
+        fused(reads, tf, ne)
+
+    QB = me % 4
+    NB = 5 if QB == 3 else 4
+    V0 = 32 if QB == 3 else 0
+    RO = 32 * QB - V0
+    NEW = 160
+
+    blocks = [T.pr if b == QB else T.pd for b in range(NB)]
+    for b in range(NB):
+        load("ys"[b % 2], w("PT", 128 * b, 128 * b + 128), blocks[b][:, :])
+    load("y", w("VB", 0, 512), T.v[:, :])
+    load("s", w("XB", 0, 1024), T.x[:, :])
+    cw = w("c_W", 0, 512)
+    load("y", (cw[0].bitcast(dt.uint8), cw[1]), T.wc[:, :])
+    load("s", w("z_W", 0, 512), T.ws[:, :])
+    load("y", w("UB", 0, 512), T.u[:, :])
+
+    TMP = [0]
+    def ftmp(n):
+        a = TMP[0]
+        TMP[0] += n
+        return w("TMPF", a, a + n)
+    kt, ioi, mp = w("KT", 0, 64), w("IOI", 0, 64), w("MAP", 0, 64)
+    iota(w("PI", 0, 1), [[0, 1]], 0, 1, small=False)
+    fill(w("ONE", 0, 520), 1.0)
+    eb, one = w("EB", 0, 520), w("ONE", 0, 520)
+    run("g", lambda: g.affine_select(eb[0], one[0], [[-1, 520]], A.is_equal, 0.0, 4, 4), [one], [eb])
+    fnat, fbl, frg, fsh, fsn, fout, fw, fc1, f1, f2 = [ftmp(n) for n in (16, 4, 4, 4, 4, 16, 2, 16, 64, 64)]
+    iota(fnat, [[1, 8], [128, 2]])
+    iota(fbl, [[4, 2], [0, 2]])
+    iota(fsh, [[0, 2], [16, 2]])
+    iota(ioi, [[0, 2], [1, 32]])
+    iota(frg, [[1, 2], [0, 2]])
+    iota(fsn, [[2, 4]])
+    iota(mp, [[128, 2], [1, 32]])
+    iota(kt, [[4, 2], [0, 32]])
+    iota(w("VALS", 0, 64), [[4, 2], [0, 8], [1, 4]])
+    iota(fw, [[128, 2]])
+
+    def col(j):
+        return w("FC", j, j + 1)
+    P16, P31, KK, QQ, B2, B3, Q0, Q1, M, ODD, B0, B1, K1, P8 = range(14)
+    for j, (sh, an) in enumerate(((0, 15), (0, 31), (2, 3), (5, 3), (2, 1), (3, 1), (5, 1), (6, 1), (0, 3), (4, 1), (0, 1), (1, 1), (1, 7), (0, 7))):
+        o, i = w("INTC", j, j + 1), w("PI", 0, 1)
+        if sh:
+            ts(o, i, sh, A.arith_shift_right, an, A.bitwise_and)
+        else:
+            ts(o, i, an, A.bitwise_and)
+    cp("v", w("FC", 0, 14), w("INTC", 0, 14))
+    C8P, CX, CSN, C16, CW2, CW, CNX, CND, C32K, COUT = range(14, 24)
+    ts(col(C8P), col(P16), 8.0, A.mult)
+    for h in range(2):
+        fill(lst("ac", 2, 2 * h), h)
+    tt(col(CNX), col(B2), col(Q0), A.not_equal)
+    tt(col(CND), col(B3), col(Q1), A.not_equal)
+    ts(lst("nat", 16), fnat, col(C8P), A.add)
+    for b in range(4):
+        quant("E", 128 * b, w("EB", 4 - b, 516 - b))
+    sa(w("NB", 0, 520), eb, -1.0)
+
+    quant("PB0", 0, w("PT", 0, 128 * NB))
+    quant("V", 0, w("VB", 0, 512))
+
+    def scores(t):
+        sc, n = "SC%d" % t, "N%d" % t
+        mm(0, 128, "PB%d" % t, 0, "V", 0)
+        cp("s", w(sc, 0, 1), w("ps", t, t + 1))
+        send_scores(t)
+        run("y", lambda: g.sync.dma_start(T[n][:, me:me + 1], T[sc][:, 0:1]), [w(sc, 0, 1)], [w(n, me, me + 1)], dma=True)
+        arrive([w(n, a, b) for a, b in ((0, me), (me + 1, 8)) if b > a], "sc%d" % t, score_count())
+
+    scores(0)
+
+    quant("X", 0, w("XB", 0, 1024))
+    pick("D0", 0, 256, "X", 256, ("LST", LISTS["nat"]))
+    quant("U", 0, w("UB", 0, 512))
+    sa(col(C32K), col(KK), 32.0)
+    sa(kt, kt, 1.0, col(KK))
+    sa(col(C16), col(ODD), 16.0)
+    sa(mp, mp, 1.0, col(C32K))
+    sa(f1, kt, 32.0)
+    sa(w("ZB", 0, 512), w("EB", 0, 512), 0.0)
+    for b in range(4):
+        mm(b, 256, "W", 128 * b, "D0", 0)
+    for h in range(2):
+        mm(4 + h, 128, "D0", 128 * h, "U", 0)
+    for b in range(4):
+        quant("E", 512 + 128 * b, w("NB", 4 - b, 516 - b))
+    ts(lst("bl", 4), fbl, col(QQ), A.add)
+    if r % 4 == 0:
+        for h in range(2):
+            fill(lst("bl", 2, 4 + 2 * h), 8 + (h if r == 0 else 1 - h))
+    else:
+        bi = w("TMPI", 12, 16)
+        ts(bi, fbl, col(QQ), A.add, float(8 - r), A.add)
+        ts(bi, bi, 7, A.bitwise_and)
+        cp("v", lst("bl", 4, 4), bi)
+    shi = w("TMPI", 0, 4)
+    ts(shi, fsh, col(P16), A.add)
+    for h in range(2):
+        n = min(max(r - 4 * h, 0), 4)
+        if n:
+            v = w("TMPI", 2 * h, 2 * h + 2, 1, 0, 32 * n)
+            ts(v, v, 31.0, A.add)
+    ts(w("LM", 0, 64), ioi, col(P31), A.is_lt)
+    ts(shi, shi, 31, A.bitwise_and)
+    cp("v", lst("sh", 2), w("TMPI", 0, 2))
+    ts(lst("sh", 2, 2), w("TMPI", 2, 4), 32.0, A.add)
+
+    def relu(tile, b, cols, bk):
+        o, i = w(tile, b, 4 * cols, 4), bank(bk, cols)
+        run("s", lambda: g.scalar.activation(o[0], i[0], F.Relu, scale=0.0625), [i], [o])
+
+    for b in range(3):
+        relu("HT0", b, 256, b)
+    cp("s", w("ACOL", 0, 2), w("ps", 2048, 3072, 512))
+    relu("HT0", 3, 256, 3)
+    sa(w("INV0", 0, 512), w("EB", 0, 512), 0.0, 8.0)
+    for b in range(4):
+        mm(4 + b, 256, "E", 512 + 128 * b, "D0", 0, True, False)
+    ts(col(CX), col(CND), 2.0, A.mult, col(CNX), A.add)
+    ts(col(CX), col(CX), 2.0, A.mult)
+    ts(lst("rg", 4), frg, col(CX), A.add)
+    ts(col(CSN), col(B2), float(r), A.mult, col(B3), A.add)
+    sni = w("TMPI", 4, 8)
+    ts(sni, fsn, col(CSN), A.add)
+    tt(col(CNX), col(B0), col(ODD), A.not_equal)
+    ts(sni, sni, 7, A.bitwise_and)
+    ts(col(CW2), col(CNX), 16.0, A.mult)
+    ts(lst("sn", 4), sni, 4.0, A.mult, col(M), A.add)
+    quant("NX", 0, w("HT0", 0, 1024))
+    for b in range(4):
+        mm(4 + b, 256, "E", 128 * b, "NX", 0, False, True)
+    for b in range(4):
+        cp("s", w("DT0", b, 1024, 4), bank(4 + b, 256))
+    x1, x2, x3 = w("TMPI", 16, 80), w("TMPI", 80, 144), w("TMPI", 144, 208)
+    ts(f2, kt, float(r), A.is_lt, 31.0, A.mult)
+    ts(x1, ioi, col(C16), A.add)
+    ts(x3, kt, float(8 - r), A.add)
+    tt(x2, f2, ioi, A.add)
+    ts(x1, x1, 31, A.bitwise_and)
+    ts(x3, x3, 7, A.bitwise_and)
+    ts(x2, x2, col(C16), A.add)
+    tt(w("OFR", 0, 64), f1, x1, A.add)
+    ts(x2, x2, 31, A.bitwise_and)
+    ts(f2, x3, 32.0, A.mult, 256.0, A.add)
+    ts(col(CW), col(B1), 256.0, A.mult, col(CW2), A.add)
+    tt(w("OFD", 0, 64), f2, x2, A.add)
+    tt(col(CW), col(CW), col(C32K), A.add)
+    ts(lst("w2", 1), col(K1), 32.0, A.mult, col(CW2), A.add)
+    ts(lst("w", 2), fw, col(CW), A.add)
+
+    def base(o):
+        return 0 if o == me else 16 + 8 * pos(me, o)
+    for kind in range(2):
+        k = 0
+        while k < 8:
+            bs = base((k - r * kind) % 8)
+            e = k
+            while e < 8 and base((e - r * kind) % 8) == bs:
+                e += 1
+            v = w("VALS", 32 * kind + 4 * k, 32 * kind + 4 * e)
+            if bs:
+                sa(v, v, 1.0, float(bs))
+            k = e
+
+    def arow():
+        ra = w("RA", 0, 64)
+        cp("v", ra, ind(w("ACOL", 0, 2), lst("ac", 4)))
+        tr(w("AROW", 0, 64), ra)
+
+    arow()
+    own16, c1 = w("OWN", 0, 16), w("C1", 0, 16)
+    iota(own16, [[16, 16]])
+    iota(w("SQ", 0, 4), [[16, 4]])
+    iota(fout, [[2, 16]])
+    iota(fc1, [[4, 8], [0, 2]])
+
+    def unpack_parities(t):
+        for b in range(4):
+            mm(4 + b, 128, "E", 128 * b, "PB%d" % t, V0)
+        for b in range(4):
+            cp("s", w("ACC", 64 * b, 64 * b + 64), bank(4 + b, 64, RO))
+
+    def zeros(n, a, b):
+        sa(w(n, a, b), w("EB", a, b), 0.0)
+
+    def late_tables():
+        quant("DC0", 32, w("ZB", 0, 512))
+        y0, y1, y2 = ftmp(1), ftmp(1), ftmp(1)
+        ts(y0, col(B2), 4.0 * ((2 * r) % 8 - r), A.mult, col(M), A.add)
+        sa(own16, own16, 1.0, col(P16))
+        ts(y0, y0, 4.0 * r, A.add)
+        quant("D0", 256, w("ZB", 0, 512))
+        ts(y1, y0, -1.0, A.mult, 32.0, A.add)
+        tt(c1, fc1, own16, A.subtract)
+        tt(y1, y1, col(B3), A.mult)
+        ts(y2, col(K1), float(QB), A.is_equal, -2.0, A.mult)
+        ts(lst("ow", 1), y0, y1, A.add)
+        for k0, k1, bs in ((0, me, base(0)), (me, me + 1, 0), (me + 1, 8, base(7))):
+            if k1 > k0:
+                v = w("C1", 2 * k0, 2 * k1)
+                sa(v, v, 1.0, float(256 - bs))
+        ts(lst("se", 1), y2, col(B0), A.add, 2.0, A.add)
+        zeros("HT1", 128, 512)
+
+    def last_tables():
+        for t in range(1, R):
+            quant("DC%d" % t, 32, w("ZB", 0, 512))
+        quant("D1", 256, w("ZB", 0, 512))
+        for t in range(1, R):
+            sa(w("INV%d" % t, 0, 512), w("EB", 0, 512), 0.0, 8.0)
+        sa(w("K4", 0, 64), kt, 4.0, 256.0)
+        sa(col(COUT), col(P8), 32.0, col(B3))
+        ts(lst("out", 16), fout, col(COUT), A.add)
+
+    def choose(t):
+        n = "N%d" % t
+        if r % 4 == 0:
+            for q in range(4):
+                cp("vs"[q % 2], w(n, 8, 10, 1, 32 * q, 32 * q + 32), w(n, q, 8, 4, 32 * (q ^ 1), 32 * (q ^ 1) + 32))
+        rb, tb = w("RB", 0, 128), w("TB", 0, 128)
+        cp("v", rb, ind(w(n, 0, 10 if r % 4 == 0 else 8), lst("bl", 8)))
+        tr(tb, rb)
+        s1, st, rr, g1, g2 = [w(x, 0, 64) for x in ("S1", "ST", "RR", "G1", "G2")]
+        tt(s1, w("AROW", 0, 64), w("TB", 0, 64), A.subtract)
+        tt(st, ind(w("TB", 64, 128), lst("sh", 4)), s1, A.subtract)
+        tr(rr, st)
+        tt(g1, st, rr, A.is_equal)
+        tt(g2, st, rr, A.is_lt)
+        tt(g1, g1, w("LM", 0, 64), A.mult)
+        def scan(h):
+            o, a, b = [w(x, 32 * h, 32 * h + 32) for x in ("CC", "G1", "G2")]
+            run("v", lambda: g.vector.tensor_tensor_scan(o[0], a[0], b[0], 0.0, A.add, A.add), [a, b], [o])
+        if t == 0:
+            quant("DL", 0, w("DT0", 0, 1024))
+        scan(0)
+        scan(1)
+        for q in range(4):
+            cp("vs"[q % 2], w("XR", 2, 4, 1, 32 * q, 32 * q + 32), w("CC", 31, 64, 32, 32 * (q ^ 1), 32 * (q ^ 1) + 32))
+        cp("v", w("XR", 0, 2), w("CC", 31, 64, 32))
+        cp("v", w("XR", 4, 8, 1, 0, 64), w("XR", 0, 4, 1, 64, 128))
+        cp("s", w("XR", 4, 8, 1, 64, 128), w("XR", 0, 4, 1, 0, 64))
+        rg, rt, m = w("RG", 0, 64), w("RT", 0, 64), w("MM", 0, 64)
+        cp("v", rg, ind(w("XR", 0, 8), lst("rg", 4)))
+        tr(rt, rg)
+        ts(m, rt, col(M), A.is_equal)
+        tt(w("MP", 0, 64), m, mp, A.mult)
+        for h in range(2):
+            red(w("L1F", h, h + 1), w("MP", 32 * h, 32 * h + 32), A.add)
+        tt(w("MPR", 0, 64), m, w("OFR", 0, 64), A.mult)
+        cp("v", w("L1U", 0, 2), w("L1F", 0, 2))
+        tt(w("MPR", 64, 128), m, w("OFD", 0, 64), A.mult)
+        dc, sn, la, ll, wl = "DC%d" % t, "SN%d" % t, "LA%d" % t, "LL%d" % t, "WL%d" % t
+        pick(dc, 0, 32, "DL", 256 + 32 * t, ("L1U", 0))
+        red(w("L2F", 0, 1), w("MPR", 0, 32), A.add)
+        pick(sn, 0, 64, dc, 32, ("LST", LISTS["sn"]))
+        send_each(0, t, lambda o: T["c_" + sn][:, 8 * o:8 * o + 8].bitcast(dt.uint8),
+                  lambda p: T["c_" + la][:, 16 + 8 * p:24 + 8 * p].bitcast(dt.uint8), [w("c_" + sn, 0, 64)])
+        send_each(1, t, lambda o: T["z_" + sn][:, 8 * o:8 * o + 8],
+                  lambda p: T["z_" + la][:, 16 + 8 * p:24 + 8 * p], [w("z_" + sn, 0, 64)])
+        for k in range(1, 4):
+            red(w("L2F", k, k + 1), w("MPR", 32 * k, 32 * k + 32), A.add)
+        l2 = w("L2U", 0, 4)
+        cp("v", l2, w("L2F", 0, 4))
+        inv, vals = w("INV%d" % t, 0, 512), w("VALS", 0, 64)
+        run("v", lambda: g.vector.tensor_copy(inv[0].indirect(l2[0]), vals[0]), [vals, l2], [inv])
+        it = w("INVT", 0, 512)
+        tr(it, inv)
+        cp("v", w(wl, 0, 32), ind(it, lst("w", 2)))
+        send_each(2, t, lambda o: T[wl][:, 4 * o:4 * o + 4], lambda p: T[ll][:, 4 * p:4 * p + 4], [w(wl, 0, 32)])
+        for name, lo, hi in (("dA%d", 0, 3), ("dB%d", 3, 7)):
+            cnt = sum(len(plan(j, s, me)) for j in range(3) for s in others if lo <= pos(s, me) < hi)
+            arrive([w("c_" + la, 16 + 8 * lo, 16 + 8 * hi), w("z_" + la, 16 + 8 * lo, 16 + 8 * hi), w(ll, 4 * lo, 4 * hi)], name % t, cnt)
+        if t == 0:
+            late_tables()
+        pick(la, 0, 16, dc, 34, ("LST", LISTS["ow"]))
+        pick("AR%d" % t, 0, 64, la, 16, (wl, 4 * me))
+        ts(w("NEQ", 28, 32), w(wl, 4 * me, 4 * me + 4), 8.0, A.not_equal)
+
+    def advance(t):
+        d, dn, it = "D%d" % t, "D%d" % (t + 1), w("INVT", 0, 512)
+        pick(d, 256, 32, "NX", 256 + 32 * t, ("L1U", 0))
+        if t < R - 1:
+            for b in range(4):
+                mm(b, 128, "W", 128 * b, d, 256)
+        if t == 0:
+            unpack_parities(0)
+            zeros("NT", 256, 512)
+            sa(w("SQ", 0, 4), w("SQ", 0, 4), 1.0, col(P16))
+            if QB:
+                sa(w("SQ", 0, 4), w("SQ", 0, 4), 1.0, 32.0 * QB)
+        wd, we = w("WD", 0, 16), w("WE", 0, 16)
+        cp("v", wd, ind(it, lst("w2", 1)))
+        ts(we, wd, 8.0, A.not_equal)
+        tt(wd, wd, c1, A.add)
+        tt(wd, wd, we, A.mult)
+        tt(wd, wd, own16, A.add)
+        cp("v", w("DLS", 0, 16), wd)
+        if t < R - 1:
+            for b in range(4):
+                relu("HT1", b, 32, b)
+            quant("NX", 256 + 32 * t, w("HT1", 0, 512))
+        pick(dn, 0, 256, d, 288, ("DLS", 0))
+        if t < R - 1:
+            for h in range(2):
+                mm(4 + h, 128, dn, 128 * h, "U", 0)
+            cp("s", w("ACOL", 0, 2), w("ps", 2048 + t + 1, 3072, 512))
+        else:
+            pick("FD", 0, 256, dn, 256, ("LST", LISTS["out"]))
+            mm(4, 256, "U", 0, "FD", 0)
+            cp("s", w("YB", 0, 256), w("ps", 2048, 2304))
+            fd = w("c_FD", 0, 256)
+            store("y", T.oc[:, 0:1024], (fd[0].bitcast(dt.uint8), fd[1]))
+            store("y", T.y[:, 0:256], w("YB", 0, 256))
+            for k in range(4):
+                store("y", T.osc[4 * k:4 * k + 4, 0:256], w("z_FD", 0, 256, 1, 32 * k, 32 * k + 4))
+
+    def patch(t):
+        la, ll, ar, pb = "LA%d" % t, "LL%d" % t, "AR%d" % t, "PB%d" % t
+        pick(ar, 64, 192, la, 40, (ll, 0))
+        for b in range(4):
+            mm(b, 256, "E", 128 * b, ar, 0)
+        pick(ar, 256, 256, la, 72, (ll, 12))
+        for b in range(4):
+            mm(4 + b, 256, "E", 128 * b, ar, 256)
+        ts(w("NEQ", 0, 28), w(ll, 0, 28), 8.0, A.not_equal)
+        for c in range(4):
+            v, o, z = w("NEQ", c, 32, 4), w("JUNK", 0, 8), w("AN", c, c + 1)
+            run("s", lambda: g.scalar.activation(o[0], v[0], F.Copy, accum_out=z[0]), [v], [o, z])
+        def slot(s):
+            return 0 if s == me else 1 + pos(s, me)
+        def add(s, b):
+            k = slot(s)
+            acc = w("ACC", 64 * b, 64 * b + 64)
+            out = w("NT", b, 256, 4) if s == n_ranks - 1 else acc
+            tt(out, acc, bank(b if k < 4 else 4 + b, 64, 64 * (k % 4)), A.add)
+        first = 0
+        while first < n_ranks and slot(first) < 4:
+            first += 1
+        for part in (range(0, first), range(first, n_ranks)):
+            for pair in ((0, 1), (2, 3)):
+                for s in part:
+                    for b in pair:
+                        add(s, b)
+            if part.start == 0:
+                se = w("SE", 0, 4)
+                ts(se, w("AN", 0, 4), 0.0, A.is_gt, float(NEW - 32 * QB), A.mult)
+                tt(se, se, w("SQ", 0, 4), A.add)
+                cp("v", w("SEL", 0, 16), ind(se, lst("se", 1)))
+        quant(pb, NEW, w("NT", 0, 512))
+        pick("PB%d" % (t + 1), 0, 32 * NB, pb, 288, ("SEL", 0))
+        if t < R - 1:
+            scores(t + 1)
+            unpack_parities(t + 1)
+            arow()
+            if t == 0:
+                zeros("DT1", 128, 512)
+            for b in range(4):
+                mm(4 + b, 128, "E", 512 + 128 * b, "D%d" % t, 256, True, False)
+                mm(4 + b, 128, "E", 128 * b, "NX", 256 + 32 * t, False, True)
+            if t == 0:
+                last_tables()
+            mask, u = w("UP", 0, 64), w("UP", 64, 128)
+            rt = w("RT", 0, 64)
+            ts(mask, rt, 4.0, A.is_lt)
+            tt(u, rt, w("K4", 0, 64), A.add)
+            tt(u, u, mp, A.subtract)
+            tt(u, u, mask, A.mult)
+            tt(mp, mp, u, A.add)
+            sa(w("K4", 0, 64), w("K4", 0, 64), 1.0, 32.0)
+            for b in range(4):
+                cp("vs"[b % 2], w("DT1", b, 128, 4), bank(4 + b, 32))
+            quant("DL", 256 + 32 * t, w("DT1", 0, 512))
+        else:
+            last, c = "PB%d" % R, 32 * QB
+            mm(0, 128, "V", 0, last, V0)
+            cc = w("c_" + last, c, c + 64)
+            store("y", T.oc[:, 1024:1280], (cc[0].bitcast(dt.uint8), cc[1]))
+            for k in range(4):
+                store("ys"[k % 2], T.osc[4 * k:4 * k + 4, 256:320], w("z_" + last, c, c + 64, 1, 32 * k, 32 * k + 4))
+            cp("v", w("YB", 256, 320), bank(0, 64, RO))
+            store("s", T.y[:, 256:320], w("YB", 256, 320))
+
+    for t in range(R):
+        choose(t)
+        advance(t)
+        patch(t)
+    for sem in sorted(total):
+        if known["g"].get(sem, 0) < total[sem]:
+            g.wait_ge(T.sem[sem], total[sem])

@@ -1,7 +1,8 @@
 from concourse.bass import DstId, RemoteDMATransfer
-from concourse.mybir import dt, AluOpType as A, AxisListType, ActivationFunctionType as F
+from concourse.mybir import dt, AluOpType as A, ActivationFunctionType as F
 
 R = 3
+NHAND = 4
 FP8, U8, BF, F32, I32, U16 = "float8_e4m3fn_x4", "uint8", "bfloat16", "float32", "int32", "uint16"
 SCRATCH = {"ps": ("psum", [128, 4096], F32)}
 
@@ -19,24 +20,85 @@ def _add(d, text, mx=False):
 _add(BF, "XB:1024 PT:640 UB:512 VB:512 ONE:520 EB:520 NB:520 ZB:512 HT0:1024 DT0:1024 HT1:512 DT1:512 NT:512 "
          "INV0:512 INV1:512 INV2:512 INVT:512 VALS:64")
 _add(FP8, "X:256 U:128 V:128 W:512 E:1024 D0:384 D1:384 D2:384 D3:256 FD:256 NX:416 DL:416 PB0:288 PB1:288 PB2:288 "
-          "PB3:160 DC0:160 DC1:160 DC2:160 SN0:64 SN1:64 SN2:64 LA0:72 LA1:72 LA2:72 AR0:512 AR1:512 AR2:512", mx=True)
+          "PB3:160 DC0:160 DC1:160 DC2:160 SN0:64 SN1:64 SN2:64 LA0:72 LA1:72 LA2:72 AR:512", mx=True)
+_add(FP8, "c_HB0:64 c_HB1:64 c_HB2:64")
 _add(U16, "WL0:32 WL1:32 WL2:32 LL0:28 LL1:28 LL2:28 L1U:2 L2U:4 DLS:16 SEL:16")
-_add(F32, "N0:12 N1:12 N2:12 SC0:1 SC1:1 SC2:1 FC:32 IOI:64 MAP:64 KT:64 K4:64 OFR:64 OFD:64 LM:64 SM:96 TMPF:256 "
-          "ACOL:8 RA:64 AROW:64 RB:128 TB:128 S1:64 ST:64 RR:64 G1:64 G2:64 CC:64 XR:8 RG:64 RT:64 MM:64 MP:64 MPR:128 "
+_add(F32, "N0:16 N1:16 N2:16 SC0:1 SC1:1 SC2:1 FC:32 IOI:64 MAP:64 KT:64 K4:64 OFR:64 OFD:64 LM:64 SM:96 TMPF:256 "
+          "ACOL:8 RA:64 AROW:64 RB:128 TB:128 S1:64 ST:64 RR:64 G1:64 G2:64 CC:64 XR:8 RG:64 RT:64 MM:64 SCN:192 DMP:64 DF:128 "
           "NEQ:32 JUNK:8 ACC:256 YB:320 UP:128")
 _add(I32, "PI:1 INTC:16 TMPI:256")
-SMALL = {"OWN": 0, "C1": 16, "WD": 32, "WE": 48, "SQ": 64, "AN": 68, "SE": 72, "L1F": 76, "L2F": 80}
+SMALL = {"OWN": 0, "C1": 16, "WD": 32, "WE": 48, "SQ": 64, "AN": 68, "SE": 72}
 LISTS = {"nat": 0, "out": 16, "bl": 32, "sh": 40, "rg": 44, "ac": 48, "w": 52, "w2": 54, "sn": 56, "ow": 60, "se": 62}
 _add(U16, "LST:64")
-SEMAPHORES = ["qg", "qv", "qs", "qt", "snt"] + [s + str(t) for s in ("sc", "dA", "dB") for t in range(R)] + ["m%d" % i for i in range(40)]
+SEMAPHORES = (["qg", "qv", "qs", "qt", "snt"] + [s + str(t) for s in ("sc", "dA", "dB", "hs") for t in range(R)]
+              + ["m%d" % i for i in range(40)])
+
+
+def pos(s, d):
+    return s if s < d else s - 1
+
+
+def bits(e):
+    return sum(1 << x for x in e)
+
+
+def _far(s, cores, topo):
+    return [o for o in range(len(cores)) if o != s and topo.chip(cores[s]) != topo.chip(cores[o])]
+
+
+def _near(src, dst, away, topo):
+    return [x for x in topo.engines(src, dst) if x not in away]
+
+
+def _plan(j, s, d, src, cores, topo):
+    fs = _far(s, cores, topo)
+    away = topo.engines(src, cores[fs[0]])
+    if d not in fs:
+        return _near(src, cores[d], away, topo)[:2]
+    half = len(away) // 2
+    one, two = (away[:half], away[half:]) if j % 2 == 0 else (away[half:], away[:half])
+    i = (fs.index(d) + 2 * j) % len(fs)
+    return [one[i]] if i < half else two[2 * (i - half):2 * (i - half) + 2]
+
+
+def _to(core, topo):
+    rid, pid = topo.addr(core)[:2]
+    return DstId(rid=rid, pnc=pid)
+
+
+def _helper(s, cores, topo):
+    return [c for c in topo.cores_of(cores[s]) if topo.die(c) == topo.die(cores[s]) and c not in cores][0]
+
+
+def _delta_sem(T, s, d, t):
+    return T.sem[("dA%d" if pos(s, d) < 3 else "dB%d") % t]
+
+
+def hand_on(g, core, s, cores, T, topo):
+    sent = 0
+    for t in range(R):
+        g.wait_ge(T.sem["hs%d" % t], NHAND)
+        tf = []
+        for o in range(len(cores)):
+            if o != s:
+                p, e = pos(s, o), _plan(0, s, o, core, cores, topo)
+                sent += len(e)
+                tf.append(RemoteDMATransfer(dst_ids=[_to(cores[o], topo)], dma_engine_mask=bits(e), remote_sem=_delta_sem(T, s, o, t),
+                                            srcs=[T["c_HB%d" % t][:, 8 * o:8 * o + 8].bitcast(dt.uint8)],
+                                            dsts=[T["c_LA%d" % t][:, 16 + 8 * p:24 + 8 * p].bitcast(dt.uint8)]))
+        g.remote_dma_fused(tf, local_sem=T.sem.snt)
+    g.wait_ge(T.sem.snt, sent)
 
 
 def rank_program(g, core, T, topo):
-    me = T.rank_of(core)
-    if me is None:
-        return
     cores = [int(c) for c in T.cores]
     n_ranks = len(cores)
+    me = T.rank_of(core)
+    if me is None:
+        for s in range(n_ranks):
+            if _helper(s, cores, topo) == core:
+                hand_on(g, core, s, cores, T, topo)
+        return
     r = me
     Q = {"g": g, "v": g.vector, "s": g.scalar, "t": g.tensor, "y": g.sync}
     csem = {"g": "qg", "v": "qv", "s": "qs", "t": "qt"}
@@ -155,9 +217,6 @@ def rank_program(g, core, T, topo):
         else:
             run("v", lambda: g.vector.tensor_scalar(out[0], a[0], S(s1), S(s2), op0, op1), [a] + deps(s1, s2), [out])
 
-    def red(out, a, op):
-        run("v", lambda: g.vector.tensor_reduce(out[0], a[0], AxisListType.X, op), [a], [out])
-
     def tr(out, a):
         run("v", lambda: g.vector.transpose(out[0], a[0]), [a], [out])
 
@@ -199,65 +258,37 @@ def rank_program(g, core, T, topo):
         run(q, lambda: Q[q].dma_start(a, src[0]), [src], [], dma=True)
 
     others = [o for o in range(n_ranks) if o != me]
-    def pos(s, d):
-        return s if s < d else s - 1
-    def far(s):
-        return [o for o in range(n_ranks) if o != s and topo.chip(cores[s]) != topo.chip(cores[o])]
+    afar = _far(me, cores, topo)
+    away = topo.engines(core, cores[afar[0]])
     def plan(j, s, d):
-        fs = far(s)
-        away = topo.engines(cores[s], cores[fs[0]])
-        e = topo.engines(cores[s], cores[d])
-        if d not in fs:
-            return [x for x in e if x not in away][:2]
-        half = len(away) // 2
-        one, two = (away[:half], away[half:]) if j % 2 == 0 else (away[half:], away[:half])
-        i = (fs.index(d) + 2 * j) % len(fs)
-        return [one[i]] if i < half else two[2 * (i - half):2 * (i - half) + 2]
-    def bits(e):
-        return sum(1 << x for x in e)
-    def to(o):
-        rid, pid = topo.addr(cores[o])[:2]
-        return DstId(rid=rid, pnc=pid)
+        return _plan(j, s, d, cores[s], cores, topo)
 
-    def fused(reads, transfers, engines):
+    def fused(reads, transfers):
         waits("g", [x for v in reads for x in v[1]], [])
-        g.remote_dma_fused(transfers, local_sem=T.sem.snt)
-        total["snt"] = total.get("snt", 0) + engines
+        g.remote_dma_fused([RemoteDMATransfer(dst_ids=[_to(c, topo) for c in ds], dma_engine_mask=bits(e), remote_sem=sem, srcs=[src], dsts=[land] * len(ds))
+                            for ds, e, sem, src, land in transfers], local_sem=T.sem.snt)
+        total["snt"] = total.get("snt", 0) + sum(len(x[1]) for x in transfers)
 
     def send_scores(t):
-        src = w("SC%d" % t, 0, 1)
-        sem, fs = T.sem["sc%d" % t], far(me)
-        e = topo.engines(cores[me], cores[fs[0]])
-        land = T["N%d" % t][:, me:me + 1]
-        tf, ne = [RemoteDMATransfer(dst_ids=[to(o) for o in fs], dma_engine_mask=bits(e), remote_sem=sem, srcs=[src[0]], dsts=[land for o in fs])], len(e)
-        for o in others:
-            if o not in fs:
-                e = plan(0, me, o)
-                tf.append(RemoteDMATransfer(dst_ids=[to(o)], dma_engine_mask=bits(e), remote_sem=sem, srcs=[src[0]], dsts=[land]))
-                ne += len(e)
-        fused([src], tf, ne)
+        src, land, sem = w("SC%d" % t, 0, 1), T["N%d" % t][:, me:me + 1], T.sem["sc%d" % t]
+        fused([src], [([cores[o] for o in afar], away, sem, src[0], land)]
+              + [([cores[o]], plan(0, me, o), sem, src[0], land) for o in others if o not in afar])
 
     def score_count():
-        return sum(len(topo.engines(cores[s], cores[me])) if me in far(s) else len(plan(0, s, me)) for s in others)
+        return sum(len(topo.engines(cores[s], core)) if s in afar else len(plan(0, s, me)) for s in others)
 
     def send_each(j, t, src_of, dst_of, reads):
-        tf, ne = [], 0
-        for o in others:
-            p = pos(me, o)
-            e = plan(j, me, o)
-            tf.append(RemoteDMATransfer(dst_ids=[to(o)], dma_engine_mask=bits(e), remote_sem=T.sem[("dA%d" if p < 3 else "dB%d") % t], srcs=[src_of(o)], dsts=[dst_of(p)]))
-            ne += len(e)
-        fused(reads, tf, ne)
+        fused(reads, [([cores[o]], plan(j, me, o), _delta_sem(T, me, o, t), src_of(o), dst_of(pos(me, o))) for o in others])
 
     QB = me % 4
     NB = 5 if QB == 3 else 4
     V0 = 32 if QB == 3 else 0
     RO = 32 * QB - V0
+    CLASH = r % 4 == 0
     NEW = 160
 
-    blocks = [T.pr if b == QB else T.pd for b in range(NB)]
     for b in range(NB):
-        load("ys"[b % 2], w("PT", 128 * b, 128 * b + 128), blocks[b][:, :])
+        load("ys"[b % 2], w("PT", 128 * b, 128 * b + 128), (T.pr if b == QB else T.pd)[:, :])
     load("y", w("VB", 0, 512), T.v[:, :])
     load("s", w("XB", 0, 1024), T.x[:, :])
     cw = w("c_W", 0, 512)
@@ -328,7 +359,11 @@ def rank_program(g, core, T, topo):
     sa(kt, kt, 1.0, col(KK))
     sa(col(C16), col(ODD), 16.0)
     sa(mp, mp, 1.0, col(C32K))
+    sa(w("DMP", 0, 64), mp, 0.0, -1.0)
+    cp("s", w("DMP", 31, 64, 32), w("MAP", 31, 64, 32))
     sa(f1, kt, 32.0)
+    sa(w("K4", 0, 64), kt, 4.0, 256.0)
+    sa(col(COUT), col(P8), 32.0, col(B3))
     sa(w("ZB", 0, 512), w("EB", 0, 512), 0.0)
     for b in range(4):
         mm(b, 256, "W", 128 * b, "D0", 0)
@@ -336,26 +371,30 @@ def rank_program(g, core, T, topo):
         mm(4 + h, 128, "D0", 128 * h, "U", 0)
     for b in range(4):
         quant("E", 512 + 128 * b, w("NB", 4 - b, 516 - b))
+    bi, shi, sni = w("TMPI", 12, 16), w("TMPI", 0, 4), w("TMPI", 4, 8)
     ts(lst("bl", 4), fbl, col(QQ), A.add)
-    if r % 4 == 0:
-        for h in range(2):
-            fill(lst("bl", 2, 4 + 2 * h), 8 + (h if r == 0 else 1 - h))
-    else:
-        bi = w("TMPI", 12, 16)
-        ts(bi, fbl, col(QQ), A.add, float(8 - r), A.add)
-        ts(bi, bi, 7, A.bitwise_and)
-        cp("v", lst("bl", 4, 4), bi)
-    shi = w("TMPI", 0, 4)
+    ts(bi, fbl, col(QQ), A.add, float(8 - r), A.add)
     ts(shi, fsh, col(P16), A.add)
+    ts(col(CX), col(CND), 2.0, A.mult, col(CNX), A.add)
+    ts(col(CSN), col(B2), float(r), A.mult, col(B3), A.add)
+    ts(bi, bi, 7, A.bitwise_and)
     for h in range(2):
         n = min(max(r - 4 * h, 0), 4)
         if n:
             v = w("TMPI", 2 * h, 2 * h + 2, 1, 0, 32 * n)
             ts(v, v, 31.0, A.add)
-    ts(w("LM", 0, 64), ioi, col(P31), A.is_lt)
+    ts(col(CX), col(CX), 2.0, A.mult)
+    ts(sni, fsn, col(CSN), A.add)
+    ts(lst("bl", 4, 4), bi, 8.0 if CLASH else 0.0, A.add)
     ts(shi, shi, 31, A.bitwise_and)
+    tt(col(CNX), col(B0), col(ODD), A.not_equal)
+    ts(lst("rg", 4), frg, col(CX), A.add)
+    ts(sni, sni, 7, A.bitwise_and)
     cp("v", lst("sh", 2), w("TMPI", 0, 2))
     ts(lst("sh", 2, 2), w("TMPI", 2, 4), 32.0, A.add)
+    ts(col(CW2), col(CNX), 16.0, A.mult)
+    ts(lst("sn", 4), sni, 4.0, A.mult, col(M), A.add)
+    ts(w("LM", 0, 64), ioi, col(P31), A.is_lt)
 
     def relu(tile, b, cols, bk):
         o, i = w(tile, b, 4 * cols, 4), bank(bk, cols)
@@ -368,16 +407,6 @@ def rank_program(g, core, T, topo):
     sa(w("INV0", 0, 512), w("EB", 0, 512), 0.0, 8.0)
     for b in range(4):
         mm(4 + b, 256, "E", 512 + 128 * b, "D0", 0, True, False)
-    ts(col(CX), col(CND), 2.0, A.mult, col(CNX), A.add)
-    ts(col(CX), col(CX), 2.0, A.mult)
-    ts(lst("rg", 4), frg, col(CX), A.add)
-    ts(col(CSN), col(B2), float(r), A.mult, col(B3), A.add)
-    sni = w("TMPI", 4, 8)
-    ts(sni, fsn, col(CSN), A.add)
-    tt(col(CNX), col(B0), col(ODD), A.not_equal)
-    ts(sni, sni, 7, A.bitwise_and)
-    ts(col(CW2), col(CNX), 16.0, A.mult)
-    ts(lst("sn", 4), sni, 4.0, A.mult, col(M), A.add)
     quant("NX", 0, w("HT0", 0, 1024))
     for b in range(4):
         mm(4 + b, 256, "E", 128 * b, "NX", 0, False, True)
@@ -413,6 +442,10 @@ def rank_program(g, core, T, topo):
             if bs:
                 sa(v, v, 1.0, float(bs))
             k = e
+
+    def differences(name, c, src):
+        tt(w(name, c, c + 63), w(src, 0, 63), w(src, 1, 64), A.subtract)
+        cp("s", w(name, c + 31, c + 64, 32), w(src, 31, 64, 32))
 
     def arow():
         ra = w("RA", 0, 64)
@@ -460,17 +493,14 @@ def rank_program(g, core, T, topo):
         quant("D1", 256, w("ZB", 0, 512))
         for t in range(1, R):
             sa(w("INV%d" % t, 0, 512), w("EB", 0, 512), 0.0, 8.0)
-        sa(w("K4", 0, 64), kt, 4.0, 256.0)
-        sa(col(COUT), col(P8), 32.0, col(B3))
-        ts(lst("out", 16), fout, col(COUT), A.add)
 
     def choose(t):
         n = "N%d" % t
-        if r % 4 == 0:
-            for q in range(4):
-                cp("vs"[q % 2], w(n, 8, 10, 1, 32 * q, 32 * q + 32), w(n, q, 8, 4, 32 * (q ^ 1), 32 * (q ^ 1) + 32))
+        if CLASH:
+            for h, q in enumerate("vs" if t else "vv"):
+                cp(q, w(n, 8, 16, 1, 64 * h, 64 * h + 64), w(n, 0, 8, 1, 64 - 64 * h, 128 - 64 * h))
         rb, tb = w("RB", 0, 128), w("TB", 0, 128)
-        cp("v", rb, ind(w(n, 0, 10 if r % 4 == 0 else 8), lst("bl", 8)))
+        cp("v", rb, ind(w(n, 0, 16 if CLASH else 8), lst("bl", 8)))
         tr(tb, rb)
         s1, st, rr, g1, g2 = [w(x, 0, 64) for x in ("S1", "ST", "RR", "G1", "G2")]
         tt(s1, w("AROW", 0, 64), w("TB", 0, 64), A.subtract)
@@ -484,6 +514,8 @@ def rank_program(g, core, T, topo):
             run("v", lambda: g.vector.tensor_tensor_scan(o[0], a[0], b[0], 0.0, A.add, A.add), [a, b], [o])
         if t == 0:
             quant("DL", 0, w("DT0", 0, 1024))
+            differences("DF", 0, "OFR")
+            differences("DF", 64, "OFD")
         scan(0)
         scan(1)
         for q in range(4):
@@ -494,25 +526,27 @@ def rank_program(g, core, T, topo):
         rg, rt, m = w("RG", 0, 64), w("RT", 0, 64), w("MM", 0, 64)
         cp("v", rg, ind(w("XR", 0, 8), lst("rg", 4)))
         tr(rt, rg)
-        ts(m, rt, col(M), A.is_equal)
-        tt(w("MP", 0, 64), m, mp, A.mult)
+        ts(m, rt, col(M), A.not_equal)
+        def entry(k, tab, h, c):
+            o, a, b = w("SCN", 32 * k, 32 * k + 32), w("MM", 32 * h, 32 * h + 32), w(tab, c, c + 32)
+            run("v", lambda: g.vector.tensor_tensor_scan(o[0], a[0], b[0], 0.0, A.mult, A.add), [a, b], [o])
         for h in range(2):
-            red(w("L1F", h, h + 1), w("MP", 32 * h, 32 * h + 32), A.add)
-        tt(w("MPR", 0, 64), m, w("OFR", 0, 64), A.mult)
-        cp("v", w("L1U", 0, 2), w("L1F", 0, 2))
-        tt(w("MPR", 64, 128), m, w("OFD", 0, 64), A.mult)
+            entry(h, "DMP", h, 32 * h)
+        entry(2, "DF", 0, 0)
+        cp("v", w("L1U", 0, 2), w("SCN", 31, 64, 32))
+        entry(3, "DF", 1, 32)
         dc, sn, la, ll, wl = "DC%d" % t, "SN%d" % t, "LA%d" % t, "LL%d" % t, "WL%d" % t
         pick(dc, 0, 32, "DL", 256 + 32 * t, ("L1U", 0))
-        red(w("L2F", 0, 1), w("MPR", 0, 32), A.add)
+        entry(4, "DF", 0, 64)
         pick(sn, 0, 64, dc, 32, ("LST", LISTS["sn"]))
-        send_each(0, t, lambda o: T["c_" + sn][:, 8 * o:8 * o + 8].bitcast(dt.uint8),
-                  lambda p: T["c_" + la][:, 16 + 8 * p:24 + 8 * p].bitcast(dt.uint8), [w("c_" + sn, 0, 64)])
+        hc = _helper(me, cores, topo)
+        fused([w("c_" + sn, 0, 64)], [([hc], _near(core, hc, away, topo)[:NHAND], T.sem["hs%d" % t],
+                                       T["c_" + sn][:, 0:64].bitcast(dt.uint8), T["c_HB%d" % t][:, 0:64].bitcast(dt.uint8))])
         send_each(1, t, lambda o: T["z_" + sn][:, 8 * o:8 * o + 8],
                   lambda p: T["z_" + la][:, 16 + 8 * p:24 + 8 * p], [w("z_" + sn, 0, 64)])
-        for k in range(1, 4):
-            red(w("L2F", k, k + 1), w("MPR", 32 * k, 32 * k + 32), A.add)
+        entry(5, "DF", 1, 96)
         l2 = w("L2U", 0, 4)
-        cp("v", l2, w("L2F", 0, 4))
+        cp("v", l2, w("SCN", 95, 192, 32))
         inv, vals = w("INV%d" % t, 0, 512), w("VALS", 0, 64)
         run("v", lambda: g.vector.tensor_copy(inv[0].indirect(l2[0]), vals[0]), [vals, l2], [inv])
         it = w("INVT", 0, 512)
@@ -525,7 +559,7 @@ def rank_program(g, core, T, topo):
         if t == 0:
             late_tables()
         pick(la, 0, 16, dc, 34, ("LST", LISTS["ow"]))
-        pick("AR%d" % t, 0, 64, la, 16, (wl, 4 * me))
+        pick("AR", 0, 64, la, 16, (wl, 4 * me))
         ts(w("NEQ", 28, 32), w(wl, 4 * me, 4 * me + 4), 8.0, A.not_equal)
 
     def advance(t):
@@ -540,6 +574,8 @@ def rank_program(g, core, T, topo):
             sa(w("SQ", 0, 4), w("SQ", 0, 4), 1.0, col(P16))
             if QB:
                 sa(w("SQ", 0, 4), w("SQ", 0, 4), 1.0, 32.0 * QB)
+        if t == 1:
+            ts(lst("out", 16), fout, col(COUT), A.add)
         wd, we = w("WD", 0, 16), w("WE", 0, 16)
         cp("v", wd, ind(it, lst("w2", 1)))
         ts(we, wd, 8.0, A.not_equal)
@@ -567,13 +603,13 @@ def rank_program(g, core, T, topo):
                 store("y", T.osc[4 * k:4 * k + 4, 0:256], w("z_FD", 0, 256, 1, 32 * k, 32 * k + 4))
 
     def patch(t):
-        la, ll, ar, pb = "LA%d" % t, "LL%d" % t, "AR%d" % t, "PB%d" % t
-        pick(ar, 64, 192, la, 40, (ll, 0))
+        la, ll, pb = "LA%d" % t, "LL%d" % t, "PB%d" % t
+        pick("AR", 64, 192, la, 40, (ll, 0))
         for b in range(4):
-            mm(b, 256, "E", 128 * b, ar, 0)
-        pick(ar, 256, 256, la, 72, (ll, 12))
+            mm(b, 256, "E", 128 * b, "AR", 0)
+        pick("AR", 256, 256, la, 72, (ll, 12))
         for b in range(4):
-            mm(4 + b, 256, "E", 128 * b, ar, 256)
+            mm(4 + b, 256, "E", 128 * b, "AR", 256)
         ts(w("NEQ", 0, 28), w(ll, 0, 28), 8.0, A.not_equal)
         for c in range(4):
             v, o, z = w("NEQ", c, 32, 4), w("JUNK", 0, 8), w("AN", c, c + 1)
@@ -585,18 +621,20 @@ def rank_program(g, core, T, topo):
             acc = w("ACC", 64 * b, 64 * b + 64)
             out = w("NT", b, 256, 4) if s == n_ranks - 1 else acc
             tt(out, acc, bank(b if k < 4 else 4 + b, 64, 64 * (k % 4)), A.add)
-        first = 0
-        while first < n_ranks and slot(first) < 4:
-            first += 1
-        for part in (range(0, first), range(first, n_ranks)):
-            for pair in ((0, 1), (2, 3)):
-                for s in part:
-                    for b in pair:
-                        add(s, b)
-            if part.start == 0:
-                se = w("SE", 0, 4)
+        free, seq, ready, step = 0.0, [], [0.0] * 4, [0] * 4
+        while len(seq) < 4 * n_ranks:
+            can = [(max(free, ready[b], 4.5 * ((1 if slot(step[b]) < 4 else 5) + b)), step[b], b) for b in range(4) if step[b] < n_ranks]
+            start, s, b = min(can)
+            seq.append((s, b))
+            free, ready[b], step[b] = start + 1, start + 3, s + 1
+        se = w("SE", 0, 4)
+        for i, (s, b) in enumerate(seq):
+            add(s, b)
+            if i == 2 * n_ranks + 3:
                 ts(se, w("AN", 0, 4), 0.0, A.is_gt, float(NEW - 32 * QB), A.mult)
+            if i == 2 * n_ranks + 6:
                 tt(se, se, w("SQ", 0, 4), A.add)
+            if i == 2 * n_ranks + 9:
                 cp("v", w("SEL", 0, 16), ind(se, lst("se", 1)))
         quant(pb, NEW, w("NT", 0, 512))
         pick("PB%d" % (t + 1), 0, 32 * NB, pb, 288, ("SEL", 0))
@@ -609,8 +647,6 @@ def rank_program(g, core, T, topo):
             for b in range(4):
                 mm(4 + b, 128, "E", 512 + 128 * b, "D%d" % t, 256, True, False)
                 mm(4 + b, 128, "E", 128 * b, "NX", 256 + 32 * t, False, True)
-            if t == 0:
-                last_tables()
             mask, u = w("UP", 0, 64), w("UP", 64, 128)
             rt = w("RT", 0, 64)
             ts(mask, rt, 4.0, A.is_lt)
@@ -618,10 +654,13 @@ def rank_program(g, core, T, topo):
             tt(u, u, mp, A.subtract)
             tt(u, u, mask, A.mult)
             tt(mp, mp, u, A.add)
+            differences("DMP", 0, "MAP")
             sa(w("K4", 0, 64), w("K4", 0, 64), 1.0, 32.0)
             for b in range(4):
                 cp("vs"[b % 2], w("DT1", b, 128, 4), bank(4 + b, 32))
             quant("DL", 256 + 32 * t, w("DT1", 0, 512))
+            if t == 0:
+                last_tables()
         else:
             last, c = "PB%d" % R, 32 * QB
             mm(0, 128, "V", 0, last, V0)

@@ -2,7 +2,9 @@ from concourse.bass import DstId, RemoteDMATransfer
 from concourse.mybir import dt, AluOpType as A, ActivationFunctionType as F
 
 R = 3
+HALF = 4
 NHAND = 4
+TINY = 2.0 ** -110
 FP8, U8, BF, F32, I32, U16 = "float8_e4m3fn_x4", "uint8", "bfloat16", "float32", "int32", "uint16"
 SCRATCH = {"ps": ("psum", [128, 4096], F32)}
 
@@ -20,16 +22,19 @@ def _add(d, text, mx=False):
 _add(BF, "XB:1024 PT:640 UB:512 VB:512 ONE:520 EB:520 NB:520 ZB:512 HT0:1024 DT0:1024 HT1:512 DT1:512 NT:512 "
          "INV0:512 INV1:512 INV2:512 INVT:512 VALS:64")
 _add(FP8, "X:256 U:128 V:128 W:512 E:1024 D0:384 D1:384 D2:384 D3:256 FD:256 NX:416 DL:416 PB0:288 PB1:288 PB2:288 "
-          "PB3:160 DC0:160 DC1:160 DC2:160 SN0:64 SN1:64 SN2:64 LA0:72 LA1:72 LA2:72 AR:512", mx=True)
-_add(FP8, "c_HB0:64 c_HB1:64 c_HB2:64")
+          "PB3:160 DC0:160 DC1:160 DC2:160 SN0:64 SN1:64 SN2:64 LA0:72 LA1:72 LA2:72 AR:448 AO:128", mx=True)
+_add(FP8, "c_HC0:32 c_HC1:32 c_HC2:32")
+_add(U8, "z_HZ0:32 z_HZ1:32 z_HZ2:32")
 _add(U16, "WL0:32 WL1:32 WL2:32 LL0:28 LL1:28 LL2:28 L1U:2 L2U:4 DLS:16 SEL:16")
-_add(F32, "N0:16 N1:16 N2:16 SC0:1 SC1:1 SC2:1 FC:32 IOI:64 MAP:64 KT:64 K4:64 OFR:64 OFD:64 LM:64 SM:96 TMPF:256 "
-          "ACOL:8 RA:64 AROW:64 RB:128 TB:128 S1:64 ST:64 RR:64 G1:64 G2:64 CC:64 XR:8 RG:64 RT:64 MM:64 SCN:192 DMP:64 DF:128 "
-          "NEQ:32 JUNK:8 ACC:256 YB:320 UP:128")
+_add(F32, "N0:16 N1:16 N2:16 SC0:1 SC1:1 SC2:1 FC:32 MAP:64 LM:64 SM:568 TMPF:256 "
+          "ACOL:8 RA:64 RB:128 TB:128 ST:64 RR:64 G1:64 G2:64 CC:64 XR:8 RG:64 RT:64 MM:64 SCN:192 DMP:64 DF:128 "
+          "NEQ:32 JUNK:8 ACC:256 OD:256 YB:320 UP:128")
 _add(I32, "PI:1 INTC:16 TMPI:256")
-SMALL = {"OWN": 0, "C1": 16, "WD": 32, "WE": 48, "SQ": 64, "AN": 68, "SE": 72}
-LISTS = {"nat": 0, "out": 16, "bl": 32, "sh": 40, "rg": 44, "ac": 48, "w": 52, "w2": 54, "sn": 56, "ow": 60, "se": 62}
-_add(U16, "LST:64")
+SMALL = {"OWN": 0, "C1": 16, "WD": 32, "WE": 48, "SQ": 64, "AN": 68, "SE": 72, "MS": 80, "SEG": 96, "MT": 160, "OS": 224, "OB": 226,
+         "MK": 228, "NM": 244, "IOI": 248, "KT": 312, "K4": 376, "OFR": 440, "OFD": 504}
+LISTS = {"nat": 0, "out": 16, "bl": 32, "sh": 40, "rg": 44, "ac": 48, "w": 52, "w2": 54, "sn": 56, "ow": 60, "se": 62, "mk": 64}
+_add(U16, "LST:66")
+TILES = ("NT", "HT0", "HT1", "DT0", "DT1")
 SEMAPHORES = (["qg", "qv", "qs", "qt", "snt"] + [s + str(t) for s in ("sc", "dA", "dB", "hs") for t in range(R)]
               + ["m%d" % i for i in range(40)])
 
@@ -50,15 +55,42 @@ def _near(src, dst, away, topo):
     return [x for x in topo.engines(src, dst) if x not in away]
 
 
-def _plan(j, s, d, src, cores, topo):
+def _helpers(s, cores, topo):
+    return [c for c in topo.cores_of(cores[s]) if topo.die(c) == topo.die(cores[s]) and c not in cores][:3]
+
+
+def _half(h, s):
+    return [o for o in range(HALF * h, HALF * h + HALF) if o != s]
+
+
+def _calls(s, cores, topo):
+    fs = _far(s, cores, topo)
+    n = len(topo.engines(cores[s], cores[fs[0]])) // 2
+    return [[o for o in range(len(cores)) if o != s and o not in fs[n:]], fs[n:]]
+
+
+def _mask(s, d, dests, src, cores, topo):
     fs = _far(s, cores, topo)
     away = topo.engines(src, cores[fs[0]])
     if d not in fs:
         return _near(src, cores[d], away, topo)[:2]
-    half = len(away) // 2
-    one, two = (away[:half], away[half:]) if j % 2 == 0 else (away[half:], away[:half])
-    i = (fs.index(d) + 2 * j) % len(fs)
-    return [one[i]] if i < half else two[2 * (i - half):2 * (i - half) + 2]
+    fs = [o for o in dests if o in fs]
+    n = 2 if len(fs) > 2 else 4
+    i = n * fs.index(d)
+    return away[i:i + n]
+
+
+def _list_mask(s, d, cores, topo):
+    dests = [c for c in _calls(s, cores, topo) if d in c][0]
+    return _mask(s, d, dests, cores[s], cores, topo)
+
+
+def _parts(s, h):
+    return _half(h, s)
+
+
+def _hand_mask(s, d, src, cores, topo):
+    return _mask(s, d, _parts(s, d // HALF), src, cores, topo)[:2]
 
 
 def _to(core, topo):
@@ -66,28 +98,29 @@ def _to(core, topo):
     return DstId(rid=rid, pnc=pid)
 
 
-def _helper(s, cores, topo):
-    return [c for c in topo.cores_of(cores[s]) if topo.die(c) == topo.die(cores[s]) and c not in cores][0]
-
-
 def _delta_sem(T, s, d, t):
     return T.sem[("dA%d" if pos(s, d) < 3 else "dB%d") % t]
 
 
 def hand_on(g, core, s, cores, T, topo):
-    sent = 0
+    k = _helpers(s, cores, topo).index(core)
+    h = k if k < 2 else 1 - s // HALF
+    dests = _half(h, s)
+    arrived = NHAND if k < 2 else len(topo.engines(cores[s], cores[_far(s, cores, topo)[0]]))
     for t in range(R):
-        g.wait_ge(T.sem["hs%d" % t], NHAND)
+        g.wait_ge(T.sem["hs%d" % t], arrived)
         tf = []
-        for o in range(len(cores)):
-            if o != s:
-                p, e = pos(s, o), _plan(0, s, o, core, cores, topo)
-                sent += len(e)
-                tf.append(RemoteDMATransfer(dst_ids=[_to(cores[o], topo)], dma_engine_mask=bits(e), remote_sem=_delta_sem(T, s, o, t),
-                                            srcs=[T["c_HB%d" % t][:, 8 * o:8 * o + 8].bitcast(dt.uint8)],
-                                            dsts=[T["c_LA%d" % t][:, 16 + 8 * p:24 + 8 * p].bitcast(dt.uint8)]))
+        for o in dests:
+            p, i = pos(s, o), o - HALF * h
+            if k < 2:
+                src = T["c_HC%d" % t][:, 8 * i:8 * i + 8].bitcast(dt.uint8)
+                land = T["c_LA%d" % t][:, 16 + 8 * p:24 + 8 * p].bitcast(dt.uint8)
+            else:
+                src, land = T["z_HZ%d" % t][:, 8 * i:8 * i + 8], T["z_LA%d" % t][:, 16 + 8 * p:24 + 8 * p]
+            tf.append(RemoteDMATransfer(dst_ids=[_to(cores[o], topo)], dma_engine_mask=bits(_hand_mask(s, o, core, cores, topo)),
+                                        remote_sem=_delta_sem(T, s, o, t), srcs=[src], dsts=[land]))
         g.remote_dma_fused(tf, local_sem=T.sem.snt)
-    g.wait_ge(T.sem.snt, sent)
+    g.wait_ge(T.sem.snt, 2 * len(dests) * R)
 
 
 def rank_program(g, core, T, topo):
@@ -96,7 +129,7 @@ def rank_program(g, core, T, topo):
     me = T.rank_of(core)
     if me is None:
         for s in range(n_ranks):
-            if _helper(s, cores, topo) == core:
+            if core in _helpers(s, cores, topo):
                 hand_on(g, core, s, cores, T, topo)
         return
     r = me
@@ -113,6 +146,9 @@ def rank_program(g, core, T, topo):
             a = t[:, c0:c1] if step == 1 else t[:, c0:c1:step]
         else:
             a = t[p0:p1, c0:c1] if step == 1 else t[p0:p1, c0:c1:step]
+        if step == 4 and name in TILES:
+            b = c0 % 4
+            return (a, [(name, c0 - b, c1, 32 * b, 32 * b + 32)])
         return (a, [(name, c0, c1, p0, p1)])
 
     def ind(v, o):
@@ -220,6 +256,9 @@ def rank_program(g, core, T, topo):
     def tr(out, a):
         run("v", lambda: g.vector.transpose(out[0], a[0]), [a], [out])
 
+    def scan(out, a, b):
+        run("v", lambda: g.vector.tensor_tensor_scan(out[0], a[0], b[0], 0.0, A.mult, A.add), [a, b], [out])
+
     def fill(out, c):
         run("v", lambda: g.vector.memset(out[0], c), [], [out])
 
@@ -260,8 +299,8 @@ def rank_program(g, core, T, topo):
     others = [o for o in range(n_ranks) if o != me]
     afar = _far(me, cores, topo)
     away = topo.engines(core, cores[afar[0]])
-    def plan(j, s, d):
-        return _plan(j, s, d, cores[s], cores, topo)
+    helpers = _helpers(me, cores, topo)
+    mine = _half(me // HALF, me)
 
     def fused(reads, transfers):
         waits("g", [x for v in reads for x in v[1]], [])
@@ -272,29 +311,33 @@ def rank_program(g, core, T, topo):
     def send_scores(t):
         src, land, sem = w("SC%d" % t, 0, 1), T["N%d" % t][:, me:me + 1], T.sem["sc%d" % t]
         fused([src], [([cores[o] for o in afar], away, sem, src[0], land)]
-              + [([cores[o]], plan(0, me, o), sem, src[0], land) for o in others if o not in afar])
+              + [([cores[o]], _near(core, cores[o], away, topo)[:2], sem, src[0], land) for o in others if o not in afar])
 
     def score_count():
-        return sum(len(topo.engines(cores[s], core)) if s in afar else len(plan(0, s, me)) for s in others)
+        return sum(len(away) if s in afar else 2 for s in others)
 
-    def send_each(j, t, src_of, dst_of, reads):
-        fused(reads, [([cores[o]], plan(j, me, o), _delta_sem(T, me, o, t), src_of(o), dst_of(pos(me, o))) for o in others])
+    def delta_count(s):
+        direct = s // HALF == me // HALF
+        scales = _mask(s, me, _half(s // HALF, s), cores[s], cores, topo) if direct else _hand_mask(s, me, _helpers(s, cores, topo)[2], cores, topo)
+        codes = _hand_mask(s, me, _helpers(s, cores, topo)[me // HALF], cores, topo)
+        return len(codes) + len(scales) + len(_list_mask(s, me, cores, topo))
 
     QB = me % 4
+    DB = QB + 1 if QB < 3 else 2
     NB = 5 if QB == 3 else 4
     V0 = 32 if QB == 3 else 0
     RO = 32 * QB - V0
     CLASH = r % 4 == 0
     NEW = 160
 
+    load("s", w("VB", 0, 512), T.v[:, :])
     for b in range(NB):
         load("ys"[b % 2], w("PT", 128 * b, 128 * b + 128), (T.pr if b == QB else T.pd)[:, :])
-    load("y", w("VB", 0, 512), T.v[:, :])
-    load("s", w("XB", 0, 1024), T.x[:, :])
+    load("y", w("XB", 0, 1024), T.x[:, :])
     cw = w("c_W", 0, 512)
     load("y", (cw[0].bitcast(dt.uint8), cw[1]), T.wc[:, :])
     load("s", w("z_W", 0, 512), T.ws[:, :])
-    load("y", w("UB", 0, 512), T.u[:, :])
+    load("s", w("UB", 0, 512), T.u[:, :])
 
     TMP = [0]
     def ftmp(n):
@@ -304,6 +347,9 @@ def rank_program(g, core, T, topo):
     kt, ioi, mp = w("KT", 0, 64), w("IOI", 0, 64), w("MAP", 0, 64)
     iota(w("PI", 0, 1), [[0, 1]], 0, 1, small=False)
     fill(w("ONE", 0, 520), 1.0)
+    fill(w("ZB", 0, 512), 0.0)
+    fill(w("HT1", 128, 512), 0.0)
+    fill(w("DT1", 128, 512), 0.0)
     eb, one = w("EB", 0, 520), w("ONE", 0, 520)
     run("g", lambda: g.affine_select(eb[0], one[0], [[-1, 520]], A.is_equal, 0.0, 4, 4), [one], [eb])
     fnat, fbl, frg, fsh, fsn, fout, fw, fc1, f1, f2 = [ftmp(n) for n in (16, 4, 4, 4, 4, 16, 2, 16, 64, 64)]
@@ -317,6 +363,7 @@ def rank_program(g, core, T, topo):
     iota(kt, [[4, 2], [0, 32]])
     iota(w("VALS", 0, 64), [[4, 2], [0, 8], [1, 4]])
     iota(fw, [[128, 2]])
+    iota(w("MT", 0, 64), [[0, 16], [1, 4]])
 
     def col(j):
         return w("FC", j, j + 1)
@@ -327,7 +374,9 @@ def rank_program(g, core, T, topo):
             ts(o, i, sh, A.arith_shift_right, an, A.bitwise_and)
         else:
             ts(o, i, an, A.bitwise_and)
+    fill(w("SEG", 0, 64), 1.0)
     cp("v", w("FC", 0, 14), w("INTC", 0, 14))
+    fill(w("SEG", 32, 33), 0.0)
     C8P, CX, CSN, C16, CW2, CW, CNX, CND, C32K, COUT = range(14, 24)
     ts(col(C8P), col(P16), 8.0, A.mult)
     for h in range(2):
@@ -339,18 +388,19 @@ def rank_program(g, core, T, topo):
         quant("E", 128 * b, w("EB", 4 - b, 516 - b))
     sa(w("NB", 0, 520), eb, -1.0)
 
-    quant("PB0", 0, w("PT", 0, 128 * NB))
     quant("V", 0, w("VB", 0, 512))
+    quant("PB0", 0, w("PT", 0, 128 * NB))
 
-    def scores(t):
+    def scores(t, make):
         sc, n = "SC%d" % t, "N%d" % t
-        mm(0, 128, "PB%d" % t, 0, "V", 0)
-        cp("s", w(sc, 0, 1), w("ps", t, t + 1))
+        make(w(sc, 0, 1))
         send_scores(t)
         run("y", lambda: g.sync.dma_start(T[n][:, me:me + 1], T[sc][:, 0:1]), [w(sc, 0, 1)], [w(n, me, me + 1)], dma=True)
         arrive([w(n, a, b) for a, b in ((0, me), (me + 1, 8)) if b > a], "sc%d" % t, score_count())
 
-    scores(0)
+    mm(0, 128, "PB0", 0, "V", 0)
+    scores(0, lambda out: cp("s", out, w("ps", 0, 1)))
+    cp("s", w("OS", 0, 2), w("ps", 1, 3))
 
     quant("X", 0, w("XB", 0, 1024))
     pick("D0", 0, 256, "X", 256, ("LST", LISTS["nat"]))
@@ -364,7 +414,6 @@ def rank_program(g, core, T, topo):
     sa(f1, kt, 32.0)
     sa(w("K4", 0, 64), kt, 4.0, 256.0)
     sa(col(COUT), col(P8), 32.0, col(B3))
-    sa(w("ZB", 0, 512), w("EB", 0, 512), 0.0)
     for b in range(4):
         mm(b, 256, "W", 128 * b, "D0", 0)
     for h in range(2):
@@ -392,9 +441,8 @@ def rank_program(g, core, T, topo):
     ts(sni, sni, 7, A.bitwise_and)
     cp("v", lst("sh", 2), w("TMPI", 0, 2))
     ts(lst("sh", 2, 2), w("TMPI", 2, 4), 32.0, A.add)
-    ts(col(CW2), col(CNX), 16.0, A.mult)
+    ts(w("LM", 0, 64), ioi, col(P31), A.is_lt, TINY, A.mult)
     ts(lst("sn", 4), sni, 4.0, A.mult, col(M), A.add)
-    ts(w("LM", 0, 64), ioi, col(P31), A.is_lt)
 
     def relu(tile, b, cols, bk):
         o, i = w(tile, b, 4 * cols, 4), bank(bk, cols)
@@ -404,60 +452,78 @@ def rank_program(g, core, T, topo):
         relu("HT0", b, 256, b)
     cp("s", w("ACOL", 0, 2), w("ps", 2048, 3072, 512))
     relu("HT0", 3, 256, 3)
-    sa(w("INV0", 0, 512), w("EB", 0, 512), 0.0, 8.0)
     for b in range(4):
         mm(4 + b, 256, "E", 512 + 128 * b, "D0", 0, True, False)
-    quant("NX", 0, w("HT0", 0, 1024))
-    for b in range(4):
-        mm(4 + b, 256, "E", 128 * b, "NX", 0, False, True)
-    for b in range(4):
-        cp("s", w("DT0", b, 1024, 4), bank(4 + b, 256))
-    x1, x2, x3 = w("TMPI", 16, 80), w("TMPI", 80, 144), w("TMPI", 144, 208)
-    ts(f2, kt, float(r), A.is_lt, 31.0, A.mult)
-    ts(x1, ioi, col(C16), A.add)
-    ts(x3, kt, float(8 - r), A.add)
-    tt(x2, f2, ioi, A.add)
-    ts(x1, x1, 31, A.bitwise_and)
-    ts(x3, x3, 7, A.bitwise_and)
-    ts(x2, x2, col(C16), A.add)
-    tt(w("OFR", 0, 64), f1, x1, A.add)
-    ts(x2, x2, 31, A.bitwise_and)
-    ts(f2, x3, 32.0, A.mult, 256.0, A.add)
-    ts(col(CW), col(B1), 256.0, A.mult, col(CW2), A.add)
-    tt(w("OFD", 0, 64), f2, x2, A.add)
-    tt(col(CW), col(CW), col(C32K), A.add)
-    ts(lst("w2", 1), col(K1), 32.0, A.mult, col(CW2), A.add)
-    ts(lst("w", 2), fw, col(CW), A.add)
+
+    def arow():
+        cp("v", w("RA", 0, 64), ind(w("ACOL", 0, 2), lst("ac", 4)))
 
     def base(o):
         return 0 if o == me else 16 + 8 * pos(me, o)
-    for kind in range(2):
-        k = 0
-        while k < 8:
-            bs = base((k - r * kind) % 8)
-            e = k
-            while e < 8 and base((e - r * kind) % 8) == bs:
-                e += 1
-            v = w("VALS", 32 * kind + 4 * k, 32 * kind + 4 * e)
-            if bs:
-                sa(v, v, 1.0, float(bs))
-            k = e
+
+    own16, c1, sq = w("OWN", 0, 16), w("C1", 0, 16), w("SQ", 0, 4)
+    iota(own16, [[16, 16]])
+    iota(sq, [[16, 4]])
+    iota(fc1, [[4, 8], [0, 2]])
+    iota(fout, [[2, 16]])
+    y0, y1, y2, y3 = ftmp(1), ftmp(1), ftmp(1), ftmp(1)
+    ts(y0, col(B2), 4.0 * ((2 * r) % 8 - r), A.mult, col(M), A.add)
+    ts(y3, col(QQ), float(QB), A.is_equal, -2.0, A.mult)
+    ts(y2, col(K1), float(QB), A.is_equal, -2.0, A.mult)
+    ts(y0, y0, 4.0 * r, A.add)
+    ts(lst("mk", 1), y3, col(ODD), A.add, 2.0, A.add)
+    ts(lst("se", 1), y2, col(B0), A.add, 2.0, A.add)
+    ts(y1, y0, -1.0, A.mult, 32.0, A.add)
+    quant("AO", 0, w("ZB", 0, 512))
+    tt(y1, y1, col(B3), A.mult)
+    quant("DC0", 32, w("ZB", 0, 512))
+    ts(lst("ow", 1), y0, y1, A.add)
+    quant("D0", 256, w("ZB", 0, 512))
+    arow()
+    quant("NX", 0, w("HT0", 0, 1024))
+    for b in range(4):
+        mm(4 + b, 256, "E", 128 * b, "NX", 0, False, True)
+    ts(own16, own16, col(P16), A.add)
+    ts(sq, sq, col(P16), A.add, 32.0 * QB, A.add)
+    ts(lst("out", 16), fout, col(COUT), A.add)
+    tt(c1, fc1, own16, A.subtract)
+    if DB < QB:
+        ts(w("SQ", 2, 4), w("SQ", 2, 4), 32.0 * (DB - QB - 1), A.add)
+    for k0, k1, bs in ((0, me, base(0)), (me, me + 1, 0), (me + 1, 8, base(7))):
+        if k1 > k0:
+            v = w("C1", 2 * k0, 2 * k1)
+            ts(v, v, float(256 - bs), A.add)
+    for b in range(4):
+        cp("sv"[b % 2], w("DT0", b, 1024, 4), bank(4 + b, 256))
 
     def differences(name, c, src):
         tt(w(name, c, c + 63), w(src, 0, 63), w(src, 1, 64), A.subtract)
         cp("s", w(name, c + 31, c + 64, 32), w(src, 31, 64, 32))
 
-    def arow():
-        ra = w("RA", 0, 64)
-        cp("v", ra, ind(w("ACOL", 0, 2), lst("ac", 4)))
-        tr(w("AROW", 0, 64), ra)
+    x1, x2, x3 = w("TMPI", 16, 80), w("TMPI", 80, 144), w("TMPI", 144, 208)
+    later = [
+        lambda: ts(f2, kt, float(r), A.is_lt, 31.0, A.mult),
+        lambda: ts(x1, ioi, col(C16), A.add),
+        lambda: tt(x2, f2, ioi, A.add),
+        lambda: ts(x3, kt, float(8 - r), A.add),
+        lambda: ts(x1, x1, 31, A.bitwise_and),
+        lambda: ts(x2, x2, col(C16), A.add),
+        lambda: quant("DL", 0, w("DT0", 0, 1024)),
+        lambda: ts(x3, x3, 7, A.bitwise_and),
+        lambda: tt(w("OFR", 0, 64), f1, x1, A.add),
+        lambda: ts(x2, x2, 31, A.bitwise_and),
+        lambda: ts(f2, x3, 32.0, A.mult, 256.0, A.add),
+        lambda: differences("DF", 0, "OFR"),
+        lambda: tt(w("OFD", 0, 64), f2, x2, A.add),
+        lambda: ts(col(CW2), col(CNX), 16.0, A.mult),
+        lambda: differences("DF", 64, "OFD"),
+        lambda: ts(col(CW), col(B1), 256.0, A.mult, col(CW2), A.add),
+        lambda: ts(lst("w2", 1), col(K1), 32.0, A.mult, col(CW2), A.add),
+        lambda: tt(col(CW), col(CW), col(C32K), A.add)]
 
-    arow()
-    own16, c1 = w("OWN", 0, 16), w("C1", 0, 16)
-    iota(own16, [[16, 16]])
-    iota(w("SQ", 0, 4), [[16, 4]])
-    iota(fout, [[2, 16]])
-    iota(fc1, [[4, 8], [0, 2]])
+    def gap():
+        if later:
+            later.pop(0)()
 
     def unpack_parities(t):
         for b in range(4):
@@ -465,34 +531,18 @@ def rank_program(g, core, T, topo):
         for b in range(4):
             cp("s", w("ACC", 64 * b, 64 * b + 64), bank(4 + b, 64, RO))
 
-    def zeros(n, a, b):
-        sa(w(n, a, b), w("EB", a, b), 0.0)
-
-    def late_tables():
-        quant("DC0", 32, w("ZB", 0, 512))
-        y0, y1, y2 = ftmp(1), ftmp(1), ftmp(1)
-        ts(y0, col(B2), 4.0 * ((2 * r) % 8 - r), A.mult, col(M), A.add)
-        sa(own16, own16, 1.0, col(P16))
-        ts(y0, y0, 4.0 * r, A.add)
-        quant("D0", 256, w("ZB", 0, 512))
-        ts(y1, y0, -1.0, A.mult, 32.0, A.add)
-        tt(c1, fc1, own16, A.subtract)
-        tt(y1, y1, col(B3), A.mult)
-        ts(y2, col(K1), float(QB), A.is_equal, -2.0, A.mult)
-        ts(lst("ow", 1), y0, y1, A.add)
-        for k0, k1, bs in ((0, me, base(0)), (me, me + 1, 0), (me + 1, 8, base(7))):
-            if k1 > k0:
-                v = w("C1", 2 * k0, 2 * k1)
-                sa(v, v, 1.0, float(256 - bs))
-        ts(lst("se", 1), y2, col(B0), A.add, 2.0, A.add)
-        zeros("HT1", 128, 512)
-
-    def last_tables():
-        for t in range(1, R):
-            quant("DC%d" % t, 32, w("ZB", 0, 512))
-        quant("D1", 256, w("ZB", 0, 512))
-        for t in range(1, R):
-            sa(w("INV%d" % t, 0, 512), w("EB", 0, 512), 0.0, 8.0)
+    def entries():
+        for kind in range(2):
+            k = 0
+            while k < 8:
+                bs = base((k - r * kind) % 8)
+                e = k
+                while e < 8 and base((e - r * kind) % 8) == bs:
+                    e += 1
+                v = w("VALS", 32 * kind + 4 * k, 32 * kind + 4 * e)
+                if bs:
+                    sa(v, v, 1.0, float(bs))
+                k = e
 
     def choose(t):
         n = "N%d" % t
@@ -500,51 +550,62 @@ def rank_program(g, core, T, topo):
             for h, q in enumerate("vs" if t else "vv"):
                 cp(q, w(n, 8, 16, 1, 64 * h, 64 * h + 64), w(n, 0, 8, 1, 64 - 64 * h, 128 - 64 * h))
         rb, tb = w("RB", 0, 128), w("TB", 0, 128)
-        cp("v", rb, ind(w(n, 0, 16 if CLASH else 8), lst("bl", 8)))
-        tr(tb, rb)
-        s1, st, rr, g1, g2 = [w(x, 0, 64) for x in ("S1", "ST", "RR", "G1", "G2")]
-        tt(s1, w("AROW", 0, 64), w("TB", 0, 64), A.subtract)
-        tt(st, ind(w("TB", 64, 128), lst("sh", 4)), s1, A.subtract)
-        tr(rr, st)
-        tt(g1, st, rr, A.is_equal)
-        tt(g2, st, rr, A.is_lt)
-        tt(g1, g1, w("LM", 0, 64), A.mult)
-        def scan(h):
-            o, a, b = [w(x, 32 * h, 32 * h + 32) for x in ("CC", "G1", "G2")]
-            run("v", lambda: g.vector.tensor_tensor_scan(o[0], a[0], b[0], 0.0, A.add, A.add), [a, b], [o])
+        tt(w("RB", 0, 64), ind(w(n, 0, 8), lst("bl", 4)), w("RA", 0, 64), A.subtract)
+        cp("s" if t else "v", w("RB", 64, 128), ind(w(n, 0, 16 if CLASH else 8), lst("bl", 4, 4)))
+        sa(w("INV%d" % t, 0, 512), w("EB", 0, 512), 0.0, 8.0)
         if t == 0:
-            quant("DL", 0, w("DT0", 0, 1024))
-            differences("DF", 0, "OFR")
-            differences("DF", 64, "OFD")
-        scan(0)
-        scan(1)
+            entries()
+        gap()
+        tr(tb, rb)
+        gap()
+        st, rr, g1, g2, cc = [w(x, 0, 64) for x in ("ST", "RR", "G1", "G2", "CC")]
+        tt(st, ind(w("TB", 64, 128), lst("sh", 4)), w("TB", 0, 64), A.add)
+        gap()
+        tr(rr, st)
+        gap()
+        tt(g1, st, rr, A.subtract)
+        gap()
+        tt(g2, g1, w("LM", 0, 64), A.is_lt)
+        gap()
+        scan(cc, w("SEG", 0, 64), g2)
+        gap()
         for q in range(4):
             cp("vs"[q % 2], w("XR", 2, 4, 1, 32 * q, 32 * q + 32), w("CC", 31, 64, 32, 32 * (q ^ 1), 32 * (q ^ 1) + 32))
         cp("v", w("XR", 0, 2), w("CC", 31, 64, 32))
         cp("v", w("XR", 4, 8, 1, 0, 64), w("XR", 0, 4, 1, 64, 128))
         cp("s", w("XR", 4, 8, 1, 64, 128), w("XR", 0, 4, 1, 0, 64))
-        rg, rt, m = w("RG", 0, 64), w("RT", 0, 64), w("MM", 0, 64)
-        cp("v", rg, ind(w("XR", 0, 8), lst("rg", 4)))
-        tr(rt, rg)
-        ts(m, rt, col(M), A.not_equal)
-        def entry(k, tab, h, c):
-            o, a, b = w("SCN", 32 * k, 32 * k + 32), w("MM", 32 * h, 32 * h + 32), w(tab, c, c + 32)
-            run("v", lambda: g.vector.tensor_tensor_scan(o[0], a[0], b[0], 0.0, A.mult, A.add), [a, b], [o])
-        for h in range(2):
-            entry(h, "DMP", h, 32 * h)
-        entry(2, "DF", 0, 0)
+        gap()
+        rg, m, xr = w("RG", 0, 64), w("MM", 0, 64), w("XR", 0, 8)
+        tt(rg, ind(xr, lst("rg", 4)), w("MT", 0, 64), A.not_equal)
+        gap()
+        tr(m, rg)
+        gap()
+        scan(w("SCN", 0, 64), m, w("DMP", 0, 64))
+        if t:
+            scan(w("SCN", 64, 128), m, w("DF", 0, 64))
+        gap()
         cp("v", w("L1U", 0, 2), w("SCN", 31, 64, 32))
-        entry(3, "DF", 1, 32)
+        if t:
+            scan(w("SCN", 128, 192), m, w("DF", 64, 128))
+        gap()
         dc, sn, la, ll, wl = "DC%d" % t, "SN%d" % t, "LA%d" % t, "LL%d" % t, "WL%d" % t
         pick(dc, 0, 32, "DL", 256 + 32 * t, ("L1U", 0))
-        entry(4, "DF", 0, 64)
+        gap()
+        gap()
         pick(sn, 0, 64, dc, 32, ("LST", LISTS["sn"]))
-        hc = _helper(me, cores, topo)
-        fused([w("c_" + sn, 0, 64)], [([hc], _near(core, hc, away, topo)[:NHAND], T.sem["hs%d" % t],
-                                       T["c_" + sn][:, 0:64].bitcast(dt.uint8), T["c_HB%d" % t][:, 0:64].bitcast(dt.uint8))])
-        send_each(1, t, lambda o: T["z_" + sn][:, 8 * o:8 * o + 8],
-                  lambda p: T["z_" + la][:, 16 + 8 * p:24 + 8 * p], [w("z_" + sn, 0, 64)])
-        entry(5, "DF", 1, 96)
+        hs, close = T.sem["hs%d" % t], _near(core, helpers[0], away, topo)
+        fused([w("c_" + sn, 0, 64)], [([helpers[h]], close[NHAND * h:NHAND * h + NHAND], hs, T["c_" + sn][:, 32 * h:32 * h + 32].bitcast(dt.uint8),
+                                       T["c_HC%d" % t][:, 0:32].bitcast(dt.uint8)) for h in range(2)])
+        a = 32 * (1 - me // HALF)
+        fused([w("z_" + sn, 0, 64)], [([helpers[2]], away, hs, T["z_" + sn][:, a:a + 32], T["z_HZ%d" % t][:, 0:32])])
+        fused([w("z_" + sn, 0, 64)], [([cores[o]], _mask(me, o, mine, core, cores, topo), _delta_sem(T, me, o, t), T["z_" + sn][:, 8 * o:8 * o + 8],
+                                       T["z_" + la][:, 16 + 8 * pos(me, o):24 + 8 * pos(me, o)]) for o in mine])
+        while later:
+            gap()
+        if t == 0:
+            scan(w("SCN", 64, 128), m, w("DF", 0, 64))
+            ts(lst("w", 2), fw, col(CW), A.add)
+            scan(w("SCN", 128, 192), m, w("DF", 64, 128))
         l2 = w("L2U", 0, 4)
         cp("v", l2, w("SCN", 95, 192, 32))
         inv, vals = w("INV%d" % t, 0, 512), w("VALS", 0, 64)
@@ -552,15 +613,28 @@ def rank_program(g, core, T, topo):
         it = w("INVT", 0, 512)
         tr(it, inv)
         cp("v", w(wl, 0, 32), ind(it, lst("w", 2)))
-        send_each(2, t, lambda o: T[wl][:, 4 * o:4 * o + 4], lambda p: T[ll][:, 4 * p:4 * p + 4], [w(wl, 0, 32)])
+        for part in _calls(me, cores, topo):
+            fused([w(wl, 0, 32)], [([cores[o]], _list_mask(me, o, cores, topo), _delta_sem(T, me, o, t), T[wl][:, 4 * o:4 * o + 4],
+                                    T[ll][:, 4 * pos(me, o):4 * pos(me, o) + 4]) for o in part])
         for name, lo, hi in (("dA%d", 0, 3), ("dB%d", 3, 7)):
-            cnt = sum(len(plan(j, s, me)) for j in range(3) for s in others if lo <= pos(s, me) < hi)
+            cnt = sum(delta_count(s) for s in others if lo <= pos(s, me) < hi)
             arrive([w("c_" + la, 16 + 8 * lo, 16 + 8 * hi), w("z_" + la, 16 + 8 * lo, 16 + 8 * hi), w(ll, 4 * lo, 4 * hi)], name % t, cnt)
-        if t == 0:
-            late_tables()
+
+    def own_columns(t):
+        dc, la, wl = "DC%d" % t, "LA%d" % t, "WL%d" % t
         pick(la, 0, 16, dc, 34, ("LST", LISTS["ow"]))
-        pick("AR", 0, 64, la, 16, (wl, 4 * me))
+        pick("AO", 0, 64, la, 16, (wl, 4 * me))
         ts(w("NEQ", 28, 32), w(wl, 4 * me, 4 * me + 4), 8.0, A.not_equal)
+
+    def own_deltas():
+        for b in range(4):
+            mm(4 + b, 128, "E", 128 * b, "AO", 0)
+        for b in range(4):
+            acc = w("ACC", 64 * b, 64 * b + 64)
+            if me == 0:
+                tt(acc, acc, bank(4 + b, 64), A.add)
+            else:
+                cp("s", w("OD", 64 * b, 64 * b + 64), bank(4 + b, 64))
 
     def advance(t):
         d, dn, it = "D%d" % t, "D%d" % (t + 1), w("INVT", 0, 512)
@@ -568,30 +642,33 @@ def rank_program(g, core, T, topo):
         if t < R - 1:
             for b in range(4):
                 mm(b, 128, "W", 128 * b, d, 256)
-        if t == 0:
-            unpack_parities(0)
-            zeros("NT", 256, 512)
-            sa(w("SQ", 0, 4), w("SQ", 0, 4), 1.0, col(P16))
-            if QB:
-                sa(w("SQ", 0, 4), w("SQ", 0, 4), 1.0, 32.0 * QB)
-        if t == 1:
-            ts(lst("out", 16), fout, col(COUT), A.add)
-        wd, we = w("WD", 0, 16), w("WE", 0, 16)
-        cp("v", wd, ind(it, lst("w2", 1)))
-        ts(we, wd, 8.0, A.not_equal)
-        tt(wd, wd, c1, A.add)
-        tt(wd, wd, we, A.mult)
-        tt(wd, wd, own16, A.add)
-        cp("v", w("DLS", 0, 16), wd)
+        own_columns(t)
+        wd, we, dls = w("WD", 0, 16), w("WE", 0, 16), w("DLS", 0, 16)
+        rg, rt, mask, u = w("RG", 0, 64), w("RT", 0, 64), w("UP", 0, 64), w("UP", 64, 128)
+        row = [lambda: cp("v", wd, ind(it, lst("w2", 1))), lambda: ts(we, wd, 8.0, A.not_equal), lambda: tt(wd, wd, c1, A.add),
+               lambda: tt(wd, wd, we, A.mult), lambda: tt(wd, wd, own16, A.add), lambda: cp("v", dls, wd)]
+        moved = [lambda: cp("v", rg, ind(w("XR", 0, 8), lst("rg", 4))), lambda: tr(rt, rg), lambda: ts(mask, rt, 4.0, A.is_lt),
+                 lambda: tt(u, rt, w("K4", 0, 64), A.add), lambda: tt(u, u, mp, A.subtract), lambda: tt(u, u, mask, A.mult)]
+        for i in range(6):
+            row[i]()
+            if t < R - 1:
+                moved[i]()
         if t < R - 1:
             for b in range(4):
                 relu("HT1", b, 32, b)
+            tt(mp, mp, u, A.add)
             quant("NX", 256 + 32 * t, w("HT1", 0, 512))
+        if t == 0:
+            unpack_parities(0)
+        own_deltas()
         pick(dn, 0, 256, d, 288, ("DLS", 0))
         if t < R - 1:
+            differences("DMP", 0, "MAP")
             for h in range(2):
                 mm(4 + h, 128, dn, 128 * h, "U", 0)
             cp("s", w("ACOL", 0, 2), w("ps", 2048 + t + 1, 3072, 512))
+            if t == 0:
+                sa(w("K4", 0, 64), w("K4", 0, 64), 1.0, 32.0)
         else:
             pick("FD", 0, 256, dn, 256, ("LST", LISTS["out"]))
             mm(4, 256, "U", 0, "FD", 0)
@@ -603,71 +680,91 @@ def rank_program(g, core, T, topo):
                 store("y", T.osc[4 * k:4 * k + 4, 0:256], w("z_FD", 0, 256, 1, 32 * k, 32 * k + 4))
 
     def patch(t):
-        la, ll, pb = "LA%d" % t, "LL%d" % t, "PB%d" % t
-        pick("AR", 64, 192, la, 40, (ll, 0))
+        la, ll, pb, last = "LA%d" % t, "LL%d" % t, "PB%d" % t, t == R - 1
+        pick("AR", 0, 192, la, 40, (ll, 0))
         for b in range(4):
-            mm(b, 256, "E", 128 * b, "AR", 0)
-        pick("AR", 256, 256, la, 72, (ll, 12))
+            mm(b, 192, "E", 128 * b, "AR", 0)
+        pick("AR", 192, 256, la, 72, (ll, 12))
         for b in range(4):
-            mm(4 + b, 256, "E", 128 * b, "AR", 256)
+            mm(4 + b, 256, "E", 128 * b, "AR", 192)
         ts(w("NEQ", 0, 28), w(ll, 0, 28), 8.0, A.not_equal)
         for c in range(4):
             v, o, z = w("NEQ", c, 32, 4), w("JUNK", 0, 8), w("AN", c, c + 1)
             run("s", lambda: g.scalar.activation(o[0], v[0], F.Copy, accum_out=z[0]), [v], [o, z])
-        def slot(s):
-            return 0 if s == me else 1 + pos(s, me)
-        def add(s, b):
-            k = slot(s)
-            acc = w("ACC", 64 * b, 64 * b + 64)
-            out = w("NT", b, 256, 4) if s == n_ranks - 1 else acc
-            tt(out, acc, bank(b if k < 4 else 4 + b, 64, 64 * (k % 4)), A.add)
-        free, seq, ready, step = 0.0, [], [0.0] * 4, [0] * 4
-        while len(seq) < 4 * n_ranks:
-            can = [(max(free, ready[b], 4.5 * ((1 if slot(step[b]) < 4 else 5) + b)), step[b], b) for b in range(4) if step[b] < n_ranks]
+        finals = [(0, 64, QB)] if QB < 3 else [(0, 32, QB), (32, 64, DB)]
+        if not last:
+            finals += [(32, 64, k) for k in range(4) if k not in (QB, DB)]
+        elif QB == 3:
+            pass
+        def source(s, b, c0, c1):
+            if s == me:
+                return w("OD", 64 * b + c0, 64 * b + c1)
+            p = pos(s, me)
+            k, c = (b, 64 * p) if p < 3 else (4 + b, 64 * (p - 3))
+            return bank(k, c1 - c0, c + c0)
+        def add(i, b):
+            if i < n_ranks - 1:
+                acc = w("ACC", 64 * b, 64 * b + 64)
+                tt(acc, acc, source(i, b, 0, 64), A.add)
+            else:
+                c0, c1, k = finals[i - n_ranks + 1]
+                tt(w("NT", 128 * k + b, 128 * k + 4 * (c1 - c0), 4), w("ACC", 64 * b + c0, 64 * b + c1), source(n_ranks - 1, b, c0, c1), A.add)
+        def there(s, b):
+            return 0.0 if s == me else 3.5 * (b + 1) if pos(s, me) < 3 else 14.0 + 4.5 * (b + 1)
+        end = n_ranks - 1 + len(finals)
+        free, seq, ready, step = 0.0, [], [0.0] * 4, [1 if me == 0 else 0] * 4
+        while min(step) < end:
+            can = [(max(free, ready[b], there(min(step[b], n_ranks - 1), b)), step[b], b) for b in range(4) if step[b] < end]
             start, s, b = min(can)
             seq.append((s, b))
-            free, ready[b], step[b] = start + 1, start + 3, s + 1
-        se = w("SE", 0, 4)
+            free, step[b] = start + (2 if s == me else 1), s + 1
+            if s < n_ranks - 1:
+                ready[b] = free + 2
+        ms, se, mk, ob = w("MS", 0, 4), w("SE", 0, 4), w("MK", 0, 16), w("OB", 0, 2)
+        aside = [lambda: ts(ms, w("AN", 0, 4), 0.0, A.is_gt)]
+        table = [lambda: ts(se, ms, float(NEW), A.mult),
+                 lambda: tt(se, se, sq, A.add),
+                 lambda: cp("v", w("SEL", 0, 16), ind(se, lst("se", 1)))]
+        if last:
+            aside += table
+        else:
+            aside += [lambda: cp("v", mk, ind(ms, lst("mk", 1))),
+                      lambda: ts(w("NM", 0, 1), w("MK", 0, 1), 0.0, A.is_equal),
+                      lambda: ts(ob, w("OS", 0, 2), w("NM", 0, 1), A.mult)]
         for i, (s, b) in enumerate(seq):
             add(s, b)
-            if i == 2 * n_ranks + 3:
-                ts(se, w("AN", 0, 4), 0.0, A.is_gt, float(NEW - 32 * QB), A.mult)
-            if i == 2 * n_ranks + 6:
-                tt(se, se, w("SQ", 0, 4), A.add)
-            if i == 2 * n_ranks + 9:
-                cp("v", w("SEL", 0, 16), ind(se, lst("se", 1)))
+            if aside and i >= 2 * n_ranks + 1 and i % 3 == 1:
+                aside.pop(0)()
+        while aside:
+            aside.pop(0)()
         quant(pb, NEW, w("NT", 0, 512))
-        pick("PB%d" % (t + 1), 0, 32 * NB, pb, 288, ("SEL", 0))
-        if t < R - 1:
-            scores(t + 1)
-            unpack_parities(t + 1)
-            arow()
+        if not last:
+            mm(0, 128, pb, NEW, "V", 0)
+            scores(t + 1, lambda out: sa(out, w("ps", t + 1, t + 2), w("MK", 0, 1), w("OB", t, t + 1)))
             if t == 0:
-                zeros("DT1", 128, 512)
+                sa(w("OS", 1, 2), w("ps", 2, 3), w("MK", 0, 1), w("OB", 1, 2))
+            for f in table:
+                f()
+        pick("PB%d" % (t + 1), 0, 32 * NB, pb, 288, ("SEL", 0))
+        if not last:
             for b in range(4):
                 mm(4 + b, 128, "E", 512 + 128 * b, "D%d" % t, 256, True, False)
                 mm(4 + b, 128, "E", 128 * b, "NX", 256 + 32 * t, False, True)
-            mask, u = w("UP", 0, 64), w("UP", 64, 128)
-            rt = w("RT", 0, 64)
-            ts(mask, rt, 4.0, A.is_lt)
-            tt(u, rt, w("K4", 0, 64), A.add)
-            tt(u, u, mp, A.subtract)
-            tt(u, u, mask, A.mult)
-            tt(mp, mp, u, A.add)
-            differences("DMP", 0, "MAP")
-            sa(w("K4", 0, 64), w("K4", 0, 64), 1.0, 32.0)
             for b in range(4):
                 cp("vs"[b % 2], w("DT1", b, 128, 4), bank(4 + b, 32))
             quant("DL", 256 + 32 * t, w("DT1", 0, 512))
+            arow()
+            unpack_parities(t + 1)
+            quant("DC%d" % (t + 1), 32, w("ZB", 0, 512))
             if t == 0:
-                last_tables()
+                quant("D1", 256, w("ZB", 0, 512))
         else:
-            last, c = "PB%d" % R, 32 * QB
-            mm(0, 128, "V", 0, last, V0)
-            cc = w("c_" + last, c, c + 64)
+            out, c = "PB%d" % R, 32 * QB
+            mm(0, 128, "V", 0, out, V0)
+            cc = w("c_" + out, c, c + 64)
             store("y", T.oc[:, 1024:1280], (cc[0].bitcast(dt.uint8), cc[1]))
             for k in range(4):
-                store("ys"[k % 2], T.osc[4 * k:4 * k + 4, 256:320], w("z_" + last, c, c + 64, 1, 32 * k, 32 * k + 4))
+                store("ys"[k % 2], T.osc[4 * k:4 * k + 4, 256:320], w("z_" + out, c, c + 64, 1, 32 * k, 32 * k + 4))
             cp("v", w("YB", 256, 320), bank(0, 64, RO))
             store("s", T.y[:, 256:320], w("YB", 256, 320))
 

@@ -5,6 +5,9 @@ R = 3
 HALF = 4
 NHAND = 4
 TINY = 2.0 ** -110
+MID = 124
+OLD = 128
+LAP = 80
 FP8, U8, BF, F32, I32, U16 = "float8_e4m3fn_x4", "uint8", "bfloat16", "float32", "int32", "uint16"
 SCRATCH = {"ps": ("psum", [128, 4096], F32)}
 
@@ -19,24 +22,29 @@ def _add(d, text, mx=False):
             SCRATCH[name] = ("sbuf", [128, int(n)], d)
 
 
-_add(BF, "XB:1024 PT:640 UB:512 VB:512 ONE:520 EB:520 NB:520 ZB:512 HT0:1024 DT0:1024 HT1:512 DT1:512 NT:512 "
-         "INV0:512 INV1:512 INV2:512 INVT:512 VALS:64")
-_add(FP8, "X:256 U:128 V:128 W:512 E:1024 D0:384 D1:384 D2:384 D3:256 FD:256 NX:416 DL:416 PB0:288 PB1:288 PB2:288 "
-          "PB3:160 DC0:160 DC1:160 DC2:160 SN0:64 SN1:64 SN2:64 LA0:72 LA1:72 LA2:72 AR:448 AO:128", mx=True)
+_add(BF, "XB:1024 PT:512 UB:512 VB:512 ONE:520 EB:520 NB:520 ZB:512 HT0:1024 DT0:1024 HT1:512 DT1:512 NT:512 "
+         "INV0:256 INV1:256 INV2:256 INVT:256 VALS:32 KX0:64 KX1:64 KX2:64 WK0:32 WK1:32 WK2:32 KW:354 CT:848 "
+         "GG:192 HH:320 HHT:320 SH:320 MS:128")
+_add(FP8, "X:256 U:128 V:128 W:512 E:1024 D0:384 D1:384 D2:384 D3:256 FD:256 NX:416 DL:416 PB0:256 PB1:256 PB2:256 "
+          "PB3:256 DC0:32 DC1:32 DC2:32 SN0:64 SN1:64 SN2:64 LA0:144 LA1:144 LA2:144 AR:128", mx=True)
 _add(FP8, "c_HC0:32 c_HC1:32 c_HC2:32")
 _add(U8, "z_HZ0:32 z_HZ1:32 z_HZ2:32")
-_add(U16, "WL0:32 WL1:32 WL2:32 LL0:28 LL1:28 LL2:28 L1U:2 L2U:4 DLS:16 SEL:16")
-_add(F32, "N0:16 N1:16 N2:16 SC0:1 SC1:1 SC2:1 FC:32 MAP:64 LM:64 SM:568 TMPF:256 "
-          "ACOL:8 RA:64 RB:128 TB:128 ST:64 RR:64 G1:64 G2:64 CC:64 XR:8 RG:64 RT:64 MM:64 SCN:192 DMP:64 DF:128 "
-          "NEQ:32 JUNK:8 ACC:256 OD:256 YB:320 UP:128")
+_add(F32, "N0:16 N1:16 N2:16 SC0:1 SC1:1 SC2:1 FC:64 MAP:64 LM:64 SM:512 TMPF:320 "
+          "ACOL:8 RA:64 RB:128 TB:128 ST:64 RR:64 G1:64 G2:64 CC:64 XR:8 RG:64 RT:64 MM:64 SCN:128 DMP:64 DF:64 "
+          "DK:32 YB:320 UP:128")
 _add(I32, "PI:1 INTC:16 TMPI:256")
-SMALL = {"OWN": 0, "C1": 16, "WD": 32, "WE": 48, "SQ": 64, "AN": 68, "SE": 72, "MS": 80, "SEG": 96, "MT": 160, "OS": 224, "OB": 226,
-         "MK": 228, "NM": 244, "IOI": 248, "KT": 312, "K4": 376, "OFR": 440, "OFD": 504}
-LISTS = {"nat": 0, "out": 16, "bl": 32, "sh": 40, "rg": 44, "ac": 48, "w": 52, "w2": 54, "sn": 56, "ow": 60, "se": 62, "mk": 64}
-_add(U16, "LST:66")
+ALIAS = {}
+for _buf, _text in (("SM", "OWN:0 C1:16 WD:32 WE:48 SQ:64 ALF:68 SX:72 SEG:96 MT:160 IOI:248 KTB:312 K4:376 OFR:440"),
+                    ("CT", "TBL:0 WT:144 MASK:272 SEGG:336 SEGH:528"),
+                    ("KW", "RGK:0 MK:32 SK:64 KB:96 KT:128 CN:160 VPB:352 VDB:353"),
+                    ("LW", "DLS:0 SEL:16 AL:32 L1U:40 L2U:42")):
+    for _item in _text.split(" "):
+        ALIAS[_item.split(":")[0]] = (_buf, int(_item.split(":")[1]))
+LISTS = {"nat": 0, "out": 16, "bl": 32, "sh": 40, "rg": 44, "ac": 48, "w2": 52, "r2": 54, "sn": 56, "ow": 60, "se": 62, "sl": 64, "pp": 66}
+_add(U16, "LST:70 LW:44")
 TILES = ("NT", "HT0", "HT1", "DT0", "DT1")
-SEMAPHORES = (["qg", "qv", "qs", "qt", "snt"] + [s + str(t) for s in ("sc", "dA", "dB", "hs") for t in range(R)]
-              + ["m%d" % i for i in range(40)])
+SEMAPHORES = (["qg", "qv", "qs", "qt", "snt"] + [s + str(t) for s in ("sc", "dl", "ls", "hs") for t in range(R)]
+              + ["m%d" % i for i in range(48)])
 
 
 def pos(s, d):
@@ -85,12 +93,8 @@ def _list_mask(s, d, cores, topo):
     return _mask(s, d, dests, cores[s], cores, topo)
 
 
-def _parts(s, h):
-    return _half(h, s)
-
-
 def _hand_mask(s, d, src, cores, topo):
-    return _mask(s, d, _parts(s, d // HALF), src, cores, topo)[:2]
+    return _mask(s, d, _half(d // HALF, s), src, cores, topo)[:2]
 
 
 def _to(core, topo):
@@ -98,17 +102,12 @@ def _to(core, topo):
     return DstId(rid=rid, pnc=pid)
 
 
-def _delta_sem(T, s, d, t):
-    return T.sem[("dA%d" if pos(s, d) < 3 else "dB%d") % t]
-
-
 def hand_on(g, core, s, cores, T, topo):
     k = _helpers(s, cores, topo).index(core)
     h = k if k < 2 else 1 - s // HALF
     dests = _half(h, s)
-    arrived = NHAND if k < 2 else len(topo.engines(cores[s], cores[_far(s, cores, topo)[0]]))
     for t in range(R):
-        g.wait_ge(T.sem["hs%d" % t], arrived)
+        g.wait_ge(T.sem["hs%d" % t], NHAND if k < 2 else 2 * NHAND)
         tf = []
         for o in dests:
             p, i = pos(s, o), o - HALF * h
@@ -118,7 +117,7 @@ def hand_on(g, core, s, cores, T, topo):
             else:
                 src, land = T["z_HZ%d" % t][:, 8 * i:8 * i + 8], T["z_LA%d" % t][:, 16 + 8 * p:24 + 8 * p]
             tf.append(RemoteDMATransfer(dst_ids=[_to(cores[o], topo)], dma_engine_mask=bits(_hand_mask(s, o, core, cores, topo)),
-                                        remote_sem=_delta_sem(T, s, o, t), srcs=[src], dsts=[land]))
+                                        remote_sem=T.sem["dl%d" % t], srcs=[src], dsts=[land]))
         g.remote_dma_fused(tf, local_sem=T.sem.snt)
     g.wait_ge(T.sem.snt, 2 * len(dests) * R)
 
@@ -139,8 +138,8 @@ def rank_program(g, core, T, topo):
     ndma = [0]
 
     def w(name, c0, c1, step=1, p0=0, p1=128):
-        if name in SMALL:
-            name, c0, c1 = "SM", c0 + SMALL[name], c1 + SMALL[name]
+        if name in ALIAS:
+            name, c0, c1 = ALIAS[name][0], c0 + ALIAS[name][1], c1 + ALIAS[name][1]
         t = T[name]
         if p0 == 0 and p1 == 128:
             a = t[:, c0:c1] if step == 1 else t[:, c0:c1:step]
@@ -273,12 +272,12 @@ def rank_program(g, core, T, topo):
         c, z = w("c_" + name, c0, c0 + n), w("z_" + name, c0, c0 + n)
         run("v", lambda: g.vector.quantize_mx(c[0], z[0], src[0]), [src], [c, z])
 
-    def pick(dst, d0, n, src, width, off):
+    def pick(dst, d0, n, src, width, off, a0=0):
         b, k = off
         o = w(b, k, k + n // 16)
-        co, ci = w("c_" + dst, d0, d0 + n), w("c_" + src, 0, width)
+        co, ci = w("c_" + dst, d0, d0 + n), w("c_" + src, a0, a0 + width)
         run("v", lambda: g.vector.tensor_copy(co[0].bitcast(dt.uint32), ci[0].bitcast(dt.uint32).indirect(o[0])), [ci, o], [co])
-        zo, zi = w("z_" + dst, d0, d0 + n), w("z_" + src, 0, width)
+        zo, zi = w("z_" + dst, d0, d0 + n), w("z_" + src, a0, a0 + width)
         run("s", lambda: g.scalar.activation(zo[0], zi[0].indirect(o[0]), F.Copy), [zi, o], [zo])
 
     def mm(bank, n, lhs, l0, rhs, r0, start=True, stop=True):
@@ -320,110 +319,126 @@ def rank_program(g, core, T, topo):
         direct = s // HALF == me // HALF
         scales = _mask(s, me, _half(s // HALF, s), cores[s], cores, topo) if direct else _hand_mask(s, me, _helpers(s, cores, topo)[2], cores, topo)
         codes = _hand_mask(s, me, _helpers(s, cores, topo)[me // HALF], cores, topo)
-        return len(codes) + len(scales) + len(_list_mask(s, me, cores, topo))
+        return len(codes) + len(scales)
 
     QB = me % 4
     DB = QB + 1 if QB < 3 else 2
-    NB = 5 if QB == 3 else 4
-    V0 = 32 if QB == 3 else 0
-    RO = 32 * QB - V0
     CLASH = r % 4 == 0
-    NEW = 160
 
     load("s", w("VB", 0, 512), T.v[:, :])
-    for b in range(NB):
+    for b in range(4):
         load("ys"[b % 2], w("PT", 128 * b, 128 * b + 128), (T.pr if b == QB else T.pd)[:, :])
     load("y", w("XB", 0, 1024), T.x[:, :])
+    load("s", w("UB", 0, 512), T.u[:, :])
     cw = w("c_W", 0, 512)
     load("y", (cw[0].bitcast(dt.uint8), cw[1]), T.wc[:, :])
     load("s", w("z_W", 0, 512), T.ws[:, :])
-    load("s", w("UB", 0, 512), T.u[:, :])
 
     TMP = [0]
     def ftmp(n):
         a = TMP[0]
         TMP[0] += n
         return w("TMPF", a, a + n)
-    kt, ioi, mp = w("KT", 0, 64), w("IOI", 0, 64), w("MAP", 0, 64)
+    kt, ioi, mp = w("KTB", 0, 64), w("IOI", 0, 64), w("MAP", 0, 64)
+    fnat, fbl, frg, fsh, fsn, fout, fr2, fc1, f1, fa, fb, fh, fkp, ktf, fm = [ftmp(n) for n in (16, 4, 4, 4, 4, 16, 2, 16, 64, 2, 2, 2, 32, 32, 64)]
     iota(w("PI", 0, 1), [[0, 1]], 0, 1, small=False)
     fill(w("ONE", 0, 520), 1.0)
-    fill(w("ZB", 0, 512), 0.0)
-    fill(w("HT1", 128, 512), 0.0)
-    fill(w("DT1", 128, 512), 0.0)
-    eb, one = w("EB", 0, 520), w("ONE", 0, 520)
-    run("g", lambda: g.affine_select(eb[0], one[0], [[-1, 520]], A.is_equal, 0.0, 4, 4), [one], [eb])
-    fnat, fbl, frg, fsh, fsn, fout, fw, fc1, f1, f2 = [ftmp(n) for n in (16, 4, 4, 4, 4, 16, 2, 16, 64, 64)]
-    iota(fnat, [[1, 8], [128, 2]])
-    iota(fbl, [[4, 2], [0, 2]])
-    iota(fsh, [[0, 2], [16, 2]])
-    iota(ioi, [[0, 2], [1, 32]])
-    iota(frg, [[1, 2], [0, 2]])
-    iota(fsn, [[2, 4]])
-    iota(mp, [[128, 2], [1, 32]])
-    iota(kt, [[4, 2], [0, 32]])
-    iota(w("VALS", 0, 64), [[4, 2], [0, 8], [1, 4]])
-    iota(fw, [[128, 2]])
-    iota(w("MT", 0, 64), [[0, 16], [1, 4]])
+    sa(w("ZB", 0, 512), w("ONE", 0, 512), 0.0)
+    sa(w("HT1", 128, 512), w("ONE", 0, 384), 0.0)
+    sa(w("DT1", 128, 512), w("ONE", 0, 384), 0.0)
 
     def col(j):
         return w("FC", j, j + 1)
-    P16, P31, KK, QQ, B2, B3, Q0, Q1, M, ODD, B0, B1, K1, P8 = range(14)
-    for j, (sh, an) in enumerate(((0, 15), (0, 31), (2, 3), (5, 3), (2, 1), (3, 1), (5, 1), (6, 1), (0, 3), (4, 1), (0, 1), (1, 1), (1, 7), (0, 7))):
+    P16, P31, KK, QQ, B2, B3, Q0, Q1, M, ODD, B0, B1, K1, P8, K2 = range(15)
+    for j, (sh, an) in enumerate(((0, 15), (0, 31), (2, 3), (5, 3), (2, 1), (3, 1), (5, 1), (6, 1), (0, 3), (4, 1), (0, 1), (1, 1), (1, 7), (0, 7), (2, 7))):
         o, i = w("INTC", j, j + 1), w("PI", 0, 1)
         if sh:
             ts(o, i, sh, A.arith_shift_right, an, A.bitwise_and)
         else:
             ts(o, i, an, A.bitwise_and)
+    C8P, CX, CSN, C16, CW2, CNX, CND, C32K, COUT, KR, SHF, PC, PC3, VP, VD, OP, C1P, MK1, SU, Y0, Y2 = range(16, 37)
     fill(w("SEG", 0, 64), 1.0)
-    cp("v", w("FC", 0, 14), w("INTC", 0, 14))
+    cp("v", w("FC", 0, 15), w("INTC", 0, 15))
     fill(w("SEG", 32, 33), 0.0)
-    C8P, CX, CSN, C16, CW2, CW, CNX, CND, C32K, COUT = range(14, 24)
-    ts(col(C8P), col(P16), 8.0, A.mult)
     for h in range(2):
         fill(lst("ac", 2, 2 * h), h)
-    tt(col(CNX), col(B2), col(Q0), A.not_equal)
-    tt(col(CND), col(B3), col(Q1), A.not_equal)
-    ts(lst("nat", 16), fnat, col(C8P), A.add)
-    for b in range(4):
-        quant("E", 128 * b, w("EB", 4 - b, 516 - b))
-    sa(w("NB", 0, 520), eb, -1.0)
+    eb, one = w("EB", 0, 520), w("ONE", 0, 520)
+    run("g", lambda: g.affine_select(eb[0], one[0], [[-1, 520]], A.is_equal, 0.0, 4, 4), [one], [eb])
+    iota(fnat, [[1, 8], [128, 2]])
+    iota(fbl, [[4, 2], [0, 2]])
+    iota(fsh, [[0, 2], [16, 2]])
 
     quant("V", 0, w("VB", 0, 512))
-    quant("PB0", 0, w("PT", 0, 128 * NB))
+    quant("PB0", OLD, w("PT", 0, 512))
 
-    def scores(t, make):
+    def scores(t):
         sc, n = "SC%d" % t, "N%d" % t
-        make(w(sc, 0, 1))
+        mm(0, 128, "PB%d" % t, OLD, "V", 0)
+        cp("s", w(sc, 0, 1), w("ps", t, t + 1))
         send_scores(t)
         run("y", lambda: g.sync.dma_start(T[n][:, me:me + 1], T[sc][:, 0:1]), [w(sc, 0, 1)], [w(n, me, me + 1)], dma=True)
         arrive([w(n, a, b) for a, b in ((0, me), (me + 1, 8)) if b > a], "sc%d" % t, score_count())
 
-    mm(0, 128, "PB0", 0, "V", 0)
-    scores(0, lambda out: cp("s", out, w("ps", 0, 1)))
-    cp("s", w("OS", 0, 2), w("ps", 1, 3))
+    scores(0)
+    iota(frg, [[1, 2], [0, 2]])
+    iota(fsn, [[2, 4]])
+    iota(ioi, [[0, 2], [1, 32]])
+    iota(w("MT", 0, 64), [[0, 16], [1, 4]])
+    iota(fr2, [[4, 2]])
+    iota(mp, [[128, 2], [1, 32]])
+    iota(kt, [[4, 2], [0, 32]])
+    iota(w("VALS", 0, 32), [[0, 8], [1, 4]])
+    own16, c1, sq = w("OWN", 0, 16), w("C1", 0, 16), w("SQ", 0, 4)
+    iota(own16, [[16, 16]])
+    iota(sq, [[16, 4]])
+    iota(fc1, [[4, 8], [0, 2]])
+    iota(fkp, [[8, 32]], -MID)
+    iota(fm, [[16, 2], [0, 2], [1, 16]])
+    iota(w("WT", 0, 128), [[16, 4], [0, 2], [1, 16]])
+    iota(fout, [[2, 16]])
 
+    ts(col(C8P), col(P16), 8.0, A.mult)
+    tt(col(CNX), col(B2), col(Q0), A.not_equal)
+    tt(col(CND), col(B3), col(Q1), A.not_equal)
+    ts(lst("nat", 16), fnat, col(C8P), A.add)
+    sa(w("NB", 0, 520), eb, -1.0)
     quant("X", 0, w("XB", 0, 1024))
     pick("D0", 0, 256, "X", 256, ("LST", LISTS["nat"]))
     quant("U", 0, w("UB", 0, 512))
-    sa(col(C32K), col(KK), 32.0)
-    sa(kt, kt, 1.0, col(KK))
-    sa(col(C16), col(ODD), 16.0)
-    sa(mp, mp, 1.0, col(C32K))
-    sa(w("DMP", 0, 64), mp, 0.0, -1.0)
-    cp("s", w("DMP", 31, 64, 32), w("MAP", 31, 64, 32))
-    sa(f1, kt, 32.0)
-    sa(w("K4", 0, 64), kt, 4.0, 256.0)
-    sa(col(COUT), col(P8), 32.0, col(B3))
-    for b in range(4):
+    for b in range(2):
         mm(b, 256, "W", 128 * b, "D0", 0)
     for h in range(2):
         mm(4 + h, 128, "D0", 128 * h, "U", 0)
+    for b in range(2, 4):
+        mm(b, 256, "W", 128 * b, "D0", 0)
     for b in range(4):
         quant("E", 512 + 128 * b, w("NB", 4 - b, 516 - b))
+
+    def relu(tile, b, cols, bk):
+        o, i = w(tile, b, 4 * cols, 4), bank(bk, cols)
+        run("s", lambda: g.scalar.activation(o[0], i[0], F.Relu, scale=0.0625), [i], [o])
+
+    relu("HT0", 0, 256, 0)
+    relu("HT0", 1, 256, 1)
+    cp("s", w("ACOL", 0, 2), w("ps", 2048, 3072, 512))
+    relu("HT0", 2, 256, 2)
+    relu("HT0", 3, 256, 3)
+    sa(col(C32K), col(KK), 32.0)
+    sa(col(C16), col(ODD), 16.0)
+    sa(kt, kt, 1.0, col(KK))
+    sa(mp, mp, 1.0, col(C32K))
+    sa(w("DMP", 0, 64), mp, 0.0, -1.0)
+    sa(f1, kt, 32.0)
+    cp("s", w("DMP", 31, 64, 32), w("MAP", 31, 64, 32))
+    for b in range(4):
+        mm(4 + b, 256, "E", 512 + 128 * b, "D0", 0, True, False)
     bi, shi, sni = w("TMPI", 12, 16), w("TMPI", 0, 4), w("TMPI", 4, 8)
-    ts(lst("bl", 4), fbl, col(QQ), A.add)
+    t0, b0, b1, hh = [w("TMPI", a, a + 2) for a in (144, 146, 148, 150)]
+    kti, k0 = w("TMPI", 80, 112), ktf[1][0][1]
+    ts(col(KR), col(Q1), float(r), A.mult, col(KK), A.add)
     ts(bi, fbl, col(QQ), A.add, float(8 - r), A.add)
     ts(shi, fsh, col(P16), A.add)
+    ts(t0, fr2, col(KR), A.add)
     ts(col(CX), col(CND), 2.0, A.mult, col(CNX), A.add)
     ts(col(CSN), col(B2), float(r), A.mult, col(B3), A.add)
     ts(bi, bi, 7, A.bitwise_and)
@@ -432,117 +447,97 @@ def rank_program(g, core, T, topo):
         if n:
             v = w("TMPI", 2 * h, 2 * h + 2, 1, 0, 32 * n)
             ts(v, v, 31.0, A.add)
+    ts(t0, t0, 7, A.bitwise_and)
     ts(col(CX), col(CX), 2.0, A.mult)
     ts(sni, fsn, col(CSN), A.add)
     ts(lst("bl", 4, 4), bi, 8.0 if CLASH else 0.0, A.add)
     ts(shi, shi, 31, A.bitwise_and)
-    tt(col(CNX), col(B0), col(ODD), A.not_equal)
+    ts(b0, t0, 1, A.bitwise_and)
     ts(lst("rg", 4), frg, col(CX), A.add)
     ts(sni, sni, 7, A.bitwise_and)
     cp("v", lst("sh", 2), w("TMPI", 0, 2))
     ts(lst("sh", 2, 2), w("TMPI", 2, 4), 32.0, A.add)
-    ts(w("LM", 0, 64), ioi, col(P31), A.is_lt, TINY, A.mult)
+    ts(lst("bl", 4), fbl, col(QQ), A.add)
     ts(lst("sn", 4), sni, 4.0, A.mult, col(M), A.add)
-
-    def relu(tile, b, cols, bk):
-        o, i = w(tile, b, 4 * cols, 4), bank(bk, cols)
-        run("s", lambda: g.scalar.activation(o[0], i[0], F.Relu, scale=0.0625), [i], [o])
-
-    for b in range(3):
-        relu("HT0", b, 256, b)
-    cp("s", w("ACOL", 0, 2), w("ps", 2048, 3072, 512))
-    relu("HT0", 3, 256, 3)
+    ts(w("LM", 0, 64), ioi, col(P31), A.is_lt, TINY, A.mult)
     for b in range(4):
-        mm(4 + b, 256, "E", 512 + 128 * b, "D0", 0, True, False)
+        quant("E", 128 * b, w("EB", 4 - b, 516 - b))
 
     def arow():
         cp("v", w("RA", 0, 64), ind(w("ACOL", 0, 2), lst("ac", 4)))
 
-    def base(o):
-        return 0 if o == me else 16 + 8 * pos(me, o)
-
-    own16, c1, sq = w("OWN", 0, 16), w("C1", 0, 16), w("SQ", 0, 4)
-    iota(own16, [[16, 16]])
-    iota(sq, [[16, 4]])
-    iota(fc1, [[4, 8], [0, 2]])
-    iota(fout, [[2, 16]])
-    y0, y1, y2, y3 = ftmp(1), ftmp(1), ftmp(1), ftmp(1)
-    ts(y0, col(B2), 4.0 * ((2 * r) % 8 - r), A.mult, col(M), A.add)
-    ts(y3, col(QQ), float(QB), A.is_equal, -2.0, A.mult)
-    ts(y2, col(K1), float(QB), A.is_equal, -2.0, A.mult)
-    ts(y0, y0, 4.0 * r, A.add)
-    ts(lst("mk", 1), y3, col(ODD), A.add, 2.0, A.add)
-    ts(lst("se", 1), y2, col(B0), A.add, 2.0, A.add)
-    ts(y1, y0, -1.0, A.mult, 32.0, A.add)
-    quant("AO", 0, w("ZB", 0, 512))
-    tt(y1, y1, col(B3), A.mult)
-    quant("DC0", 32, w("ZB", 0, 512))
-    ts(lst("ow", 1), y0, y1, A.add)
-    quant("D0", 256, w("ZB", 0, 512))
     arow()
     quant("NX", 0, w("HT0", 0, 1024))
     for b in range(4):
         mm(4 + b, 256, "E", 128 * b, "NX", 0, False, True)
-    ts(own16, own16, col(P16), A.add)
-    ts(sq, sq, col(P16), A.add, 32.0 * QB, A.add)
-    ts(lst("out", 16), fout, col(COUT), A.add)
-    tt(c1, fc1, own16, A.subtract)
-    if DB < QB:
-        ts(w("SQ", 2, 4), w("SQ", 2, 4), 32.0 * (DB - QB - 1), A.add)
-    for k0, k1, bs in ((0, me, base(0)), (me, me + 1, 0), (me + 1, 8, base(7))):
-        if k1 > k0:
-            v = w("C1", 2 * k0, 2 * k1)
-            ts(v, v, float(256 - bs), A.add)
     for b in range(4):
-        cp("sv"[b % 2], w("DT0", b, 1024, 4), bank(4 + b, 256))
+        cp("s", w("DT0", b, 1024, 4), bank(4 + b, 256))
 
     def differences(name, c, src):
         tt(w(name, c, c + 63), w(src, 0, 63), w(src, 1, 64), A.subtract)
         cp("s", w(name, c + 31, c + 64, 32), w(src, 31, 64, 32))
 
-    x1, x2, x3 = w("TMPI", 16, 80), w("TMPI", 80, 144), w("TMPI", 144, 208)
-    later = [
-        lambda: ts(f2, kt, float(r), A.is_lt, 31.0, A.mult),
+    x1 = w("TMPI", 16, 80)
+    gaps = [
+        lambda: ts(col(SHF), col(K2), float(8 - r), A.is_ge, 31.0, A.mult),
+        lambda: ts(b1, t0, 1, A.arith_shift_right, 1, A.bitwise_and),
+        lambda: ts(col(SHF), col(SHF), col(Q1), A.mult),
+        lambda: ts(fa, b0, col(Q0), A.not_equal, 2.0, A.mult),
+        lambda: ts(kti, w("IOI", 0, 32), col(SHF), A.add),
+        lambda: ts(fb, b1, col(Q1), A.not_equal, 4.0, A.mult),
+        lambda: ts(hh, t0, 2, A.arith_shift_right, 1, A.bitwise_and),
+        lambda: ts(kti, kti, 31, A.bitwise_and),
+        lambda: tt(fa, fa, fb, A.add),
+        lambda: ts(fh, hh, 1.0, A.mult),
+        lambda: ts(ktf, kti, 8.0, A.mult, float(r - MID), A.add),
         lambda: ts(x1, ioi, col(C16), A.add),
-        lambda: tt(x2, f2, ioi, A.add),
-        lambda: ts(x3, kt, float(8 - r), A.add),
+        lambda: tt(fa, fa, fh, A.add),
+        lambda: tt(w("DK", 0, 31), w("TMPF", k0, k0 + 31), w("TMPF", k0 + 1, k0 + 32), A.subtract),
+        lambda: cp("v", w("DK", 31, 32), w("TMPF", k0 + 31, k0 + 32)),
+        lambda: cp("v", lst("r2", 2), fa)]
+    after = [
         lambda: ts(x1, x1, 31, A.bitwise_and),
-        lambda: ts(x2, x2, col(C16), A.add),
-        lambda: quant("DL", 0, w("DT0", 0, 1024)),
-        lambda: ts(x3, x3, 7, A.bitwise_and),
+        lambda: tt(col(CNX), col(B0), col(ODD), A.not_equal),
+        lambda: ts(sq, sq, col(P16), A.add, 32.0 * QB, A.add),
         lambda: tt(w("OFR", 0, 64), f1, x1, A.add),
-        lambda: ts(x2, x2, 31, A.bitwise_and),
-        lambda: ts(f2, x3, 32.0, A.mult, 256.0, A.add),
-        lambda: differences("DF", 0, "OFR"),
-        lambda: tt(w("OFD", 0, 64), f2, x2, A.add),
         lambda: ts(col(CW2), col(CNX), 16.0, A.mult),
-        lambda: differences("DF", 64, "OFD"),
-        lambda: ts(col(CW), col(B1), 256.0, A.mult, col(CW2), A.add),
+        lambda: ts(col(Y0), col(B2), 4.0 * ((2 * r) % 8 - r), A.mult, col(M), A.add),
+        lambda: differences("DF", 0, "OFR"),
         lambda: ts(lst("w2", 1), col(K1), 32.0, A.mult, col(CW2), A.add),
-        lambda: tt(col(CW), col(CW), col(C32K), A.add)]
+        lambda: ts(w("SQ", 2, 4), w("SQ", 2, 4), 32.0 * (DB - QB - 1) if DB < QB else 0.0, A.add),
+        lambda: ts(lst("ow", 1), col(Y0), 4.0 * r, A.add),
+        lambda: ts(own16, own16, col(P16), A.add),
+        lambda: quant("D0", 256, w("ZB", 0, 512)),
+        lambda: cp("v", lst("pp", 4), sq),
+        lambda: tt(c1, fc1, own16, A.subtract)]
+    owner = [
+        lambda: ts(col(VP), col(Q1), 32.0, A.mult, float(LAP), A.add),
+        lambda: ts(col(VD), col(K2), 7.0, A.is_equal, -72.0, A.mult),
+        lambda: ts(c1, c1, 256.0, A.add),
+        lambda: ts(col(SU), col(K2), 8.0, A.mult, 16.0, A.add),
+        lambda: ts(col(OP), col(Q1), 32.0 * (DB - QB), A.mult, OLD + 32.0 * QB, A.add),
+        lambda: tt(w("VPB", 0, 1), col(VP), col(P31), A.add),
+        lambda: tt(col(VD), col(VD), col(M), A.add),
+        lambda: ts(col(C1P), col(Q1), 64.0, A.mult, -1.0, A.add),
+        lambda: tt(col(OP), col(OP), col(P31), A.add),
+        lambda: tt(col(VD), col(VD), col(SU), A.add),
+        lambda: ts(col(SU), col(Q1), 4.0, A.mult),
+        lambda: ts(col(PC), col(P31), 8.0, A.mult, -MID - 0.5, A.add),
+        lambda: tt(col(C1P), col(C1P), col(OP), A.subtract),
+        lambda: tt(w("VDB", 0, 1), col(VD), col(SU), A.add),
+        lambda: ts(col(PC3), col(P31), 8.0, A.mult, 7.5 - MID, A.add),
+        lambda: fill(w("TBL", 0, LAP), 1.0),
+        lambda: fill(w("TBL", LAP, 144), 0.0),
+        lambda: ts(w("MASK", 0, 64), fm, col(P31), A.is_equal),
+        lambda: ts(col(Y2), col(K1), float(QB), A.is_equal, -2.0, A.mult),
+        lambda: cp("v", lst("sl", 1), col(M)),
+        lambda: pick("LA0", LAP, 64, "PB0", 128, ("LST", LISTS["pp"]), OLD),
+        lambda: ts(lst("se", 1), col(Y2), col(B0), A.add, 2.0, A.add)]
 
-    def gap():
-        if later:
-            later.pop(0)()
-
-    def unpack_parities(t):
-        for b in range(4):
-            mm(4 + b, 128, "E", 128 * b, "PB%d" % t, V0)
-        for b in range(4):
-            cp("s", w("ACC", 64 * b, 64 * b + 64), bank(4 + b, 64, RO))
-
-    def entries():
-        for kind in range(2):
-            k = 0
-            while k < 8:
-                bs = base((k - r * kind) % 8)
-                e = k
-                while e < 8 and base((e - r * kind) % 8) == bs:
-                    e += 1
-                v = w("VALS", 32 * kind + 4 * k, 32 * kind + 4 * e)
-                if bs:
-                    sa(v, v, 1.0, float(bs))
-                k = e
+    def gap(n=1):
+        for i in range(n):
+            if gaps:
+                gaps.pop(0)()
 
     def choose(t):
         n = "N%d" % t
@@ -552,97 +547,82 @@ def rank_program(g, core, T, topo):
         rb, tb = w("RB", 0, 128), w("TB", 0, 128)
         tt(w("RB", 0, 64), ind(w(n, 0, 8), lst("bl", 4)), w("RA", 0, 64), A.subtract)
         cp("s" if t else "v", w("RB", 64, 128), ind(w(n, 0, 16 if CLASH else 8), lst("bl", 4, 4)))
-        sa(w("INV%d" % t, 0, 512), w("EB", 0, 512), 0.0, 8.0)
-        if t == 0:
-            entries()
-        gap()
+        gap(2)
         tr(tb, rb)
-        gap()
+        gap(2)
         st, rr, g1, g2, cc = [w(x, 0, 64) for x in ("ST", "RR", "G1", "G2", "CC")]
         tt(st, ind(w("TB", 64, 128), lst("sh", 4)), w("TB", 0, 64), A.add)
-        gap()
+        gap(2)
         tr(rr, st)
-        gap()
+        gap(2)
         tt(g1, st, rr, A.subtract)
-        gap()
+        gap(2)
         tt(g2, g1, w("LM", 0, 64), A.is_lt)
-        gap()
+        gap(2)
         scan(cc, w("SEG", 0, 64), g2)
-        gap()
+        gap(2)
         for q in range(4):
             cp("vs"[q % 2], w("XR", 2, 4, 1, 32 * q, 32 * q + 32), w("CC", 31, 64, 32, 32 * (q ^ 1), 32 * (q ^ 1) + 32))
         cp("v", w("XR", 0, 2), w("CC", 31, 64, 32))
         cp("v", w("XR", 4, 8, 1, 0, 64), w("XR", 0, 4, 1, 64, 128))
         cp("s", w("XR", 4, 8, 1, 64, 128), w("XR", 0, 4, 1, 0, 64))
-        gap()
+        gap(len(gaps))
         rg, m, xr = w("RG", 0, 64), w("MM", 0, 64), w("XR", 0, 8)
+        wk = "WK%d" % t
         tt(rg, ind(xr, lst("rg", 4)), w("MT", 0, 64), A.not_equal)
-        gap()
+        tt(w("RGK", 0, 32), ind(xr, lst("r2", 2)), w("MT", 0, 32), A.not_equal)
         tr(m, rg)
-        gap()
+        tr(w("MK", 0, 32), w("RGK", 0, 32))
         scan(w("SCN", 0, 64), m, w("DMP", 0, 64))
+        scan(w("SK", 0, 32), w("MK", 0, 32), w("DK", 0, 32))
+        cp("v", w("L1U", 0, 2), w("SCN", 31, 64, 32))
+        ts(w("KB", 0, 32), w("ONE", 0, 32), w("SK", 31, 32), A.mult)
+        if t == 0:
+            quant("DL", 0, w("DT0", 0, 1024))
+        dc, sn, la, kx = "DC%d" % t, "SN%d" % t, "LA%d" % t, "KX%d" % t
+        pick(dc, 0, 32, "DL", 256 + 32 * t, ("L1U", 0))
+        tr(w(wk, 0, 32), w("KB", 0, 32))
         if t:
             scan(w("SCN", 64, 128), m, w("DF", 0, 64))
-        gap()
-        cp("v", w("L1U", 0, 2), w("SCN", 31, 64, 32))
-        if t:
-            scan(w("SCN", 128, 192), m, w("DF", 64, 128))
-        gap()
-        dc, sn, la, ll, wl = "DC%d" % t, "SN%d" % t, "LA%d" % t, "LL%d" % t, "WL%d" % t
-        pick(dc, 0, 32, "DL", 256 + 32 * t, ("L1U", 0))
-        gap()
-        gap()
         pick(sn, 0, 64, dc, 32, ("LST", LISTS["sn"]))
         hs, close = T.sem["hs%d" % t], _near(core, helpers[0], away, topo)
         fused([w("c_" + sn, 0, 64)], [([helpers[h]], close[NHAND * h:NHAND * h + NHAND], hs, T["c_" + sn][:, 32 * h:32 * h + 32].bitcast(dt.uint8),
                                        T["c_HC%d" % t][:, 0:32].bitcast(dt.uint8)) for h in range(2)])
         a = 32 * (1 - me // HALF)
-        fused([w("z_" + sn, 0, 64)], [([helpers[2]], away, hs, T["z_" + sn][:, a:a + 32], T["z_HZ%d" % t][:, 0:32])])
-        fused([w("z_" + sn, 0, 64)], [([cores[o]], _mask(me, o, mine, core, cores, topo), _delta_sem(T, me, o, t), T["z_" + sn][:, 8 * o:8 * o + 8],
-                                       T["z_" + la][:, 16 + 8 * pos(me, o):24 + 8 * pos(me, o)]) for o in mine])
-        while later:
-            gap()
-        if t == 0:
-            scan(w("SCN", 64, 128), m, w("DF", 0, 64))
-            ts(lst("w", 2), fw, col(CW), A.add)
-            scan(w("SCN", 128, 192), m, w("DF", 64, 128))
-        l2 = w("L2U", 0, 4)
-        cp("v", l2, w("SCN", 95, 192, 32))
-        inv, vals = w("INV%d" % t, 0, 512), w("VALS", 0, 64)
-        run("v", lambda: g.vector.tensor_copy(inv[0].indirect(l2[0]), vals[0]), [vals, l2], [inv])
-        it = w("INVT", 0, 512)
-        tr(it, inv)
-        cp("v", w(wl, 0, 32), ind(it, lst("w", 2)))
+        fused([w("z_" + sn, 0, 64)], [([helpers[2]], close[:2 * NHAND], hs, T["z_" + sn][:, a:a + 32], T["z_HZ%d" % t][:, 0:32])])
         for part in _calls(me, cores, topo):
-            fused([w(wl, 0, 32)], [([cores[o]], _list_mask(me, o, cores, topo), _delta_sem(T, me, o, t), T[wl][:, 4 * o:4 * o + 4],
-                                    T[ll][:, 4 * pos(me, o):4 * pos(me, o) + 4]) for o in part])
-        for name, lo, hi in (("dA%d", 0, 3), ("dB%d", 3, 7)):
-            cnt = sum(delta_count(s) for s in others if lo <= pos(s, me) < hi)
-            arrive([w("c_" + la, 16 + 8 * lo, 16 + 8 * hi), w("z_" + la, 16 + 8 * lo, 16 + 8 * hi), w(ll, 4 * lo, 4 * hi)], name % t, cnt)
-
-    def own_columns(t):
-        dc, la, wl = "DC%d" % t, "LA%d" % t, "WL%d" % t
-        pick(la, 0, 16, dc, 34, ("LST", LISTS["ow"]))
-        pick("AO", 0, 64, la, 16, (wl, 4 * me))
-        ts(w("NEQ", 28, 32), w(wl, 4 * me, 4 * me + 4), 8.0, A.not_equal)
-
-    def own_deltas():
-        for b in range(4):
-            mm(4 + b, 128, "E", 128 * b, "AO", 0)
-        for b in range(4):
-            acc = w("ACC", 64 * b, 64 * b + 64)
-            if me == 0:
-                tt(acc, acc, bank(4 + b, 64), A.add)
-            else:
-                cp("s", w("OD", 64 * b, 64 * b + 64), bank(4 + b, 64))
+            fused([w(wk, 0, 32)], [([cores[o]], _list_mask(me, o, cores, topo), T.sem["ls%d" % t], T[wk][:, 4 * o:4 * o + 4],
+                                    T[kx][:, 32 + 4 * pos(me, o):36 + 4 * pos(me, o)]) for o in part])
+        fused([w("z_" + sn, 0, 64)], [([cores[o]], _mask(me, o, mine, core, cores, topo), T.sem["dl%d" % t], T["z_" + sn][:, 8 * o:8 * o + 8],
+                                       T["z_" + la][:, 16 + 8 * pos(me, o):24 + 8 * pos(me, o)]) for o in mine])
+        run("y", lambda: g.sync.dma_start(T[kx][:, 60:64], T[wk][:, 4 * me:4 * me + 4]), [w(wk, 4 * me, 4 * me + 4)], [w(kx, 60, 64)], dma=True)
+        arrive([w(kx, 32, 60)], "ls%d" % t, sum(len(_list_mask(s, me, cores, topo)) for s in others))
+        arrive([w("c_" + la, 16, 72), w("z_" + la, 16, 72)], "dl%d" % t, sum(delta_count(s) for s in others))
+        inv, vals, l2 = w("INV%d" % t, 0, 256), w("VALS", 0, 32), w("L2U", 0, 2)
+        sa(inv, w("EB", 0, 256), 0.0, 8.0)
+        if t == 0:
+            for k in range(R):
+                sa(w("KX%d" % k, 0, 32), fkp, 1.0, -0.5)
+            sa(w("SEGG", 0, 192), w("ONE", 0, 192), 0.0, 1.0)
+            sa(w("SEGH", 0, 320), w("ONE", 0, 320), 0.0, 1.0)
+            sa(col(COUT), col(P8), 32.0, col(B3))
+            sa(w("K4", 0, 64), kt, 4.0, 256.0)
+            sa(w("SEGG", 0, 192, 64), w("ONE", 0, 3), 0.0)
+            sa(w("SEGH", 0, 320, 32), w("ONE", 0, 10), 0.0)
+            for f in after:
+                f()
+            scan(w("SCN", 64, 128), m, w("DF", 0, 64))
+        cp("v", l2, w("SCN", 95, 128, 32))
+        run("v", lambda: g.vector.tensor_copy(inv[0].indirect(l2[0]), vals[0]), [vals, l2], [inv])
+        pick(la, 0, 16, dc, 32, ("LST", LISTS["ow"]))
+        tr(w("INVT", 0, 256), inv)
 
     def advance(t):
-        d, dn, it = "D%d" % t, "D%d" % (t + 1), w("INVT", 0, 512)
+        d, dn, it = "D%d" % t, "D%d" % (t + 1), w("INVT", 0, 256)
         pick(d, 256, 32, "NX", 256 + 32 * t, ("L1U", 0))
         if t < R - 1:
             for b in range(4):
                 mm(b, 128, "W", 128 * b, d, 256)
-        own_columns(t)
         wd, we, dls = w("WD", 0, 16), w("WE", 0, 16), w("DLS", 0, 16)
         rg, rt, mask, u = w("RG", 0, 64), w("RT", 0, 64), w("UP", 0, 64), w("UP", 64, 128)
         row = [lambda: cp("v", wd, ind(it, lst("w2", 1))), lambda: ts(we, wd, 8.0, A.not_equal), lambda: tt(wd, wd, c1, A.add),
@@ -653,14 +633,14 @@ def rank_program(g, core, T, topo):
             row[i]()
             if t < R - 1:
                 moved[i]()
+            if t == 0:
+                for f in owner[4 * i:4 * i + 4]:
+                    f()
         if t < R - 1:
             for b in range(4):
                 relu("HT1", b, 32, b)
             tt(mp, mp, u, A.add)
             quant("NX", 256 + 32 * t, w("HT1", 0, 512))
-        if t == 0:
-            unpack_parities(0)
-        own_deltas()
         pick(dn, 0, 256, d, 288, ("DLS", 0))
         if t < R - 1:
             differences("DMP", 0, "MAP")
@@ -670,6 +650,7 @@ def rank_program(g, core, T, topo):
             if t == 0:
                 sa(w("K4", 0, 64), w("K4", 0, 64), 1.0, 32.0)
         else:
+            ts(lst("out", 16), fout, col(COUT), A.add)
             pick("FD", 0, 256, dn, 256, ("LST", LISTS["out"]))
             mm(4, 256, "U", 0, "FD", 0)
             cp("s", w("YB", 0, 256), w("ps", 2048, 2304))
@@ -680,73 +661,44 @@ def rank_program(g, core, T, topo):
                 store("y", T.osc[4 * k:4 * k + 4, 0:256], w("z_FD", 0, 256, 1, 32 * k, 32 * k + 4))
 
     def patch(t):
-        la, ll, pb, last = "LA%d" % t, "LL%d" % t, "PB%d" % t, t == R - 1
-        pick("AR", 0, 192, la, 40, (ll, 0))
+        la, kx, pb, pn, last = "LA%d" % t, "KX%d" % t, "PB%d" % t, "PB%d" % (t + 1), t == R - 1
+        tr(w("KT", 0, 32), w(kx, 32, 64))
+        ts(w("GG", 0, 64), w(kx, 0, 64), col(PC), A.is_lt)
+        ts(w("GG", 128, 192), w(kx, 0, 64), col(PC3), A.is_lt)
+        ts(w("GG", 64, 128), w(kx, 0, 64), w("KT", 0, 1), A.is_lt)
+        scan(w("CN", 0, 192), w("SEGG", 0, 192), w("GG", 0, 192))
+        pp, pd, p3 = w("CN", 63, 64), w("CN", 127, 128), w("CN", 191, 192)
+        ts(w("HH", 0, 128), w("WT", 0, 128), pp, A.is_equal, w("VPB", 0, 1), A.mult)
+        ts(w("HH", 128, 256), w("WT", 0, 128), pd, A.is_equal, w("VDB", 0, 1), A.mult)
+        ts(col(MK1), p3, pp, A.subtract, 1.0, A.is_gt)
+        tr(w("HHT", 0, 256), w("HH", 0, 256))
+        ts(col(SU), p3, col(C1P), A.add, col(MK1), A.mult)
+        scan(w("SH", 0, 256), w("SEGH", 0, 256), w("HHT", 0, 256))
+        ts(col(SU), col(SU), col(OP), A.add)
+        tt(w("ALF", 0, 4), w("SH", 31, 128, 32), w("SH", 159, 256, 32), A.add)
+        ts(w("HH", 256, 320), w("MASK", 0, 64), col(SU), A.mult)
+        for k in range(2):
+            for h in range(2):
+                cp("v", w("AL", 4 * k, 4 * k + 4, 1, 64 * h, 64 * h + 64), w("ALF", 0, 4, 1, 64 * k, 64 * k + 64))
+        ms, tb, al = w("MS", 0, 128), w("TBL", 0, 144), w("AL", 0, 8)
+        pick("AR", 0, 128, la, 144, ("AL", 0))
+        run("s", lambda: g.scalar.activation(ms[0], tb[0].indirect(al[0]), F.Copy), [tb, al], [ms])
         for b in range(4):
-            mm(b, 192, "E", 128 * b, "AR", 0)
-        pick("AR", 192, 256, la, 72, (ll, 12))
+            mm(b, 128, "E", 128 * b, "AR", 0)
+        tr(w("HHT", 256, 320), w("HH", 256, 320))
+        scan(w("SH", 256, 320), w("SEGH", 256, 320), w("HHT", 256, 320))
+        for k in range(2):
+            for h in range(2):
+                cp("s", w("SX", 2 * k, 2 * k + 2, 1, 64 * h, 64 * h + 64), w("SH", 287, 320, 32, 64 * k, 64 * k + 64))
         for b in range(4):
-            mm(4 + b, 256, "E", 128 * b, "AR", 192)
-        ts(w("NEQ", 0, 28), w(ll, 0, 28), 8.0, A.not_equal)
-        for c in range(4):
-            v, o, z = w("NEQ", c, 32, 4), w("JUNK", 0, 8), w("AN", c, c + 1)
-            run("s", lambda: g.scalar.activation(o[0], v[0], F.Copy, accum_out=z[0]), [v], [o, z])
-        finals = [(0, 64, QB)] if QB < 3 else [(0, 32, QB), (32, 64, DB)]
+            scan(w("NT", b, 512, 4), ms, bank(b, 128))
+            if b == 2:
+                cp("v", w("SEL", 0, 16), ind(w("SX", 0, 4), lst("sl" if last else "se", 1)))
+        quant(pb, 0, w("NT", 0, 512))
+        pick(pn, OLD, 128, pb, 256, ("SEL", 0))
         if not last:
-            finals += [(32, 64, k) for k in range(4) if k not in (QB, DB)]
-        elif QB == 3:
-            pass
-        def source(s, b, c0, c1):
-            if s == me:
-                return w("OD", 64 * b + c0, 64 * b + c1)
-            p = pos(s, me)
-            k, c = (b, 64 * p) if p < 3 else (4 + b, 64 * (p - 3))
-            return bank(k, c1 - c0, c + c0)
-        def add(i, b):
-            if i < n_ranks - 1:
-                acc = w("ACC", 64 * b, 64 * b + 64)
-                tt(acc, acc, source(i, b, 0, 64), A.add)
-            else:
-                c0, c1, k = finals[i - n_ranks + 1]
-                tt(w("NT", 128 * k + b, 128 * k + 4 * (c1 - c0), 4), w("ACC", 64 * b + c0, 64 * b + c1), source(n_ranks - 1, b, c0, c1), A.add)
-        def there(s, b):
-            return 0.0 if s == me else 3.5 * (b + 1) if pos(s, me) < 3 else 14.0 + 4.5 * (b + 1)
-        end = n_ranks - 1 + len(finals)
-        free, seq, ready, step = 0.0, [], [0.0] * 4, [1 if me == 0 else 0] * 4
-        while min(step) < end:
-            can = [(max(free, ready[b], there(min(step[b], n_ranks - 1), b)), step[b], b) for b in range(4) if step[b] < end]
-            start, s, b = min(can)
-            seq.append((s, b))
-            free, step[b] = start + (2 if s == me else 1), s + 1
-            if s < n_ranks - 1:
-                ready[b] = free + 2
-        ms, se, mk, ob = w("MS", 0, 4), w("SE", 0, 4), w("MK", 0, 16), w("OB", 0, 2)
-        aside = [lambda: ts(ms, w("AN", 0, 4), 0.0, A.is_gt)]
-        table = [lambda: ts(se, ms, float(NEW), A.mult),
-                 lambda: tt(se, se, sq, A.add),
-                 lambda: cp("v", w("SEL", 0, 16), ind(se, lst("se", 1)))]
-        if last:
-            aside += table
-        else:
-            aside += [lambda: cp("v", mk, ind(ms, lst("mk", 1))),
-                      lambda: ts(w("NM", 0, 1), w("MK", 0, 1), 0.0, A.is_equal),
-                      lambda: ts(ob, w("OS", 0, 2), w("NM", 0, 1), A.mult)]
-        for i, (s, b) in enumerate(seq):
-            add(s, b)
-            if aside and i >= 2 * n_ranks + 1 and i % 3 == 1:
-                aside.pop(0)()
-        while aside:
-            aside.pop(0)()
-        quant(pb, NEW, w("NT", 0, 512))
-        if not last:
-            mm(0, 128, pb, NEW, "V", 0)
-            scores(t + 1, lambda out: sa(out, w("ps", t + 1, t + 2), w("MK", 0, 1), w("OB", t, t + 1)))
-            if t == 0:
-                sa(w("OS", 1, 2), w("ps", 2, 3), w("MK", 0, 1), w("OB", 1, 2))
-            for f in table:
-                f()
-        pick("PB%d" % (t + 1), 0, 32 * NB, pb, 288, ("SEL", 0))
-        if not last:
+            scores(t + 1)
+            pick("LA%d" % (t + 1), LAP, 64, pn, 128, ("LST", LISTS["pp"]), OLD)
             for b in range(4):
                 mm(4 + b, 128, "E", 512 + 128 * b, "D%d" % t, 256, True, False)
                 mm(4 + b, 128, "E", 128 * b, "NX", 256 + 32 * t, False, True)
@@ -754,18 +706,15 @@ def rank_program(g, core, T, topo):
                 cp("vs"[b % 2], w("DT1", b, 128, 4), bank(4 + b, 32))
             quant("DL", 256 + 32 * t, w("DT1", 0, 512))
             arow()
-            unpack_parities(t + 1)
-            quant("DC%d" % (t + 1), 32, w("ZB", 0, 512))
             if t == 0:
                 quant("D1", 256, w("ZB", 0, 512))
         else:
-            out, c = "PB%d" % R, 32 * QB
-            mm(0, 128, "V", 0, out, V0)
-            cc = w("c_" + out, c, c + 64)
+            mm(0, 128, "V", 0, pn, OLD)
+            cc = w("c_" + pn, OLD, OLD + 64)
             store("y", T.oc[:, 1024:1280], (cc[0].bitcast(dt.uint8), cc[1]))
             for k in range(4):
-                store("ys"[k % 2], T.osc[4 * k:4 * k + 4, 256:320], w("z_" + out, c, c + 64, 1, 32 * k, 32 * k + 4))
-            cp("v", w("YB", 256, 320), bank(0, 64, RO))
+                store("ys"[k % 2], T.osc[4 * k:4 * k + 4, 256:320], w("z_" + pn, OLD, OLD + 64, 1, 32 * k, 32 * k + 4))
+            cp("v", w("YB", 256, 320), bank(0, 64))
             store("s", T.y[:, 256:320], w("YB", 256, 320))
 
     for t in range(R):

from concourse.bass import DstId, RemoteDMATransfer
from concourse.mybir import dt, AluOpType as A, ActivationFunctionType as F

R = 3
HALF = 4
NHAND = 4
TINY = 2.0 ** -110
MID = 124
OLD = 128
LAP = 80
FP8, U8, BF, F32, I32, U16 = "float8_e4m3fn_x4", "uint8", "bfloat16", "float32", "int32", "uint16"
SCRATCH = {"ps": ("psum", [128, 4096], F32)}


def _add(d, text, mx=False):
    for item in text.split():
        name, n = item.split(":")
        if mx:
            SCRATCH["c_" + name] = ("sbuf", [128, int(n)], FP8)
            SCRATCH["z_" + name] = ("sbuf", [128, int(n)], U8)
        else:
            SCRATCH[name] = ("sbuf", [128, int(n)], d)


_add(BF, "XB:1024 PT:512 UB:512 VB:512 ONE:520 EB:520 NB:520 ZB:512 HT0:1024 DT0:1024 HT1:512 DT1:512 NT:512 "
         "INV0:256 INV1:256 INV2:256 INVT:256 VALS:32 KX0:64 KX1:64 KX2:64 WK0:32 WK1:32 WK2:32 KW:354 CT:848 "
         "GG:192 HH:320 HHT:320 SH:320 MS:128")
_add(FP8, "X:256 U:128 V:128 W:512 E:1024 D0:384 D1:384 D2:384 D3:256 FD:256 NX:416 DL:416 PB0:256 PB1:256 PB2:256 "
          "PB3:256 DC0:32 DC1:32 DC2:32 SN0:64 SN1:64 SN2:64 LA0:144 LA1:144 LA2:144 AR:128", mx=True)
_add(FP8, "c_HC0:32 c_HC1:32 c_HC2:32")
_add(U8, "z_HZ0:32 z_HZ1:32 z_HZ2:32")
_add(F32, "N0:16 N1:16 N2:16 SC0:1 SC1:1 SC2:1 FC:64 MAP:64 LM:64 SM:512 TMPF:320 "
          "ACOL:8 RA:64 RB:128 TB:128 ST:64 RR:64 G1:64 G2:64 CC:64 XR:8 RG:64 RT:64 MM:64 SCN:128 DMP:64 DF:64 "
          "DK:32 YB:320 UP:128")
_add(I32, "PI:1 INTC:16 TMPI:256")
ALIAS = {}
for _buf, _text in (("SM", "OWN:0 C1:16 WD:32 WE:48 SQ:64 ALF:68 SX:72 SEG:96 MT:160 IOI:248 KTB:312 K4:376 OFR:440"),
                    ("CT", "TBL:0 WT:144 MASK:272 SEGG:336 SEGH:528"),
                    ("KW", "RGK:0 MK:32 SK:64 KB:96 KT:128 CN:160 VPB:352 VDB:353"),
                    ("LW", "DLS:0 SEL:16 AL:32 L1U:40 L2U:42")):
    for _item in _text.split(" "):
        ALIAS[_item.split(":")[0]] = (_buf, int(_item.split(":")[1]))
LISTS = {"nat": 0, "out": 16, "bl": 32, "sh": 40, "rg": 44, "ac": 48, "w2": 52, "r2": 54, "sn": 56, "ow": 60, "se": 62, "sl": 64, "pp": 66}
_add(U16, "LST:70 LW:44")
TILES = ("NT", "HT0", "HT1", "DT0", "DT1")
SEMAPHORES = (["qg", "qv", "qs", "qt", "snt"] + [s + str(t) for s in ("sc", "dl", "ls", "hs") for t in range(R)]
              + ["m%d" % i for i in range(48)])


def pos(s, d):
    return s if s < d else s - 1


def bits(e):
    return sum(1 << x for x in e)


def _far(s, cores, topo):
    return [o for o in range(len(cores)) if o != s and topo.chip(cores[s]) != topo.chip(cores[o])]


def _near(src, dst, away, topo):
    return [x for x in topo.engines(src, dst) if x not in away]


def _helpers(s, cores, topo):
    return [c for c in topo.cores_of(cores[s]) if topo.die(c) == topo.die(cores[s]) and c not in cores][:3]


def _half(h, s):
    return [o for o in range(HALF * h, HALF * h + HALF) if o != s]


def _calls(s, cores, topo):
    fs = _far(s, cores, topo)
    n = len(topo.engines(cores[s], cores[fs[0]])) // 2
    return [[o for o in range(len(cores)) if o != s and o not in fs[n:]], fs[n:]]


def _mask(s, d, dests, src, cores, topo):
    fs = _far(s, cores, topo)
    away = topo.engines(src, cores[fs[0]])
    if d not in fs:
        return _near(src, cores[d], away, topo)[:2]
    fs = [o for o in dests if o in fs]
    n = 2 if len(fs) > 2 else 4
    i = n * fs.index(d)
    return away[i:i + n]


def _list_mask(s, d, cores, topo):
    dests = [c for c in _calls(s, cores, topo) if d in c][0]
    return _mask(s, d, dests, cores[s], cores, topo)


def _hand_mask(s, d, src, cores, topo):
    return _mask(s, d, _half(d // HALF, s), src, cores, topo)[:2]


def _to(core, topo):
    rid, pid = topo.addr(core)[:2]
    return DstId(rid=rid, pnc=pid)


def hand_on(g, core, s, cores, T, topo):
    k = _helpers(s, cores, topo).index(core)
    h = k if k < 2 else 1 - s // HALF
    dests = _half(h, s)
    for t in range(R):
        g.wait_ge(T.sem["hs%d" % t], NHAND if k < 2 else 2 * NHAND)
        tf = []
        for o in dests:
            p, i = pos(s, o), o - HALF * h
            if k < 2:
                src = T["c_HC%d" % t][:, 8 * i:8 * i + 8].bitcast(dt.uint8)
                land = T["c_LA%d" % t][:, 16 + 8 * p:24 + 8 * p].bitcast(dt.uint8)
            else:
                src, land = T["z_HZ%d" % t][:, 8 * i:8 * i + 8], T["z_LA%d" % t][:, 16 + 8 * p:24 + 8 * p]
            tf.append(RemoteDMATransfer(dst_ids=[_to(cores[o], topo)], dma_engine_mask=bits(_hand_mask(s, o, core, cores, topo)),
                                        remote_sem=T.sem["dl%d" % t], srcs=[src], dsts=[land]))
        g.remote_dma_fused(tf, local_sem=T.sem.snt)
    g.wait_ge(T.sem.snt, 2 * len(dests) * R)


def rank_program(g, core, T, topo):
    cores = [int(c) for c in T.cores]
    n_ranks = len(cores)
    me = T.rank_of(core)
    if me is None:
        for s in range(n_ranks):
            if core in _helpers(s, cores, topo):
                hand_on(g, core, s, cores, T, topo)
        return
    r = me
    Q = {"g": g, "v": g.vector, "s": g.scalar, "t": g.tensor, "y": g.sync}
    csem = {"g": "qg", "v": "qv", "s": "qs", "t": "qt"}
    total, known, hist = {}, {q: {} for q in Q}, {}
    ndma = [0]

    def w(name, c0, c1, step=1, p0=0, p1=128):
        if name in ALIAS:
            name, c0, c1 = ALIAS[name][0], c0 + ALIAS[name][1], c1 + ALIAS[name][1]
        t = T[name]
        if p0 == 0 and p1 == 128:
            a = t[:, c0:c1] if step == 1 else t[:, c0:c1:step]
        else:
            a = t[p0:p1, c0:c1] if step == 1 else t[p0:p1, c0:c1:step]
        if step == 4 and name in TILES:
            b = c0 % 4
            return (a, [(name, c0 - b, c1, 32 * b, 32 * b + 32)])
        return (a, [(name, c0, c1, p0, p1)])

    def ind(v, o):
        return (v[0].indirect(o[0]), v[1] + o[1])

    def lst(name, n, off=0):
        a = LISTS[name] + off
        return w("LST", a, a + n)

    def norm(reg):
        name, c0, c1, p0, p1 = reg
        if name == "ps":
            return (name, c0 // 512 * 512, (c1 + 511) // 512 * 512, 0, 128)
        return reg

    def waits(q, reads, writes):
        need = {}
        def want(h):
            sem, n, clock = h[7], h[8], h[9]
            if known[q].get(sem, 0) >= n:
                return
            if sem not in need or need[sem][0] < n:
                need[sem] = (n, clock)
        for reg in reads:
            name, c0, c1, p0, p1 = norm(reg)
            for h in hist.get(name, ()):
                if h[0] < c1 and c0 < h[1] and h[2] < p1 and p0 < h[3] and (h[4] or (name == "ps" and h[5] != q)):
                    want(h)
        for reg in writes:
            name, c0, c1, p0, p1 = norm(reg)
            for h in hist.get(name, ()):
                if h[0] < c1 and c0 < h[1] and h[2] < p1 and p0 < h[3]:
                    if name == "ps" and h[5] == q:
                        continue
                    want(h)
        for sem in sorted(need):
            n, clock = need[sem]
            if any(s2 != sem and c2.get(sem, 0) >= n for s2, (n2, c2) in need.items()):
                continue
            Q[q].wait_ge(T.sem[sem], n)
        for sem in need:
            n, clock = need[sem]
            for k, v in clock.items():
                if known[q].get(k, 0) < v:
                    known[q][k] = v
            known[q][sem] = max(known[q].get(sem, 0), n)

    def record(q, reads, writes, sem, n, clock, dma):
        for reg in writes:
            reg = norm(reg)
            name, c0, c1, p0, p1 = reg
            hs = [h for h in hist.get(name, ()) if not (c0 <= h[0] and h[1] <= c1 and p0 <= h[2] and h[3] <= p1)]
            hs.append((c0, c1, p0, p1, True, q, dma, sem, n, clock))
            hist[name] = hs
        for reg in reads:
            reg = norm(reg)
            name, c0, c1, p0, p1 = reg
            hs = [h for h in hist.get(name, ()) if not (not h[4] and not dma and not h[6] and h[5] == q and (c0, c1, p0, p1) == tuple(h[:4]))]
            hs.append((c0, c1, p0, p1, False, q, dma, sem, n, clock))
            hist[name] = hs

    def run(q, call, reads, writes, dma=False):
        rr = [x for v in reads for x in v[1]]
        ww = [x for v in writes for x in v[1]]
        waits(q, rr, ww)
        if dma:
            sem, inc = "m%d" % ndma[0], 16
            ndma[0] += 1
        else:
            sem, inc = csem[q], 1
        total[sem] = total.get(sem, 0) + inc
        call().then_inc(T.sem[sem], inc)
        clock = dict(known[q])
        clock[sem] = total[sem]
        record(q, rr, ww, sem, total[sem], clock, dma)

    def arrive(views, sem, n):
        total[sem] = n
        record("x", [], [x for v in views for x in v[1]], sem, n, {sem: n}, True)

    def S(x):
        return x[0] if isinstance(x, tuple) else x

    def deps(*xs):
        return [x for x in xs if isinstance(x, tuple)]

    def cp(q, out, a):
        if q == "v":
            run("v", lambda: g.vector.tensor_copy(out[0], a[0]), [a], [out])
        else:
            run("s", lambda: g.scalar.activation(out[0], a[0], F.Copy), [a], [out])

    def sa(out, a, scale=1.0, bias=0.0):
        run("s", lambda: g.scalar.activation(out[0], a[0], F.Identity, bias=S(bias), scale=S(scale)), [a] + deps(scale, bias), [out])

    def tt(out, a, b, op):
        run("v", lambda: g.vector.tensor_tensor(out[0], a[0], b[0], op), [a, b], [out])

    def ts(out, a, s1, op0, s2=None, op1=None):
        if op1 is None:
            run("v", lambda: g.vector.tensor_scalar(out[0], a[0], S(s1), None, op0), [a] + deps(s1), [out])
        else:
            run("v", lambda: g.vector.tensor_scalar(out[0], a[0], S(s1), S(s2), op0, op1), [a] + deps(s1, s2), [out])

    def tr(out, a):
        run("v", lambda: g.vector.transpose(out[0], a[0]), [a], [out])

    def scan(out, a, b):
        run("v", lambda: g.vector.tensor_tensor_scan(out[0], a[0], b[0], 0.0, A.mult, A.add), [a, b], [out])

    def fill(out, c):
        run("v", lambda: g.vector.memset(out[0], c), [], [out])

    def iota(out, pattern, base=0, ch=0, small=True):
        if small:
            run("g", lambda: g.iota(out[0], pattern, base, ch, allow_small_or_imprecise_dtypes=True), [], [out])
        else:
            run("g", lambda: g.iota(out[0], pattern, base, ch), [], [out])

    def quant(name, c0, src):
        n = (src[1][0][2] - src[1][0][1]) // 4
        c, z = w("c_" + name, c0, c0 + n), w("z_" + name, c0, c0 + n)
        run("v", lambda: g.vector.quantize_mx(c[0], z[0], src[0]), [src], [c, z])

    def pick(dst, d0, n, src, width, off, a0=0):
        b, k = off
        o = w(b, k, k + n // 16)
        co, ci = w("c_" + dst, d0, d0 + n), w("c_" + src, a0, a0 + width)
        run("v", lambda: g.vector.tensor_copy(co[0].bitcast(dt.uint32), ci[0].bitcast(dt.uint32).indirect(o[0])), [ci, o], [co])
        zo, zi = w("z_" + dst, d0, d0 + n), w("z_" + src, a0, a0 + width)
        run("s", lambda: g.scalar.activation(zo[0], zi[0].indirect(o[0]), F.Copy), [zi, o], [zo])

    def mm(bank, n, lhs, l0, rhs, r0, start=True, stop=True):
        out = w("ps", 512 * bank, 512 * bank + n)
        a, az = w("c_" + lhs, l0, l0 + 128), w("z_" + lhs, l0, l0 + 128)
        b, bz = w("c_" + rhs, r0, r0 + n), w("z_" + rhs, r0, r0 + n)
        run("t", lambda: g.tensor.matmul_mx(out[0], a[0], az[0], b[0], bz[0], start, stop), [a, az, b, bz], [out])

    def bank(b, n, c0=0):
        return w("ps", 512 * b + c0, 512 * b + c0 + n)

    def load(q, out, a):
        run(q, lambda: Q[q].dma_start(out[0], a), [], [out], dma=True)

    def store(q, a, src):
        run(q, lambda: Q[q].dma_start(a, src[0]), [src], [], dma=True)

    others = [o for o in range(n_ranks) if o != me]
    afar = _far(me, cores, topo)
    away = topo.engines(core, cores[afar[0]])
    helpers = _helpers(me, cores, topo)
    mine = _half(me // HALF, me)

    def fused(reads, transfers):
        waits("g", [x for v in reads for x in v[1]], [])
        g.remote_dma_fused([RemoteDMATransfer(dst_ids=[_to(c, topo) for c in ds], dma_engine_mask=bits(e), remote_sem=sem, srcs=[src], dsts=[land] * len(ds))
                            for ds, e, sem, src, land in transfers], local_sem=T.sem.snt)
        total["snt"] = total.get("snt", 0) + sum(len(x[1]) for x in transfers)

    def send_scores(t):
        src, land, sem = w("SC%d" % t, 0, 1), T["N%d" % t][:, me:me + 1], T.sem["sc%d" % t]
        fused([src], [([cores[o] for o in afar], away, sem, src[0], land)]
              + [([cores[o]], _near(core, cores[o], away, topo)[:2], sem, src[0], land) for o in others if o not in afar])

    def score_count():
        return sum(len(away) if s in afar else 2 for s in others)

    def delta_count(s):
        direct = s // HALF == me // HALF
        scales = _mask(s, me, _half(s // HALF, s), cores[s], cores, topo) if direct else _hand_mask(s, me, _helpers(s, cores, topo)[2], cores, topo)
        codes = _hand_mask(s, me, _helpers(s, cores, topo)[me // HALF], cores, topo)
        return len(codes) + len(scales)

    QB = me % 4
    DB = QB + 1 if QB < 3 else 2
    CLASH = r % 4 == 0

    load("s", w("VB", 0, 512), T.v[:, :])
    for b in range(4):
        load("ys"[b % 2], w("PT", 128 * b, 128 * b + 128), (T.pr if b == QB else T.pd)[:, :])
    load("y", w("XB", 0, 1024), T.x[:, :])
    load("s", w("UB", 0, 512), T.u[:, :])
    cw = w("c_W", 0, 512)
    load("y", (cw[0].bitcast(dt.uint8), cw[1]), T.wc[:, :])
    load("s", w("z_W", 0, 512), T.ws[:, :])

    TMP = [0]
    def ftmp(n):
        a = TMP[0]
        TMP[0] += n
        return w("TMPF", a, a + n)
    kt, ioi, mp = w("KTB", 0, 64), w("IOI", 0, 64), w("MAP", 0, 64)
    fnat, fbl, frg, fsh, fsn, fout, fr2, fc1, f1, fa, fb, fh, fkp, ktf, fm = [ftmp(n) for n in (16, 4, 4, 4, 4, 16, 2, 16, 64, 2, 2, 2, 32, 32, 64)]
    iota(w("PI", 0, 1), [[0, 1]], 0, 1, small=False)
    fill(w("ONE", 0, 520), 1.0)
    sa(w("ZB", 0, 512), w("ONE", 0, 512), 0.0)
    sa(w("HT1", 128, 512), w("ONE", 0, 384), 0.0)
    sa(w("DT1", 128, 512), w("ONE", 0, 384), 0.0)

    def col(j):
        return w("FC", j, j + 1)
    P16, P31, KK, QQ, B2, B3, Q0, Q1, M, ODD, B0, B1, K1, P8, K2 = range(15)
    for j, (sh, an) in enumerate(((0, 15), (0, 31), (2, 3), (5, 3), (2, 1), (3, 1), (5, 1), (6, 1), (0, 3), (4, 1), (0, 1), (1, 1), (1, 7), (0, 7), (2, 7))):
        o, i = w("INTC", j, j + 1), w("PI", 0, 1)
        if sh:
            ts(o, i, sh, A.arith_shift_right, an, A.bitwise_and)
        else:
            ts(o, i, an, A.bitwise_and)
    C8P, CX, CSN, C16, CW2, CNX, CND, C32K, COUT, KR, SHF, PC, PC3, VP, VD, OP, C1P, MK1, SU, Y0, Y2 = range(16, 37)
    fill(w("SEG", 0, 64), 1.0)
    cp("v", w("FC", 0, 15), w("INTC", 0, 15))
    fill(w("SEG", 32, 33), 0.0)
    for h in range(2):
        fill(lst("ac", 2, 2 * h), h)
    eb, one = w("EB", 0, 520), w("ONE", 0, 520)
    run("g", lambda: g.affine_select(eb[0], one[0], [[-1, 520]], A.is_equal, 0.0, 4, 4), [one], [eb])
    iota(fnat, [[1, 8], [128, 2]])
    iota(fbl, [[4, 2], [0, 2]])
    iota(fsh, [[0, 2], [16, 2]])

    quant("V", 0, w("VB", 0, 512))
    quant("PB0", OLD, w("PT", 0, 512))

    def scores(t):
        sc, n = "SC%d" % t, "N%d" % t
        mm(0, 128, "PB%d" % t, OLD, "V", 0)
        cp("s", w(sc, 0, 1), w("ps", t, t + 1))
        send_scores(t)
        run("y", lambda: g.sync.dma_start(T[n][:, me:me + 1], T[sc][:, 0:1]), [w(sc, 0, 1)], [w(n, me, me + 1)], dma=True)
        arrive([w(n, a, b) for a, b in ((0, me), (me + 1, 8)) if b > a], "sc%d" % t, score_count())

    scores(0)
    iota(frg, [[1, 2], [0, 2]])
    iota(fsn, [[2, 4]])
    iota(ioi, [[0, 2], [1, 32]])
    iota(w("MT", 0, 64), [[0, 16], [1, 4]])
    iota(fr2, [[4, 2]])
    iota(mp, [[128, 2], [1, 32]])
    iota(kt, [[4, 2], [0, 32]])
    iota(w("VALS", 0, 32), [[0, 8], [1, 4]])
    own16, c1, sq = w("OWN", 0, 16), w("C1", 0, 16), w("SQ", 0, 4)
    iota(own16, [[16, 16]])
    iota(sq, [[16, 4]])
    iota(fc1, [[4, 8], [0, 2]])
    iota(fkp, [[8, 32]], -MID)
    iota(fm, [[16, 2], [0, 2], [1, 16]])
    iota(w("WT", 0, 128), [[16, 4], [0, 2], [1, 16]])
    iota(fout, [[2, 16]])

    ts(col(C8P), col(P16), 8.0, A.mult)
    tt(col(CNX), col(B2), col(Q0), A.not_equal)
    tt(col(CND), col(B3), col(Q1), A.not_equal)
    ts(lst("nat", 16), fnat, col(C8P), A.add)
    sa(w("NB", 0, 520), eb, -1.0)
    quant("X", 0, w("XB", 0, 1024))
    pick("D0", 0, 256, "X", 256, ("LST", LISTS["nat"]))
    quant("U", 0, w("UB", 0, 512))
    for b in range(2):
        mm(b, 256, "W", 128 * b, "D0", 0)
    for h in range(2):
        mm(4 + h, 128, "D0", 128 * h, "U", 0)
    for b in range(2, 4):
        mm(b, 256, "W", 128 * b, "D0", 0)
    for b in range(4):
        quant("E", 512 + 128 * b, w("NB", 4 - b, 516 - b))

    def relu(tile, b, cols, bk):
        o, i = w(tile, b, 4 * cols, 4), bank(bk, cols)
        run("s", lambda: g.scalar.activation(o[0], i[0], F.Relu, scale=0.0625), [i], [o])

    relu("HT0", 0, 256, 0)
    relu("HT0", 1, 256, 1)
    cp("s", w("ACOL", 0, 2), w("ps", 2048, 3072, 512))
    relu("HT0", 2, 256, 2)
    relu("HT0", 3, 256, 3)
    sa(col(C32K), col(KK), 32.0)
    sa(col(C16), col(ODD), 16.0)
    sa(kt, kt, 1.0, col(KK))
    sa(mp, mp, 1.0, col(C32K))
    sa(w("DMP", 0, 64), mp, 0.0, -1.0)
    sa(f1, kt, 32.0)
    cp("s", w("DMP", 31, 64, 32), w("MAP", 31, 64, 32))
    for b in range(4):
        mm(4 + b, 256, "E", 512 + 128 * b, "D0", 0, True, False)
    bi, shi, sni = w("TMPI", 12, 16), w("TMPI", 0, 4), w("TMPI", 4, 8)
    t0, b0, b1, hh = [w("TMPI", a, a + 2) for a in (144, 146, 148, 150)]
    kti, k0 = w("TMPI", 80, 112), ktf[1][0][1]
    ts(col(KR), col(Q1), float(r), A.mult, col(KK), A.add)
    ts(bi, fbl, col(QQ), A.add, float(8 - r), A.add)
    ts(shi, fsh, col(P16), A.add)
    ts(t0, fr2, col(KR), A.add)
    ts(col(CX), col(CND), 2.0, A.mult, col(CNX), A.add)
    ts(col(CSN), col(B2), float(r), A.mult, col(B3), A.add)
    ts(bi, bi, 7, A.bitwise_and)
    for h in range(2):
        n = min(max(r - 4 * h, 0), 4)
        if n:
            v = w("TMPI", 2 * h, 2 * h + 2, 1, 0, 32 * n)
            ts(v, v, 31.0, A.add)
    ts(t0, t0, 7, A.bitwise_and)
    ts(col(CX), col(CX), 2.0, A.mult)
    ts(sni, fsn, col(CSN), A.add)
    ts(lst("bl", 4, 4), bi, 8.0 if CLASH else 0.0, A.add)
    ts(shi, shi, 31, A.bitwise_and)
    ts(b0, t0, 1, A.bitwise_and)
    ts(lst("rg", 4), frg, col(CX), A.add)
    ts(sni, sni, 7, A.bitwise_and)
    cp("v", lst("sh", 2), w("TMPI", 0, 2))
    ts(lst("sh", 2, 2), w("TMPI", 2, 4), 32.0, A.add)
    ts(lst("bl", 4), fbl, col(QQ), A.add)
    ts(lst("sn", 4), sni, 4.0, A.mult, col(M), A.add)
    ts(w("LM", 0, 64), ioi, col(P31), A.is_lt, TINY, A.mult)
    for b in range(4):
        quant("E", 128 * b, w("EB", 4 - b, 516 - b))

    def arow():
        cp("v", w("RA", 0, 64), ind(w("ACOL", 0, 2), lst("ac", 4)))

    arow()
    quant("NX", 0, w("HT0", 0, 1024))
    for b in range(4):
        mm(4 + b, 256, "E", 128 * b, "NX", 0, False, True)
    for b in range(4):
        cp("s", w("DT0", b, 1024, 4), bank(4 + b, 256))

    def differences(name, c, src):
        tt(w(name, c, c + 63), w(src, 0, 63), w(src, 1, 64), A.subtract)
        cp("s", w(name, c + 31, c + 64, 32), w(src, 31, 64, 32))

    x1 = w("TMPI", 16, 80)
    gaps = [
        lambda: ts(col(SHF), col(K2), float(8 - r), A.is_ge, 31.0, A.mult),
        lambda: ts(b1, t0, 1, A.arith_shift_right, 1, A.bitwise_and),
        lambda: ts(col(SHF), col(SHF), col(Q1), A.mult),
        lambda: ts(fa, b0, col(Q0), A.not_equal, 2.0, A.mult),
        lambda: ts(kti, w("IOI", 0, 32), col(SHF), A.add),
        lambda: ts(fb, b1, col(Q1), A.not_equal, 4.0, A.mult),
        lambda: ts(hh, t0, 2, A.arith_shift_right, 1, A.bitwise_and),
        lambda: ts(kti, kti, 31, A.bitwise_and),
        lambda: tt(fa, fa, fb, A.add),
        lambda: ts(fh, hh, 1.0, A.mult),
        lambda: ts(ktf, kti, 8.0, A.mult, float(r - MID), A.add),
        lambda: ts(x1, ioi, col(C16), A.add),
        lambda: tt(fa, fa, fh, A.add),
        lambda: tt(w("DK", 0, 31), w("TMPF", k0, k0 + 31), w("TMPF", k0 + 1, k0 + 32), A.subtract),
        lambda: cp("v", w("DK", 31, 32), w("TMPF", k0 + 31, k0 + 32)),
        lambda: cp("v", lst("r2", 2), fa)]
    after = [
        lambda: ts(x1, x1, 31, A.bitwise_and),
        lambda: tt(col(CNX), col(B0), col(ODD), A.not_equal),
        lambda: ts(sq, sq, col(P16), A.add, 32.0 * QB, A.add),
        lambda: tt(w("OFR", 0, 64), f1, x1, A.add),
        lambda: ts(col(CW2), col(CNX), 16.0, A.mult),
        lambda: ts(col(Y0), col(B2), 4.0 * ((2 * r) % 8 - r), A.mult, col(M), A.add),
        lambda: differences("DF", 0, "OFR"),
        lambda: ts(lst("w2", 1), col(K1), 32.0, A.mult, col(CW2), A.add),
        lambda: ts(w("SQ", 2, 4), w("SQ", 2, 4), 32.0 * (DB - QB - 1) if DB < QB else 0.0, A.add),
        lambda: ts(lst("ow", 1), col(Y0), 4.0 * r, A.add),
        lambda: ts(own16, own16, col(P16), A.add),
        lambda: quant("D0", 256, w("ZB", 0, 512)),
        lambda: cp("v", lst("pp", 4), sq),
        lambda: tt(c1, fc1, own16, A.subtract)]
    owner = [
        lambda: ts(col(VP), col(Q1), 32.0, A.mult, float(LAP), A.add),
        lambda: ts(col(VD), col(K2), 7.0, A.is_equal, -72.0, A.mult),
        lambda: ts(c1, c1, 256.0, A.add),
        lambda: ts(col(SU), col(K2), 8.0, A.mult, 16.0, A.add),
        lambda: ts(col(OP), col(Q1), 32.0 * (DB - QB), A.mult, OLD + 32.0 * QB, A.add),
        lambda: tt(w("VPB", 0, 1), col(VP), col(P31), A.add),
        lambda: tt(col(VD), col(VD), col(M), A.add),
        lambda: ts(col(C1P), col(Q1), 64.0, A.mult, -1.0, A.add),
        lambda: tt(col(OP), col(OP), col(P31), A.add),
        lambda: tt(col(VD), col(VD), col(SU), A.add),
        lambda: ts(col(SU), col(Q1), 4.0, A.mult),
        lambda: ts(col(PC), col(P31), 8.0, A.mult, -MID - 0.5, A.add),
        lambda: tt(col(C1P), col(C1P), col(OP), A.subtract),
        lambda: tt(w("VDB", 0, 1), col(VD), col(SU), A.add),
        lambda: ts(col(PC3), col(P31), 8.0, A.mult, 7.5 - MID, A.add),
        lambda: fill(w("TBL", 0, LAP), 1.0),
        lambda: fill(w("TBL", LAP, 144), 0.0),
        lambda: ts(w("MASK", 0, 64), fm, col(P31), A.is_equal),
        lambda: ts(col(Y2), col(K1), float(QB), A.is_equal, -2.0, A.mult),
        lambda: cp("v", lst("sl", 1), col(M)),
        lambda: pick("LA0", LAP, 64, "PB0", 128, ("LST", LISTS["pp"]), OLD),
        lambda: ts(lst("se", 1), col(Y2), col(B0), A.add, 2.0, A.add)]

    def gap(n=1):
        for i in range(n):
            if gaps:
                gaps.pop(0)()

    def choose(t):
        n = "N%d" % t
        if CLASH:
            for h, q in enumerate("vs" if t else "vv"):
                cp(q, w(n, 8, 16, 1, 64 * h, 64 * h + 64), w(n, 0, 8, 1, 64 - 64 * h, 128 - 64 * h))
        rb, tb = w("RB", 0, 128), w("TB", 0, 128)
        tt(w("RB", 0, 64), ind(w(n, 0, 8), lst("bl", 4)), w("RA", 0, 64), A.subtract)
        cp("s" if t else "v", w("RB", 64, 128), ind(w(n, 0, 16 if CLASH else 8), lst("bl", 4, 4)))
        gap(2)
        tr(tb, rb)
        gap(2)
        st, rr, g1, g2, cc = [w(x, 0, 64) for x in ("ST", "RR", "G1", "G2", "CC")]
        tt(st, ind(w("TB", 64, 128), lst("sh", 4)), w("TB", 0, 64), A.add)
        gap(2)
        tr(rr, st)
        gap(2)
        tt(g1, st, rr, A.subtract)
        gap(2)
        tt(g2, g1, w("LM", 0, 64), A.is_lt)
        gap(2)
        scan(cc, w("SEG", 0, 64), g2)
        gap(2)
        for q in range(4):
            cp("vs"[q % 2], w("XR", 2, 4, 1, 32 * q, 32 * q + 32), w("CC", 31, 64, 32, 32 * (q ^ 1), 32 * (q ^ 1) + 32))
        cp("v", w("XR", 0, 2), w("CC", 31, 64, 32))
        cp("v", w("XR", 4, 8, 1, 0, 64), w("XR", 0, 4, 1, 64, 128))
        cp("s", w("XR", 4, 8, 1, 64, 128), w("XR", 0, 4, 1, 0, 64))
        gap(len(gaps))
        rg, m, xr = w("RG", 0, 64), w("MM", 0, 64), w("XR", 0, 8)
        wk = "WK%d" % t
        tt(rg, ind(xr, lst("rg", 4)), w("MT", 0, 64), A.not_equal)
        tt(w("RGK", 0, 32), ind(xr, lst("r2", 2)), w("MT", 0, 32), A.not_equal)
        tr(m, rg)
        tr(w("MK", 0, 32), w("RGK", 0, 32))
        scan(w("SCN", 0, 64), m, w("DMP", 0, 64))
        scan(w("SK", 0, 32), w("MK", 0, 32), w("DK", 0, 32))
        cp("v", w("L1U", 0, 2), w("SCN", 31, 64, 32))
        ts(w("KB", 0, 32), w("ONE", 0, 32), w("SK", 31, 32), A.mult)
        if t == 0:
            quant("DL", 0, w("DT0", 0, 1024))
        dc, sn, la, kx = "DC%d" % t, "SN%d" % t, "LA%d" % t, "KX%d" % t
        pick(dc, 0, 32, "DL", 256 + 32 * t, ("L1U", 0))
        tr(w(wk, 0, 32), w("KB", 0, 32))
        if t:
            scan(w("SCN", 64, 128), m, w("DF", 0, 64))
        pick(sn, 0, 64, dc, 32, ("LST", LISTS["sn"]))
        hs, close = T.sem["hs%d" % t], _near(core, helpers[0], away, topo)
        fused([w("c_" + sn, 0, 64)], [([helpers[h]], close[NHAND * h:NHAND * h + NHAND], hs, T["c_" + sn][:, 32 * h:32 * h + 32].bitcast(dt.uint8),
                                       T["c_HC%d" % t][:, 0:32].bitcast(dt.uint8)) for h in range(2)])
        a = 32 * (1 - me // HALF)
        fused([w("z_" + sn, 0, 64)], [([helpers[2]], close[:2 * NHAND], hs, T["z_" + sn][:, a:a + 32], T["z_HZ%d" % t][:, 0:32])])
        for part in _calls(me, cores, topo):
            fused([w(wk, 0, 32)], [([cores[o]], _list_mask(me, o, cores, topo), T.sem["ls%d" % t], T[wk][:, 4 * o:4 * o + 4],
                                    T[kx][:, 32 + 4 * pos(me, o):36 + 4 * pos(me, o)]) for o in part])
        fused([w("z_" + sn, 0, 64)], [([cores[o]], _mask(me, o, mine, core, cores, topo), T.sem["dl%d" % t], T["z_" + sn][:, 8 * o:8 * o + 8],
                                       T["z_" + la][:, 16 + 8 * pos(me, o):24 + 8 * pos(me, o)]) for o in mine])
        run("y", lambda: g.sync.dma_start(T[kx][:, 60:64], T[wk][:, 4 * me:4 * me + 4]), [w(wk, 4 * me, 4 * me + 4)], [w(kx, 60, 64)], dma=True)
        arrive([w(kx, 32, 60)], "ls%d" % t, sum(len(_list_mask(s, me, cores, topo)) for s in others))
        arrive([w("c_" + la, 16, 72), w("z_" + la, 16, 72)], "dl%d" % t, sum(delta_count(s) for s in others))
        inv, vals, l2 = w("INV%d" % t, 0, 256), w("VALS", 0, 32), w("L2U", 0, 2)
        sa(inv, w("EB", 0, 256), 0.0, 8.0)
        if t == 0:
            for k in range(R):
                sa(w("KX%d" % k, 0, 32), fkp, 1.0, -0.5)
            sa(w("SEGG", 0, 192), w("ONE", 0, 192), 0.0, 1.0)
            sa(w("SEGH", 0, 320), w("ONE", 0, 320), 0.0, 1.0)
            sa(col(COUT), col(P8), 32.0, col(B3))
            sa(w("K4", 0, 64), kt, 4.0, 256.0)
            sa(w("SEGG", 0, 192, 64), w("ONE", 0, 3), 0.0)
            sa(w("SEGH", 0, 320, 32), w("ONE", 0, 10), 0.0)
            for f in after:
                f()
            scan(w("SCN", 64, 128), m, w("DF", 0, 64))
        cp("v", l2, w("SCN", 95, 128, 32))
        run("v", lambda: g.vector.tensor_copy(inv[0].indirect(l2[0]), vals[0]), [vals, l2], [inv])
        pick(la, 0, 16, dc, 32, ("LST", LISTS["ow"]))
        tr(w("INVT", 0, 256), inv)

    def advance(t):
        d, dn, it = "D%d" % t, "D%d" % (t + 1), w("INVT", 0, 256)
        pick(d, 256, 32, "NX", 256 + 32 * t, ("L1U", 0))
        if t < R - 1:
            for b in range(4):
                mm(b, 128, "W", 128 * b, d, 256)
        wd, we, dls = w("WD", 0, 16), w("WE", 0, 16), w("DLS", 0, 16)
        rg, rt, mask, u = w("RG", 0, 64), w("RT", 0, 64), w("UP", 0, 64), w("UP", 64, 128)
        row = [lambda: cp("v", wd, ind(it, lst("w2", 1))), lambda: ts(we, wd, 8.0, A.not_equal), lambda: tt(wd, wd, c1, A.add),
               lambda: tt(wd, wd, we, A.mult), lambda: tt(wd, wd, own16, A.add), lambda: cp("v", dls, wd)]
        moved = [lambda: cp("v", rg, ind(w("XR", 0, 8), lst("rg", 4))), lambda: tr(rt, rg), lambda: ts(mask, rt, 4.0, A.is_lt),
                 lambda: tt(u, rt, w("K4", 0, 64), A.add), lambda: tt(u, u, mp, A.subtract), lambda: tt(u, u, mask, A.mult)]
        for i in range(6):
            row[i]()
            if t < R - 1:
                moved[i]()
            if t == 0:
                for f in owner[4 * i:4 * i + 4]:
                    f()
        if t < R - 1:
            for b in range(4):
                relu("HT1", b, 32, b)
            tt(mp, mp, u, A.add)
            quant("NX", 256 + 32 * t, w("HT1", 0, 512))
        pick(dn, 0, 256, d, 288, ("DLS", 0))
        if t < R - 1:
            differences("DMP", 0, "MAP")
            for h in range(2):
                mm(4 + h, 128, dn, 128 * h, "U", 0)
            cp("s", w("ACOL", 0, 2), w("ps", 2048 + t + 1, 3072, 512))
            if t == 0:
                sa(w("K4", 0, 64), w("K4", 0, 64), 1.0, 32.0)
        else:
            ts(lst("out", 16), fout, col(COUT), A.add)
            pick("FD", 0, 256, dn, 256, ("LST", LISTS["out"]))
            mm(4, 256, "U", 0, "FD", 0)
            cp("s", w("YB", 0, 256), w("ps", 2048, 2304))
            fd = w("c_FD", 0, 256)
            store("y", T.oc[:, 0:1024], (fd[0].bitcast(dt.uint8), fd[1]))
            store("y", T.y[:, 0:256], w("YB", 0, 256))
            for k in range(4):
                store("y", T.osc[4 * k:4 * k + 4, 0:256], w("z_FD", 0, 256, 1, 32 * k, 32 * k + 4))

    def patch(t):
        la, kx, pb, pn, last = "LA%d" % t, "KX%d" % t, "PB%d" % t, "PB%d" % (t + 1), t == R - 1
        tr(w("KT", 0, 32), w(kx, 32, 64))
        ts(w("GG", 0, 64), w(kx, 0, 64), col(PC), A.is_lt)
        ts(w("GG", 128, 192), w(kx, 0, 64), col(PC3), A.is_lt)
        ts(w("GG", 64, 128), w(kx, 0, 64), w("KT", 0, 1), A.is_lt)
        scan(w("CN", 0, 192), w("SEGG", 0, 192), w("GG", 0, 192))
        pp, pd, p3 = w("CN", 63, 64), w("CN", 127, 128), w("CN", 191, 192)
        ts(w("HH", 0, 128), w("WT", 0, 128), pp, A.is_equal, w("VPB", 0, 1), A.mult)
        ts(w("HH", 128, 256), w("WT", 0, 128), pd, A.is_equal, w("VDB", 0, 1), A.mult)
        ts(col(MK1), p3, pp, A.subtract, 1.0, A.is_gt)
        tr(w("HHT", 0, 256), w("HH", 0, 256))
        ts(col(SU), p3, col(C1P), A.add, col(MK1), A.mult)
        scan(w("SH", 0, 256), w("SEGH", 0, 256), w("HHT", 0, 256))
        ts(col(SU), col(SU), col(OP), A.add)
        tt(w("ALF", 0, 4), w("SH", 31, 128, 32), w("SH", 159, 256, 32), A.add)
        ts(w("HH", 256, 320), w("MASK", 0, 64), col(SU), A.mult)
        for k in range(2):
            for h in range(2):
                cp("v", w("AL", 4 * k, 4 * k + 4, 1, 64 * h, 64 * h + 64), w("ALF", 0, 4, 1, 64 * k, 64 * k + 64))
        ms, tb, al = w("MS", 0, 128), w("TBL", 0, 144), w("AL", 0, 8)
        pick("AR", 0, 128, la, 144, ("AL", 0))
        run("s", lambda: g.scalar.activation(ms[0], tb[0].indirect(al[0]), F.Copy), [tb, al], [ms])
        for b in range(4):
            mm(b, 128, "E", 128 * b, "AR", 0)
        tr(w("HHT", 256, 320), w("HH", 256, 320))
        scan(w("SH", 256, 320), w("SEGH", 256, 320), w("HHT", 256, 320))
        for k in range(2):
            for h in range(2):
                cp("s", w("SX", 2 * k, 2 * k + 2, 1, 64 * h, 64 * h + 64), w("SH", 287, 320, 32, 64 * k, 64 * k + 64))
        for b in range(4):
            scan(w("NT", b, 512, 4), ms, bank(b, 128))
            if b == 2:
                cp("v", w("SEL", 0, 16), ind(w("SX", 0, 4), lst("sl" if last else "se", 1)))
        quant(pb, 0, w("NT", 0, 512))
        pick(pn, OLD, 128, pb, 256, ("SEL", 0))
        if not last:
            scores(t + 1)
            pick("LA%d" % (t + 1), LAP, 64, pn, 128, ("LST", LISTS["pp"]), OLD)
            for b in range(4):
                mm(4 + b, 128, "E", 512 + 128 * b, "D%d" % t, 256, True, False)
                mm(4 + b, 128, "E", 128 * b, "NX", 256 + 32 * t, False, True)
            for b in range(4):
                cp("vs"[b % 2], w("DT1", b, 128, 4), bank(4 + b, 32))
            quant("DL", 256 + 32 * t, w("DT1", 0, 512))
            arow()
            if t == 0:
                quant("D1", 256, w("ZB", 0, 512))
        else:
            mm(0, 128, "V", 0, pn, OLD)
            cc = w("c_" + pn, OLD, OLD + 64)
            store("y", T.oc[:, 1024:1280], (cc[0].bitcast(dt.uint8), cc[1]))
            for k in range(4):
                store("ys"[k % 2], T.osc[4 * k:4 * k + 4, 256:320], w("z_" + pn, OLD, OLD + 64, 1, 32 * k, 32 * k + 4))
            cp("v", w("YB", 256, 320), bank(0, 64))
            store("s", T.y[:, 256:320], w("YB", 256, 320))

    for t in range(R):
        choose(t)
        advance(t)
        patch(t)
    for sem in sorted(total):
        if known["g"].get(sem, 0) < total[sem]:
            g.wait_ge(T.sem[sem], total[sem])
